import numpy as np
import ml_dtypes


def mxq(x, axis, fmt="e4m3"):
    dtype, down = {"e4m3": (ml_dtypes.float8_e4m3fn, 7), "e5m2": (ml_dtypes.float8_e5m2, 14)}[fmt]
    v = np.moveaxis(np.asarray(x, np.float32).astype(ml_dtypes.bfloat16).astype(np.float64), axis, -1)
    blocks = v.reshape(v.shape[:-1] + (-1, 32))
    amax = np.abs(blocks).max(-1, keepdims=True)
    byte = np.maximum(np.where(amax > 0, np.frexp(amax)[1] - 1 + 127, 0) - down, 1)
    scale = np.exp2(byte - 127.0)
    codes = (blocks / scale).astype(np.float32).astype(dtype).astype(np.float64)
    return np.moveaxis((codes * scale).reshape(v.shape), -1, axis)


WIDE = False


def mx_kscale(k):
    if not WIDE:
        return np.ones(k)
    levels = np.array([10, -10, 5, -5, 0])
    if k % 512:
        return np.exp2(np.random.permutation(np.resize(levels, k // 32))).repeat(32)
    a = np.empty((k // 512, 16))
    for p in range(k // 512):
        a[p, :8] = np.random.permutation(np.resize(levels, 8))
        for g in range(8):
            far = levels[np.abs(levels - a[p, g]) >= 10]
            a[p, g + 8] = far[np.random.randint(len(far))]
    return np.exp2(a.ravel()).repeat(32)


def f64(x):
    return np.asarray(x).astype(np.float64)


def striped(idx):
    return np.tile(idx.reshape(-1, 16).T, (8, 1)).astype(np.uint16)


def unstriped(offs):
    return offs[:16].T.reshape(-1).astype(np.int64)


E2M1 = np.array([0.0, 0.5, 1.0, 1.5, 2.0, 3.0, 4.0, 6.0, -0.0, -0.5, -1.0, -1.5, -2.0, -3.0, -4.0, -6.0])


def pack_weight(w, fmt):
    k, n = w.shape
    w = f64(np.asarray(w, np.float32).astype(ml_dtypes.bfloat16)).reshape(k // 32, 32, n)
    amax = np.abs(w).max(1)
    if fmt == "e4m3":
        byte = np.frexp(amax)[1] - 1 + 127 - 7
    else:
        mant, ex = np.frexp(amax / 6.0)
        byte = np.where(mant > 0.5, ex, ex - 1) + 127
    byte = np.clip(np.where(amax > 0, byte, 1), 1, 254)
    scaled = (w * np.exp2(127.0 - byte)[:, None, :]).reshape(k, n).astype(np.float32)
    by_word = np.ascontiguousarray(scaled.reshape(k // 512, 128, 4, n).transpose(0, 1, 3, 2))
    if fmt == "e4m3":
        words = by_word.astype(ml_dtypes.float8_e4m3fn).view(np.uint8)
    else:
        c = by_word.astype(ml_dtypes.float4_e2m1fn).view(np.uint8) & 0xF
        words = (c[..., 0::2] | (c[..., 1::2] << 4)).reshape(k // 512, 128, 2 * n)
    return np.ascontiguousarray(words), np.ascontiguousarray(byte.astype(np.uint8).reshape(k // 512, 16, n))


def unpack_weight(words, scales, fmt):
    g, _, n = scales.shape
    words = np.ascontiguousarray(words).reshape(g, 128, n, -1)
    if fmt == "e4m3":
        vals = words.view(ml_dtypes.float8_e4m3fn).astype(np.float64)
    else:
        nib = np.empty((g, 128, n, 4), np.uint8)
        nib[..., 0::2] = words & 0xF
        nib[..., 1::2] = words >> 4
        vals = E2M1[nib]
    vals = vals * np.repeat(np.exp2(scales.astype(np.float64) - 127.0), 8, axis=1)[..., None]
    return vals.transpose(0, 1, 3, 2).reshape(g * 512, n)


def gelu(v):
    return 0.5 * v * (1.0 + np.tanh(np.sqrt(2.0 / np.pi) * (v + 0.044715 * v**3)))


K, T, S, M, N = 1536, 2048, 1024, 512, 768

def setup_inputs():
    n = np.random.standard_normal
    s = mx_kscale(K)[:, None]
    u = mx_kscale(S)
    idx = np.random.permutation(T)[:S]
    tab_words, tab_scales = pack_weight(n((K, T)) / np.sqrt(K) * s, "e4m3")
    tab2_words, tab2_scales = pack_weight(n((K, T)) / np.sqrt(K) * s, "e4m3")
    xn_words, xn_scales = pack_weight(n((K, M)) / s, "e2m1")
    wdT = n((N, T)) / np.sqrt(S)
    wdT[:, idx] /= u
    return {
        "tab_words": tab_words, "tab_scales": tab_scales,
        "tab2_words": tab2_words, "tab2_scales": tab2_scales,
        "offs": striped(idx),
        "xc": (n((K, M)) / s).astype(np.float32),
        "xn_words": xn_words, "xn_scales": xn_scales,
        "g": (np.exp(0.3 * n(S)) * u).astype(np.float32),
        "wdT": wdT.astype(np.float32),
        "b": (0.5 * n(N)).astype(np.float32),
        "ew": np.exp(0.3 * n(M)).astype(np.float32),
    }

def reference(tab_words, tab_scales, tab2_words, tab2_scales, offs, xc, xn_words, xn_scales, g, wdT, b, ew):
    v = unpack_weight(tab_words, tab_scales, "e4m3")[:, unstriped(offs)]
    v2 = unpack_weight(tab2_words, tab2_scales, "e4m3")[:, unstriped(offs)]
    xn = unpack_weight(xn_words, xn_scales, "e2m1")
    wd = f64(wdT)[:, unstriped(offs)]
    a = v.T @ mxq(f64(xc), 0, "e4m3")
    c = v2.T @ xn
    h = np.maximum(a, c) * f64(g)[:, None]
    y = mxq(wd, 1, "e4m3") @ mxq(h, 0, "e4m3")
    return (y + f64(b)[:, None]) * f64(ew)[None, :]

@@ -1,0 +1,278 @@
+from contextlib import ExitStack
+
+import concourse.mybir as mybir
+from concourse.masks import make_identity
+
+K, T, S, M, N = 1536, 2048, 1024, 512, 768
+FLOPS = 2 * K * S * M * 2 + 2 * N * S * M
+
+F32 = mybir.dt.float32
+BF16 = mybir.dt.bfloat16
+I32 = mybir.dt.int32
+U32 = mybir.dt.uint32
+U16 = mybir.dt.uint16
+U8 = mybir.dt.uint8
+FP8X4 = mybir.dt.float8_e4m3fn_x4
+FP4X4 = mybir.dt.float4_e2m1fn_x4
+ALU = mybir.AluOpType
+ACT = mybir.ActivationFunctionType
+
+P = 128
+PACK = 4
+K_PASSES = K // (P * PACK)
+J_PASSES = S // (P * PACK)
+N_TILES = N // P
+QUADS = 4
+SHIFT_ROWS = 112
+BIAS_ROW = PACK
+EW_ROW = BIAS_ROW + N_TILES
+
+
+def by_slot(ap):
+    return ap.rearrange("p (t c r) -> p c t r", t=PACK, r=8)
+
+
+def slot_cols(b, t):
+    start = t * (S // PACK) + b * P
+    return slice(start, start + P)
+
+
+def tile_list_sparse_edge_maxout_kernel(
+    tc, tab_words, tab_scales, tab2_words, tab2_scales, offs, xc, xn_words, xn_scales, g, wdT, b, ew, out
+):
+    nc = tc.nc
+    with ExitStack() as ctx:
+        keep = ctx.enter_context(tc.tile_pool(name="keep", bufs=1))
+        ring = ctx.enter_context(tc.tile_pool(name="ring", bufs=2))
+        psum = ctx.enter_context(tc.psum_pool(name="psum", bufs=1))
+
+        offsets = keep.tile([P, S // 16], U16, name="offsets")
+        nc.sync.dma_start(offsets[:], offs)
+
+        swin2 = keep.tile([P, T // 4], I32, name="swin2", align_bytes=64)
+        swin1 = keep.tile([P, T // 4], I32, name="swin1", align_bytes=64)
+        xn_s = keep.tile([P, K_PASSES, M // 4], I32, name="xn_s", align_bytes=64)
+        small = keep.tile([P, 2 * P], F32, name="small", align_bytes=64)
+        moved = keep.tile([P, K_PASSES - 1, S // 4], I32, name="moved", align_bytes=64)
+        nc.vector.memset(swin2[:], 0)
+        nc.vector.memset(swin1[:], 0)
+        nc.vector.memset(xn_s[:], 0)
+        nc.vector.memset(small[:], 0.0)
+        nc.vector.memset(moved[:], 0)
+
+        def load_words(src, a, name):
+            win = keep.tile([P, T], I32, name=name, align_bytes=64)
+            nc.sync.dma_start(win[:], src[a].rearrange("p n t -> p (n t)").bitcast(I32))
+            return win
+
+        def load_xc(a):
+            raw = keep.tile([P, PACK, M], F32, name=f"xc_raw{a}", align_bytes=64)
+            nc.sync.dma_start(raw[:], xc[a * P * PACK : (a + 1) * P * PACK, :].rearrange("(p i) m -> p i m", i=PACK))
+            return raw
+
+        def load_wd(i):
+            win = keep.tile([P, T], F32, name=f"wd_win{i}", align_bytes=64)
+            nc.sync.dma_start(win[:], wdT[i * P : (i + 1) * P, :])
+            return win
+
+        def load_scales(win, src):
+            for q in range(QUADS):
+                nc.sync.dma_start(win[32 * q : 32 * q + 4 * K_PASSES, :], src[:, 4 * q : 4 * q + 4, :].bitcast(I32))
+
+        win2 = [load_words(tab2_words, a, f"win2_{a}") for a in range(K_PASSES)]
+        load_scales(swin2, tab2_scales)
+        win1 = [load_words(tab_words, 0, "win1_0")]
+        load_scales(swin1, tab_scales)
+        win1.append(load_words(tab_words, 1, "win1_1"))
+        for q in range(QUADS):
+            nc.sync.dma_start(
+                xn_s[32 * q : 32 * q + 4, :, :],
+                xn_scales[:, 4 * q : 4 * q + 4, :].rearrange("a r m -> r a m").bitcast(I32),
+            )
+        xn_w = keep.tile([P, K_PASSES, 2 * M], U8, name="xn_w", align_bytes=64)
+        nc.sync.dma_start(xn_w[:].bitcast(I32), xn_words.rearrange("a p c -> p a c").bitcast(I32))
+        win1.append(load_words(tab_words, 2, "win1_2"))
+        xc_raw = [load_xc(a) for a in range(K_PASSES)]
+        wd_win = [load_wd(i) for i in range(N_TILES)]
+
+        nc.scalar.dma_start(
+            small[0:PACK, :].rearrange("t (c r) -> t c r", r=8), g.rearrange("(c t r) -> t c r", t=PACK, r=8)
+        )
+        nc.scalar.dma_start(small[BIAS_ROW:EW_ROW, 0:P], b.rearrange("(i p) -> i p", p=P))
+        nc.scalar.dma_start(small[EW_ROW : EW_ROW + M // P, 0:P], ew.rearrange("(c p) -> c p", p=P))
+        ident_f = keep.tile([P, P], F32, name="ident_f", align_bytes=64)
+        ident_b = keep.tile([P, P], BF16, name="ident_b", align_bytes=64)
+        make_identity(nc, ident_f[:])
+        nc.scalar.copy(ident_b[:], ident_f[:])
+
+        cols = keep.tile([P, J_PASSES, 16], F32, name="cols", align_bytes=64)
+        turned = psum.tile([P, J_PASSES, P], F32, name="turned", tag="y", bufs=2)
+        for jb in range(J_PASSES):
+            nc.tensor.transpose(turned[:, jb, :], small[:, jb * P : (jb + 1) * P], ident_f[:])
+        nc.scalar.copy(cols[:], turned[:, :, 0:16])
+        spread = psum.tile([P, M // P, P], F32, name="spread", tag="y", bufs=2)
+        for c in range(M // P):
+            nc.tensor.transpose(spread[:, c, :], cols[:, 0, EW_ROW + c : EW_ROW + c + 1].to_broadcast([P, P]), ident_f[:])
+        ew_all = keep.tile([P, M], F32, name="ew_all", align_bytes=64)
+        nc.scalar.copy(ew_all[:], spread[:].rearrange("p c m -> p (c m)"))
+
+        def gather_words(win, name):
+            got = keep.tile([P, S], U32, name=name, align_bytes=64)
+            nc.vector.tensor_copy(by_slot(got[:]), win[:].bitcast(U32).indirect(offsets[:]))
+            return got
+
+        def gather_scales(win, name):
+            got = keep.tile([P, S], U8, name=name + "_listed", align_bytes=64)
+            nc.vector.tensor_copy(got[:], win[:].bitcast(U8).indirect(offsets[:]))
+            return got
+
+        def order_scales(got, name):
+            ordered = keep.tile([P, S], U8, name=name, align_bytes=64)
+            nc.vector.tensor_copy(
+                ordered[:].bitcast(I32).rearrange("p (t c w) -> p t c w", t=PACK, w=2),
+                got[:].bitcast(I32).rearrange("p (c t w) -> p t c w", t=PACK, w=2),
+            )
+            return ordered
+
+        v2 = [gather_words(win2[a], f"v2_{a}") for a in range(K_PASSES)]
+        listed2 = gather_scales(swin2, "v2_s")
+        v2_s = order_scales(listed2, "v2_s")
+        for a in range(1, K_PASSES):
+            nc.scalar.dma_start(moved[0:SHIFT_ROWS, a - 1, :], v2_s[4 * a : 4 * a + SHIFT_ROWS, :].bitcast(I32))
+        v1 = [gather_words(win1[0], "v1_0")]
+        listed1 = gather_scales(swin1, "v1_s")
+        v1.append(gather_words(win1[1], "v1_1"))
+        v1_s = order_scales(listed1, "v1_s")
+        v1.append(gather_words(win1[2], "v1_2"))
+
+        def v2_plane(a, cs):
+            if a == 0:
+                return v2_s[:, cs]
+            return moved[:, a - 1, :].bitcast(U8)[:, cs]
+
+        tiles = [(jb, t) for jb in range(J_PASSES) for t in range(PACK)]
+        resp = keep.tile([P, J_PASSES, PACK, M], F32, name="resp", align_bytes=64)
+        for jb, t in tiles:
+            acc = psum.tile([P, M], F32, name="acc", tag="acc", bufs=4)
+            cs = slot_cols(jb, t)
+            for a in range(K_PASSES):
+                nc.tensor.matmul_mx(
+                    out=acc[:],
+                    lhsT=v2[a][:, cs].bitcast(FP8X4),
+                    lhsT_scale=v2_plane(a, cs),
+                    rhs=xn_w[:, a, :].bitcast(FP4X4),
+                    rhs_scale=xn_s[:, a, :].bitcast(U8),
+                    start=(a == 0),
+                    stop=(a == K_PASSES - 1),
+                )
+            nc.scalar.copy(resp[:, jb, t, :], acc[:])
+
+        xc_q = keep.tile([P, K_PASSES, M], U32, name="xc_q", align_bytes=64)
+        xc_s = keep.tile([P, K_PASSES, M], U8, name="xc_s", align_bytes=64)
+        for a in range(K_PASSES):
+            grouped = ring.tile([P, M, PACK], BF16, name="grouped", align_bytes=64)
+            nc.scalar.copy(
+                grouped[:].rearrange("p (c i) t -> p c t i", i=4),
+                xc_raw[a][:].rearrange("p t (c i) -> p c t i", i=4),
+            )
+            nc.vector.quantize_mx(
+                out=xc_q[:, a, :].bitcast(FP8X4), scales=xc_s[:, a, :], in_=grouped[:].rearrange("p m t -> p (m t)")
+            )
+
+        wd_q = keep.tile([P, N_TILES, J_PASSES * P], U32, name="wd_q", align_bytes=64)
+        wd_s = keep.tile([P, N_TILES, J_PASSES * P], U8, name="wd_s", align_bytes=64)
+
+        def gather_wd(i):
+            picked = ring.tile([P, S], BF16, name="picked", align_bytes=64)
+            nc.vector.tensor_copy(by_slot(picked[:]), wd_win[i][:].indirect(offsets[:]))
+            wd_b = ring.tile([P, J_PASSES, P, PACK], BF16, name="wd_b", align_bytes=64)
+            for jb in range(J_PASSES):
+                bank = psum.tile([P, PACK, P], BF16, name="bank", tag="bank", bufs=2)
+                for t in range(PACK):
+                    nc.tensor.transpose(bank[:, t, :], picked[:, slot_cols(jb, t)], ident_b[:])
+                nc.scalar.copy(wd_b[:, jb, :, :], bank[:].rearrange("p t n -> p n t"))
+            return wd_b
+
+        def quantise_wd(i, wd_b):
+            nc.vector.quantize_mx(
+                out=wd_q[:, i, :].bitcast(FP8X4), scales=wd_s[:, i, :], in_=wd_b[:].rearrange("p b n t -> p (b n t)")
+            )
+
+        h_q = keep.tile([P, J_PASSES, M], U32, name="h_q", align_bytes=64)
+        h_s = keep.tile([P, J_PASSES, M], U8, name="h_s", align_bytes=64)
+        h_planes = keep.tile([P, J_PASSES, PACK, M], BF16, name="h_planes", align_bytes=64)
+
+        def respond(jb, t):
+            acc = psum.tile([P, M], F32, name="acc", tag="acc", bufs=4)
+            cs = slot_cols(jb, t)
+            for a in range(K_PASSES):
+                nc.tensor.matmul_mx(
+                    out=acc[:],
+                    lhsT=v1[a][:, cs].bitcast(FP8X4),
+                    lhsT_scale=v1_s[4 * a : P, cs],
+                    rhs=xc_q[:, a, :].bitcast(FP8X4),
+                    rhs_scale=xc_s[:, a, :],
+                    start=(a == 0),
+                    stop=(a == K_PASSES - 1),
+                )
+            nc.vector.tensor_tensor(resp[:, jb, t, :], acc[:], resp[:, jb, t, :], ALU.max)
+            nc.scalar.activation(h_planes[:, jb, t, :], resp[:, jb, t, :], ACT.Copy, scale=cols[:, jb, t : t + 1])
+
+        def group_h(jb):
+            grouped = ring.tile([P, M, PACK], BF16, name="grouped", align_bytes=64)
+            nc.scalar.copy(
+                grouped[:].rearrange("p (c i) t -> p c t i", i=4),
+                h_planes[:, jb, :, :].rearrange("p t (c i) -> p c t i", i=4),
+            )
+            return grouped
+
+        def quantise_h(jb, grouped):
+            nc.vector.quantize_mx(
+                out=h_q[:, jb, :].bitcast(FP8X4), scales=h_s[:, jb, :], in_=grouped[:].rearrange("p m t -> p (m t)")
+            )
+
+        def project(i):
+            y = psum.tile([P, M], F32, name="y", tag="y", bufs=2)
+            for jb in range(J_PASSES):
+                cs = slice(jb * P, (jb + 1) * P)
+                nc.tensor.matmul_mx(
+                    out=y[:],
+                    lhsT=wd_q[:, i, cs].bitcast(FP8X4),
+                    lhsT_scale=wd_s[:, i, cs],
+                    rhs=h_q[:, jb, :].bitcast(FP8X4),
+                    rhs_scale=h_s[:, jb, :],
+                    start=(jb == 0),
+                    stop=(jb == J_PASSES - 1),
+                )
+            res = ring.tile([P, M], F32, name="res", align_bytes=64, bufs=3)
+            nc.vector.scalar_tensor_tensor(
+                res[:], y[:], cols[:, 0, BIAS_ROW + i : BIAS_ROW + i + 1], ew_all[:], ALU.add, ALU.mult
+            )
+            nc.sync.dma_start(out[i * P : (i + 1) * P, :], res[:])
+
+        w0 = gather_wd(0)
+        for t in range(PACK):
+            respond(0, t)
+        quantise_wd(0, w0)
+        w1 = gather_wd(1)
+        h0 = group_h(0)
+        for t in range(PACK):
+            respond(1, t)
+        quantise_wd(1, w1)
+        w2 = gather_wd(2)
+        quantise_h(0, h0)
+        h1 = group_h(1)
+        w3 = gather_wd(3)
+        quantise_wd(2, w2)
+        quantise_h(1, h1)
+        w4 = gather_wd(4)
+        quantise_wd(3, w3)
+        project(0)
+        project(1)
+        w5 = gather_wd(5)
+        quantise_wd(4, w4)
+        project(2)
+        project(3)
+        project(4)
+        quantise_wd(5, w5)
+        project(5)

@@ -22,6 +22,7 @@ PACK = 4
 K_PASSES = K // (P * PACK)
 J_PASSES = S // (P * PACK)
 N_TILES = N // P
+N_PAIRS = N_TILES // 2
 QUADS = 4
 SHIFT_ROWS = 112
 BIAS_ROW = PACK
@@ -32,8 +33,8 @@ def by_slot(ap):
     return ap.rearrange("p (t c r) -> p c t r", t=PACK, r=8)
 
 
-def slot_cols(b, t):
-    start = t * (S // PACK) + b * P
+def slot_cols(jb, t):
+    start = t * (S // PACK) + jb * P
     return slice(start, start + P)
 
 
@@ -54,67 +55,77 @@ def tile_list_sparse_edge_maxout_kernel(
         xn_s = keep.tile([P, K_PASSES, M // 4], I32, name="xn_s", align_bytes=64)
         small = keep.tile([P, 2 * P], F32, name="small", align_bytes=64)
         moved = keep.tile([P, K_PASSES - 1, S // 4], I32, name="moved", align_bytes=64)
-        nc.vector.memset(swin2[:], 0)
+        nc.gpsimd.memset(swin2[:], 0)
         nc.vector.memset(swin1[:], 0)
-        nc.vector.memset(xn_s[:], 0)
         nc.vector.memset(small[:], 0.0)
+        nc.vector.memset(xn_s[:], 0)
         nc.vector.memset(moved[:], 0)
+        ident_f = keep.tile([P, P], F32, name="ident_f", align_bytes=64)
+        make_identity(nc, ident_f[:])
+
+        def load_vectors():
+            nc.sync.dma_start(
+                small[0:PACK, :].rearrange("t (c r) -> t c r", r=8), g.rearrange("(c t r) -> t c r", t=PACK, r=8)
+            )
+            nc.sync.dma_start(small[BIAS_ROW:EW_ROW, 0:P], b.rearrange("(i p) -> i p", p=P))
+            nc.sync.dma_start(small[EW_ROW : EW_ROW + M // P, 0:P], ew.rearrange("(c p) -> c p", p=P))
 
         def load_words(src, a, name):
             win = keep.tile([P, T], I32, name=name, align_bytes=64)
             nc.sync.dma_start(win[:], src[a].rearrange("p n t -> p (n t)").bitcast(I32))
             return win
 
-        def load_xc(a):
-            raw = keep.tile([P, PACK, M], F32, name=f"xc_raw{a}", align_bytes=64)
-            nc.sync.dma_start(raw[:], xc[a * P * PACK : (a + 1) * P * PACK, :].rearrange("(p i) m -> p i m", i=PACK))
-            return raw
-
-        def load_wd(i):
-            win = keep.tile([P, T], F32, name=f"wd_win{i}", align_bytes=64)
-            nc.sync.dma_start(win[:], wdT[i * P : (i + 1) * P, :])
-            return win
-
         def load_scales(win, src):
             for q in range(QUADS):
                 nc.sync.dma_start(win[32 * q : 32 * q + 4 * K_PASSES, :], src[:, 4 * q : 4 * q + 4, :].bitcast(I32))
 
-        win2 = [load_words(tab2_words, a, f"win2_{a}") for a in range(K_PASSES)]
-        load_scales(swin2, tab2_scales)
-        win1 = [load_words(tab_words, 0, "win1_0")]
-        load_scales(swin1, tab_scales)
-        win1.append(load_words(tab_words, 1, "win1_1"))
-        for q in range(QUADS):
-            nc.sync.dma_start(
-                xn_s[32 * q : 32 * q + 4, :, :],
-                xn_scales[:, 4 * q : 4 * q + 4, :].rearrange("a r m -> r a m").bitcast(I32),
-            )
-        xn_w = keep.tile([P, K_PASSES, 2 * M], U8, name="xn_w", align_bytes=64)
-        nc.sync.dma_start(xn_w[:].bitcast(I32), xn_words.rearrange("a p c -> p a c").bitcast(I32))
-        win1.append(load_words(tab_words, 2, "win1_2"))
-        xc_raw = [load_xc(a) for a in range(K_PASSES)]
-        wd_win = [load_wd(i) for i in range(N_TILES)]
+        def load_xc(a):
+            raw = ring.tile([P, PACK, M], F32, name="xc_raw", tag="raw", align_bytes=64, bufs=3)
+            nc.sync.dma_start(raw[:], xc[a * P * PACK : (a + 1) * P * PACK, :].rearrange("(p i) m -> p i m", i=PACK))
+            return raw
 
-        nc.scalar.dma_start(
-            small[0:PACK, :].rearrange("t (c r) -> t c r", r=8), g.rearrange("(c t r) -> t c r", t=PACK, r=8)
-        )
-        nc.scalar.dma_start(small[BIAS_ROW:EW_ROW, 0:P], b.rearrange("(i p) -> i p", p=P))
-        nc.scalar.dma_start(small[EW_ROW : EW_ROW + M // P, 0:P], ew.rearrange("(c p) -> c p", p=P))
-        ident_f = keep.tile([P, P], F32, name="ident_f", align_bytes=64)
-        ident_b = keep.tile([P, P], BF16, name="ident_b", align_bytes=64)
-        make_identity(nc, ident_f[:])
-        nc.scalar.copy(ident_b[:], ident_f[:])
+        def load_wd(i, u):
+            rows = wdT[2 * i * P : 2 * (i + 1) * P, :].rearrange("(p e) t -> p e t", e=2)
+            raw = ring.tile([P, 2, T // 2], F32, name="wd_raw", tag="raw", align_bytes=64, bufs=3)
+            nc.sync.dma_start(raw[:], rows[:, :, u * (T // 2) : (u + 1) * (T // 2)])
+            return raw
+
+        def load_xn_scales():
+            for q in range(QUADS):
+                nc.sync.dma_start(
+                    xn_s[32 * q : 32 * q + 4, :, :],
+                    xn_scales[:, 4 * q : 4 * q + 4, :].rearrange("a r m -> r a m").bitcast(I32),
+                )
+
+        xn_w = keep.tile([P, K_PASSES, 2 * M], U8, name="xn_w", align_bytes=64)
+
+        def load_xn_words():
+            nc.sync.dma_start(xn_w[:].bitcast(I32), xn_words.rearrange("a p c -> p a c").bitcast(I32))
+
+        win1, win2, xc_raw, wd_raw = {}, {}, {}, {}
 
         cols = keep.tile([P, J_PASSES, 16], F32, name="cols", align_bytes=64)
-        turned = psum.tile([P, J_PASSES, P], F32, name="turned", tag="y", bufs=2)
-        for jb in range(J_PASSES):
-            nc.tensor.transpose(turned[:, jb, :], small[:, jb * P : (jb + 1) * P], ident_f[:])
-        nc.scalar.copy(cols[:], turned[:, :, 0:16])
-        spread = psum.tile([P, M // P, P], F32, name="spread", tag="y", bufs=2)
-        for c in range(M // P):
-            nc.tensor.transpose(spread[:, c, :], cols[:, 0, EW_ROW + c : EW_ROW + c + 1].to_broadcast([P, P]), ident_f[:])
         ew_all = keep.tile([P, M], F32, name="ew_all", align_bytes=64)
-        nc.scalar.copy(ew_all[:], spread[:].rearrange("p c m -> p (c m)"))
+
+        def constants():
+            turned = psum.tile([P, J_PASSES, P], F32, name="turned", tag="bank", bufs=2)
+            for jb in range(J_PASSES):
+                nc.tensor.transpose(turned[:, jb, :], small[:, jb * P : (jb + 1) * P], ident_f[:])
+            nc.scalar.copy(cols[:], turned[:, :, 0:16])
+            spread = psum.tile([P, M // P, P], F32, name="spread", tag="bank", bufs=2)
+            for c in range(M // P):
+                nc.tensor.transpose(
+                    spread[:, c, :], cols[:, 0, EW_ROW + c : EW_ROW + c + 1].to_broadcast([P, P]), ident_f[:]
+                )
+            nc.scalar.copy(ew_all[:], spread[:].rearrange("p c m -> p (c m)"))
+
+        def copy_on(engine, dst, src):
+            if engine == "V":
+                nc.vector.tensor_copy(dst, src)
+            elif engine == "G":
+                nc.gpsimd.tensor_scalar(dst, src, 1.0, 0.0, ALU.mult, ALU.add)
+            else:
+                nc.scalar.copy(dst, src)
 
         def gather_words(win, name):
             got = keep.tile([P, S], U32, name=name, align_bytes=64)
@@ -124,9 +135,6 @@ def tile_list_sparse_edge_maxout_kernel(
         def gather_scales(win, name):
             got = keep.tile([P, S], U8, name=name + "_listed", align_bytes=64)
             nc.vector.tensor_copy(got[:], win[:].bitcast(U8).indirect(offsets[:]))
-            return got
-
-        def order_scales(got, name):
             ordered = keep.tile([P, S], U8, name=name, align_bytes=64)
             nc.vector.tensor_copy(
                 ordered[:].bitcast(I32).rearrange("p (t c w) -> p t c w", t=PACK, w=2),
@@ -134,26 +142,23 @@ def tile_list_sparse_edge_maxout_kernel(
             )
             return ordered
 
-        v2 = [gather_words(win2[a], f"v2_{a}") for a in range(K_PASSES)]
-        listed2 = gather_scales(swin2, "v2_s")
-        v2_s = order_scales(listed2, "v2_s")
-        for a in range(1, K_PASSES):
-            nc.scalar.dma_start(moved[0:SHIFT_ROWS, a - 1, :], v2_s[4 * a : 4 * a + SHIFT_ROWS, :].bitcast(I32))
-        v1 = [gather_words(win1[0], "v1_0")]
-        listed1 = gather_scales(swin1, "v1_s")
-        v1.append(gather_words(win1[1], "v1_1"))
-        v1_s = order_scales(listed1, "v1_s")
-        v1.append(gather_words(win1[2], "v1_2"))
+        v1, v2, planes = {}, {}, {}
+
+        def shift_planes():
+            for a in range(1, K_PASSES):
+                nc.sync.dma_start(
+                    moved[0:SHIFT_ROWS, a - 1, :], planes[2][4 * a : 4 * a + SHIFT_ROWS, :].bitcast(I32)
+                )
 
         def v2_plane(a, cs):
             if a == 0:
-                return v2_s[:, cs]
+                return planes[2][:, cs]
             return moved[:, a - 1, :].bitcast(U8)[:, cs]
 
-        tiles = [(jb, t) for jb in range(J_PASSES) for t in range(PACK)]
         resp = keep.tile([P, J_PASSES, PACK, M], F32, name="resp", align_bytes=64)
-        for jb, t in tiles:
-            acc = psum.tile([P, M], F32, name="acc", tag="acc", bufs=4)
+
+        def neighbour(jb, t):
+            acc = psum.tile([P, M], F32, name="acc", tag="acc", bufs=6)
             cs = slot_cols(jb, t)
             for a in range(K_PASSES):
                 nc.tensor.matmul_mx(
@@ -167,49 +172,69 @@ def tile_list_sparse_edge_maxout_kernel(
                 )
             nc.scalar.copy(resp[:, jb, t, :], acc[:])
 
+        def interleave(engine, planes_ap):
+            grouped = ring.tile([P, M, PACK], BF16, name="grouped", align_bytes=64, bufs=2)
+            copy_on(
+                engine,
+                grouped[:].rearrange("p (c i) t -> p c t i", i=4),
+                planes_ap.rearrange("p t (c i) -> p c t i", i=4),
+            )
+            return grouped[:].rearrange("p m t -> p (m t)")
+
         xc_q = keep.tile([P, K_PASSES, M], U32, name="xc_q", align_bytes=64)
         xc_s = keep.tile([P, K_PASSES, M], U8, name="xc_s", align_bytes=64)
-        for a in range(K_PASSES):
-            grouped = ring.tile([P, M, PACK], BF16, name="grouped", align_bytes=64)
-            nc.scalar.copy(
-                grouped[:].rearrange("p (c i) t -> p c t i", i=4),
-                xc_raw[a][:].rearrange("p t (c i) -> p c t i", i=4),
-            )
-            nc.vector.quantize_mx(
-                out=xc_q[:, a, :].bitcast(FP8X4), scales=xc_s[:, a, :], in_=grouped[:].rearrange("p m t -> p (m t)")
+
+        def quantise_xc(a, engine):
+            grouped = interleave(engine, xc_raw[a][:])
+            nc.vector.quantize_mx(out=xc_q[:, a, :].bitcast(FP8X4), scales=xc_s[:, a, :], in_=grouped)
+
+        wd_q = keep.tile([P, N_PAIRS, J_PASSES, 2 * P], U32, name="wd_q", align_bytes=64)
+        wd_s = keep.tile([P, N_PAIRS, J_PASSES, 2 * P], U8, name="wd_s", align_bytes=64)
+        wd_win = [keep.tile([P, T, 2], BF16, name=f"wd_win{i}", align_bytes=64) for i in range(N_PAIRS)]
+        wd_b = {}
+
+        def cast_wd(i, u, engine):
+            copy_on(
+                engine, wd_win[i][:, u * (T // 2) : (u + 1) * (T // 2), :], wd_raw[i, u][:].rearrange("p e t -> p t e")
             )
 
-        wd_q = keep.tile([P, N_TILES, J_PASSES * P], U32, name="wd_q", align_bytes=64)
-        wd_s = keep.tile([P, N_TILES, J_PASSES * P], U8, name="wd_s", align_bytes=64)
-
-        def gather_wd(i):
-            picked = ring.tile([P, S], BF16, name="picked", align_bytes=64)
-            nc.vector.tensor_copy(by_slot(picked[:]), wd_win[i][:].indirect(offsets[:]))
-            wd_b = ring.tile([P, J_PASSES, P, PACK], BF16, name="wd_b", align_bytes=64)
+        def gather_wd(i, pieces):
+            picked = ring.tile([P, S], U32, name="picked", align_bytes=64, bufs=2)
+            window = wd_win[i][:].rearrange("p t e -> p (t e)").bitcast(U32)
+            blocks = S // 32 // pieces
+            for h in range(pieces):
+                nc.vector.tensor_copy(
+                    by_slot(picked[:])[:, h * blocks : (h + 1) * blocks, :, :],
+                    window.indirect(offsets[:, 2 * h * blocks : 2 * (h + 1) * blocks]),
+                )
+            wd_b[i] = ring.tile([P, J_PASSES, 2 * P, PACK], BF16, name="wd_b", align_bytes=64, bufs=1)
             for jb in range(J_PASSES):
-                bank = psum.tile([P, PACK, P], BF16, name="bank", tag="bank", bufs=2)
+                bank = psum.tile([P, PACK, P], F32, name="bank", tag="bank", bufs=2)
                 for t in range(PACK):
-                    nc.tensor.transpose(bank[:, t, :], picked[:, slot_cols(jb, t)], ident_b[:])
-                nc.scalar.copy(wd_b[:, jb, :, :], bank[:].rearrange("p t n -> p n t"))
-            return wd_b
+                    nc.tensor.transpose(bank[:, t, :], picked[:, slot_cols(jb, t)].bitcast(F32), ident_f[:])
+                nc.scalar.copy(wd_b[i][:, jb, :, :], bank[:].bitcast(BF16).rearrange("p t n -> p n t"))
 
-        def quantise_wd(i, wd_b):
-            nc.vector.quantize_mx(
-                out=wd_q[:, i, :].bitcast(FP8X4), scales=wd_s[:, i, :], in_=wd_b[:].rearrange("p b n t -> p (b n t)")
-            )
+        def quantise_wd(i, pieces):
+            step = J_PASSES // pieces
+            for jb in range(0, J_PASSES, step):
+                nc.vector.quantize_mx(
+                    out=wd_q[:, i, jb : jb + step, :].rearrange("p b n -> p (b n)").bitcast(FP8X4),
+                    scales=wd_s[:, i, jb : jb + step, :].rearrange("p b n -> p (b n)"),
+                    in_=wd_b[i][:, jb : jb + step, :, :].rearrange("p b n t -> p (b n t)"),
+                )
 
         h_q = keep.tile([P, J_PASSES, M], U32, name="h_q", align_bytes=64)
         h_s = keep.tile([P, J_PASSES, M], U8, name="h_s", align_bytes=64)
         h_planes = keep.tile([P, J_PASSES, PACK, M], BF16, name="h_planes", align_bytes=64)
 
-        def respond(jb, t):
-            acc = psum.tile([P, M], F32, name="acc", tag="acc", bufs=4)
+        def centre(jb, t):
+            acc = psum.tile([P, M], F32, name="acc", tag="acc", bufs=6)
             cs = slot_cols(jb, t)
             for a in range(K_PASSES):
                 nc.tensor.matmul_mx(
                     out=acc[:],
                     lhsT=v1[a][:, cs].bitcast(FP8X4),
-                    lhsT_scale=v1_s[4 * a : P, cs],
+                    lhsT_scale=planes[1][4 * a : P, cs],
                     rhs=xc_q[:, a, :].bitcast(FP8X4),
                     rhs_scale=xc_s[:, a, :],
                     start=(a == 0),
@@ -218,61 +243,95 @@ def tile_list_sparse_edge_maxout_kernel(
             nc.vector.tensor_tensor(resp[:, jb, t, :], acc[:], resp[:, jb, t, :], ALU.max)
             nc.scalar.activation(h_planes[:, jb, t, :], resp[:, jb, t, :], ACT.Copy, scale=cols[:, jb, t : t + 1])
 
-        def group_h(jb):
-            grouped = ring.tile([P, M, PACK], BF16, name="grouped", align_bytes=64)
-            nc.scalar.copy(
-                grouped[:].rearrange("p (c i) t -> p c t i", i=4),
-                h_planes[:, jb, :, :].rearrange("p t (c i) -> p c t i", i=4),
-            )
-            return grouped
-
-        def quantise_h(jb, grouped):
-            nc.vector.quantize_mx(
-                out=h_q[:, jb, :].bitcast(FP8X4), scales=h_s[:, jb, :], in_=grouped[:].rearrange("p m t -> p (m t)")
-            )
+        def quantise_h(jb, engine):
+            grouped = interleave(engine, h_planes[:, jb, :, :])
+            nc.vector.quantize_mx(out=h_q[:, jb, :].bitcast(FP8X4), scales=h_s[:, jb, :], in_=grouped)
 
         def project(i):
-            y = psum.tile([P, M], F32, name="y", tag="y", bufs=2)
+            y = psum.tile([P, M], F32, name="y", tag="acc", bufs=6)
+            cs = slice(i % 2 * P, (i % 2 + 1) * P)
             for jb in range(J_PASSES):
-                cs = slice(jb * P, (jb + 1) * P)
                 nc.tensor.matmul_mx(
                     out=y[:],
-                    lhsT=wd_q[:, i, cs].bitcast(FP8X4),
-                    lhsT_scale=wd_s[:, i, cs],
+                    lhsT=wd_q[:, i // 2, jb, cs].bitcast(FP8X4),
+                    lhsT_scale=wd_s[:, i // 2, jb, cs],
                     rhs=h_q[:, jb, :].bitcast(FP8X4),
                     rhs_scale=h_s[:, jb, :],
                     start=(jb == 0),
                     stop=(jb == J_PASSES - 1),
                 )
-            res = ring.tile([P, M], F32, name="res", align_bytes=64, bufs=3)
+            res = ring.tile([P, M], F32, name="res", align_bytes=64, bufs=4)
             nc.vector.scalar_tensor_tensor(
                 res[:], y[:], cols[:, 0, BIAS_ROW + i : BIAS_ROW + i + 1], ew_all[:], ALU.add, ALU.mult
             )
             nc.sync.dma_start(out[i * P : (i + 1) * P, :], res[:])
 
-        w0 = gather_wd(0)
-        for t in range(PACK):
-            respond(0, t)
-        quantise_wd(0, w0)
-        w1 = gather_wd(1)
-        h0 = group_h(0)
-        for t in range(PACK):
-            respond(1, t)
-        quantise_wd(1, w1)
-        w2 = gather_wd(2)
-        quantise_h(0, h0)
-        h1 = group_h(1)
-        w3 = gather_wd(3)
-        quantise_wd(2, w2)
-        quantise_h(1, h1)
-        w4 = gather_wd(4)
-        quantise_wd(3, w3)
-        project(0)
-        project(1)
-        w5 = gather_wd(5)
-        quantise_wd(4, w4)
+        win2[1] = load_words(tab2_words, 1, "win2_1")
+        load_xn_words()
+        load_scales(swin2, tab2_scales)
+        win2[0] = load_words(tab2_words, 0, "win2_0")
+        win2[2] = load_words(tab2_words, 2, "win2_2")
+        v2[2] = gather_words(win2[2], "v2_2")
+        v2[0] = gather_words(win2[0], "v2_0")
+        load_scales(swin1, tab_scales)
+        wd_raw[0, 0] = load_wd(0, 0)
+        load_xn_scales()
+        wd_raw[0, 1] = load_wd(0, 1)
+        xc_raw[0] = load_xc(0)
+        load_vectors()
+        constants()
+        planes[2] = gather_scales(swin2, "v2_s")
+        shift_planes()
+        win1[0] = load_words(tab_words, 0, "win1_0")
+        xc_raw[1] = load_xc(1)
+        win1[1] = load_words(tab_words, 1, "win1_1")
+        win1[2] = load_words(tab_words, 2, "win1_2")
+        v1[2] = gather_words(win1[2], "v1_2")
+        v1[0] = gather_words(win1[0], "v1_0")
+        quantise_xc(0, "S")
+        v2[1] = gather_words(win2[1], "v2_1")
+        v1[1] = gather_words(win1[1], "v1_1")
+        xc_raw[2] = load_xc(2)
+        wd_raw[1, 0] = load_wd(1, 0)
+        cast_wd(1, 0, "S")
+        neighbour(0, 1)
+        neighbour(0, 3)
+        quantise_xc(1, "V")
+        neighbour(0, 0)
+        neighbour(1, 3)
+        wd_raw[1, 1] = load_wd(1, 1)
+        cast_wd(1, 1, "S")
+        neighbour(0, 2)
+        neighbour(1, 1)
+        planes[1] = gather_scales(swin1, "v1_s")
+        quantise_xc(2, "S")
+        cast_wd(0, 0, "S")
+        neighbour(1, 0)
+        centre(0, 3)
+        centre(0, 0)
+        cast_wd(0, 1, "S")
+        centre(0, 2)
+        gather_wd(0, 1)
+        neighbour(1, 2)
+        centre(1, 1)
+        centre(1, 0)
+        wd_raw[2, 1] = load_wd(2, 1)
+        centre(0, 1)
+        quantise_h(0, "S")
+        centre(1, 2)
+        centre(1, 3)
+        gather_wd(1, 1)
+        cast_wd(2, 1, "V")
+        wd_raw[2, 0] = load_wd(2, 0)
+        cast_wd(2, 0, "V")
+        quantise_h(1, "S")
+        quantise_wd(0, 1)
+        quantise_wd(1, 1)
         project(2)
+        gather_wd(2, 2)
+        project(0)
+        quantise_wd(2, 2)
         project(3)
-        project(4)
-        quantise_wd(5, w5)
         project(5)
+        project(1)
+        project(4)

@@ -4,7 +4,7 @@ import concourse.mybir as mybir
 from concourse.masks import make_identity
 
 K, T, S, M, N = 1536, 2048, 1024, 512, 768
-FLOPS = 2 * K * S * M * 2 + 2 * N * S * M
+FLOPS = 2 * (2 * K * S * M) + 2 * N * S * M
 
 F32 = mybir.dt.float32
 BF16 = mybir.dt.bfloat16
@@ -15,22 +15,28 @@ U8 = mybir.dt.uint8
 FP8X4 = mybir.dt.float8_e4m3fn_x4
 FP4X4 = mybir.dt.float4_e2m1fn_x4
 ALU = mybir.AluOpType
-ACT = mybir.ActivationFunctionType
 
 P = 128
 PACK = 4
+RUN = 8
 K_PASSES = K // (P * PACK)
 J_PASSES = S // (P * PACK)
 N_TILES = N // P
 N_PAIRS = N_TILES // 2
 QUADS = 4
+PLANE_ROWS = 4
 SHIFT_ROWS = 112
 BIAS_ROW = PACK
 EW_ROW = BIAS_ROW + N_TILES
+VEC_ROWS = 16
+RAW_BUFS = 5
+SUM_BANKS = 6
+TURN_BANKS = 2
+RESULT_BUFS = 4
 
 
-def by_slot(ap):
-    return ap.rearrange("p (t c r) -> p c t r", t=PACK, r=8)
+def in_slot_order(ap):
+    return ap.rearrange("p (t c r) -> p c t r", t=PACK, r=RUN)
 
 
 def slot_cols(jb, t):
@@ -50,288 +56,253 @@ def tile_list_sparse_edge_maxout_kernel(
         offsets = keep.tile([P, S // 16], U16, name="offsets")
         nc.sync.dma_start(offsets[:], offs)
 
-        swin2 = keep.tile([P, T // 4], I32, name="swin2", align_bytes=64)
-        swin1 = keep.tile([P, T // 4], I32, name="swin1", align_bytes=64)
-        xn_s = keep.tile([P, K_PASSES, M // 4], I32, name="xn_s", align_bytes=64)
-        small = keep.tile([P, 2 * P], F32, name="small", align_bytes=64)
-        moved = keep.tile([P, K_PASSES - 1, S // 4], I32, name="moved", align_bytes=64)
-        nc.gpsimd.memset(swin2[:], 0)
-        nc.vector.memset(swin1[:], 0)
-        nc.vector.memset(small[:], 0.0)
-        nc.vector.memset(xn_s[:], 0)
-        nc.vector.memset(moved[:], 0)
-        ident_f = keep.tile([P, P], F32, name="ident_f", align_bytes=64)
-        make_identity(nc, ident_f[:])
+        v2_scale_win = keep.tile([P, T // 4], I32, name="v2_scale_win", align_bytes=64)
+        v_scale_win = keep.tile([P, T // 4], I32, name="v_scale_win", align_bytes=64)
+        xn_planes = keep.tile([P, K_PASSES, M // 4], I32, name="xn_planes", align_bytes=64)
+        vec_rows = keep.tile([P, J_PASSES * P], F32, name="vec_rows", align_bytes=64)
+        v2_moved = keep.tile([P, K_PASSES - 1, S // 4], I32, name="v2_moved", align_bytes=64)
+        identity = keep.tile([P, P], F32, name="identity", align_bytes=64)
+        nc.gpsimd.memset(v2_scale_win[:], 0)
+        nc.vector.memset(v_scale_win[:], 0)
+        nc.vector.memset(vec_rows[:], 0.0)
+        nc.vector.memset(xn_planes[:], 0)
+        nc.vector.memset(v2_moved[:], 0)
+        nc.vector.memset(identity[:], 0.0)
 
-        def load_vectors():
-            nc.sync.dma_start(
-                small[0:PACK, :].rearrange("t (c r) -> t c r", r=8), g.rearrange("(c t r) -> t c r", t=PACK, r=8)
-            )
-            nc.sync.dma_start(small[BIAS_ROW:EW_ROW, 0:P], b.rearrange("(i p) -> i p", p=P))
-            nc.sync.dma_start(small[EW_ROW : EW_ROW + M // P, 0:P], ew.rearrange("(c p) -> c p", p=P))
+        for win, src in ((v2_scale_win, tab2_scales), (v_scale_win, tab_scales)):
+            for q in range(QUADS):
+                nc.gpsimd.dma_start(
+                    win[32 * q : 32 * q + PLANE_ROWS * K_PASSES, :],
+                    src[:, PLANE_ROWS * q : PLANE_ROWS * (q + 1), :].bitcast(I32),
+                )
+        make_identity(nc, identity[:], nomemset=True)
 
         def load_words(src, a, name):
-            win = keep.tile([P, T], I32, name=name, align_bytes=64)
-            nc.sync.dma_start(win[:], src[a].rearrange("p n t -> p (n t)").bitcast(I32))
+            win = keep.tile([P, T], I32, name=f"{name}{a}", align_bytes=64)
+            nc.sync.dma_start(win[:], src[a].rearrange("p n i -> p (n i)").bitcast(I32))
             return win
 
-        def load_scales(win, src):
-            for q in range(QUADS):
-                nc.sync.dma_start(win[32 * q : 32 * q + 4 * K_PASSES, :], src[:, 4 * q : 4 * q + 4, :].bitcast(I32))
-
         def load_xc(a):
-            raw = ring.tile([P, PACK, M], F32, name="xc_raw", tag="raw", align_bytes=64, bufs=3)
+            raw = ring.tile([P, PACK, M], F32, name="xc_raw", tag="raw", align_bytes=64, bufs=RAW_BUFS)
             nc.sync.dma_start(raw[:], xc[a * P * PACK : (a + 1) * P * PACK, :].rearrange("(p i) m -> p i m", i=PACK))
             return raw
 
-        def load_wd(i, u):
-            rows = wdT[2 * i * P : 2 * (i + 1) * P, :].rearrange("(p e) t -> p e t", e=2)
-            raw = ring.tile([P, 2, T // 2], F32, name="wd_raw", tag="raw", align_bytes=64, bufs=3)
-            nc.sync.dma_start(raw[:], rows[:, :, u * (T // 2) : (u + 1) * (T // 2)])
+        def load_wd(pair, half):
+            rows = wdT[2 * pair * P : 2 * (pair + 1) * P, :].rearrange("(p e) t -> p e t", e=2)
+            raw = ring.tile([P, 2, T // 2], F32, name="wd_raw", tag="raw", align_bytes=64, bufs=RAW_BUFS)
+            nc.sync.dma_start(raw[:], rows[:, :, half * (T // 2) : (half + 1) * (T // 2)])
             return raw
 
         def load_xn_scales():
             for q in range(QUADS):
                 nc.sync.dma_start(
-                    xn_s[32 * q : 32 * q + 4, :, :],
-                    xn_scales[:, 4 * q : 4 * q + 4, :].rearrange("a r m -> r a m").bitcast(I32),
+                    xn_planes[32 * q : 32 * q + PLANE_ROWS, :, :],
+                    xn_scales[:, PLANE_ROWS * q : PLANE_ROWS * (q + 1), :].rearrange("a r m -> r a m").bitcast(I32),
                 )
 
-        xn_w = keep.tile([P, K_PASSES, 2 * M], U8, name="xn_w", align_bytes=64)
-
-        def load_xn_words():
-            nc.sync.dma_start(xn_w[:].bitcast(I32), xn_words.rearrange("a p c -> p a c").bitcast(I32))
-
-        win1, win2, xc_raw, wd_raw = {}, {}, {}, {}
-
-        cols = keep.tile([P, J_PASSES, 16], F32, name="cols", align_bytes=64)
-        ew_all = keep.tile([P, M], F32, name="ew_all", align_bytes=64)
-
-        def constants():
-            turned = psum.tile([P, J_PASSES, P], F32, name="turned", tag="bank", bufs=2)
-            for jb in range(J_PASSES):
-                nc.tensor.transpose(turned[:, jb, :], small[:, jb * P : (jb + 1) * P], ident_f[:])
-            nc.scalar.copy(cols[:], turned[:, :, 0:16])
-            spread = psum.tile([P, M // P, P], F32, name="spread", tag="bank", bufs=2)
-            for c in range(M // P):
-                nc.tensor.transpose(
-                    spread[:, c, :], cols[:, 0, EW_ROW + c : EW_ROW + c + 1].to_broadcast([P, P]), ident_f[:]
-                )
-            nc.scalar.copy(ew_all[:], spread[:].rearrange("p c m -> p (c m)"))
-
-        def copy_on(engine, dst, src):
-            if engine == "V":
-                nc.vector.tensor_copy(dst, src)
-            elif engine == "G":
-                nc.gpsimd.tensor_scalar(dst, src, 1.0, 0.0, ALU.mult, ALU.add)
-            else:
-                nc.scalar.copy(dst, src)
-
-        def gather_words(win, name):
-            got = keep.tile([P, S], U32, name=name, align_bytes=64)
-            nc.vector.tensor_copy(by_slot(got[:]), win[:].bitcast(U32).indirect(offsets[:]))
-            return got
-
-        def gather_scales(win, name):
-            got = keep.tile([P, S], U8, name=name + "_listed", align_bytes=64)
-            nc.vector.tensor_copy(got[:], win[:].bitcast(U8).indirect(offsets[:]))
-            ordered = keep.tile([P, S], U8, name=name, align_bytes=64)
-            nc.vector.tensor_copy(
-                ordered[:].bitcast(I32).rearrange("p (t c w) -> p t c w", t=PACK, w=2),
-                got[:].bitcast(I32).rearrange("p (c t w) -> p t c w", t=PACK, w=2),
+        def load_vectors():
+            nc.sync.dma_start(
+                vec_rows[0:PACK, :].rearrange("t (c r) -> t c r", r=RUN),
+                g.rearrange("(c t r) -> t c r", t=PACK, r=RUN),
             )
-            return ordered
+            nc.sync.dma_start(vec_rows[BIAS_ROW:EW_ROW, 0:P], b.rearrange("(i p) -> i p", p=P))
+            nc.sync.dma_start(vec_rows[EW_ROW : EW_ROW + M // P, 0:P], ew.rearrange("(c p) -> c p", p=P))
 
-        v1, v2, planes = {}, {}, {}
+        def pick_words(win, name):
+            picked = keep.tile([P, S], U32, name=name, align_bytes=64)
+            nc.vector.tensor_copy(in_slot_order(picked[:]), win[:].bitcast(U32).indirect(offsets[:]))
+            return picked
 
-        def shift_planes():
-            for a in range(1, K_PASSES):
-                nc.sync.dma_start(
-                    moved[0:SHIFT_ROWS, a - 1, :], planes[2][4 * a : 4 * a + SHIFT_ROWS, :].bitcast(I32)
-                )
+        def pick_scales(win, name):
+            listed = keep.tile([P, S], U8, name=name + "_listed", align_bytes=64)
+            nc.vector.tensor_copy(listed[:], win[:].bitcast(U8).indirect(offsets[:]))
+            planes = keep.tile([P, S], U8, name=name, align_bytes=64)
+            nc.vector.tensor_copy(
+                planes[:].bitcast(I32).rearrange("p (t c w) -> p t c w", t=PACK, w=RUN // 4),
+                listed[:].bitcast(I32).rearrange("p (c t w) -> p t c w", t=PACK, w=RUN // 4),
+            )
+            return planes
 
-        def v2_plane(a, cs):
-            if a == 0:
-                return planes[2][:, cs]
-            return moved[:, a - 1, :].bitcast(U8)[:, cs]
+        v2_win, v_win, xc_raw, wd_raw = {}, {}, {}, {}
+        v2_win[0] = load_words(tab2_words, 0, "v2_win")
+        v2_win[1] = load_words(tab2_words, 1, "v2_win")
+        load_xn_scales()
+        v2_win[2] = load_words(tab2_words, 2, "v2_win")
+        load_vectors()
+        wd_raw[0, 0] = load_wd(0, 0)
+        xc_raw[0] = load_xc(0)
+        wd_raw[0, 1] = load_wd(0, 1)
+
+        v2_codes = [pick_words(v2_win[a], f"v2_codes{a}") for a in range(K_PASSES - 1)]
+        v2_planes = pick_scales(v2_scale_win, "v2_planes")
+        for a in range(1, K_PASSES):
+            nc.sync.dma_start(
+                v2_moved[0:SHIFT_ROWS, a - 1, :], v2_planes[PLANE_ROWS * a : PLANE_ROWS * a + SHIFT_ROWS, :].bitcast(I32)
+            )
+
+        xn_codes = keep.tile([P, K_PASSES, 2 * M], U8, name="xn_codes", align_bytes=64)
+        nc.sync.dma_start(xn_codes[:].bitcast(I32), xn_words.rearrange("a p c -> p a c").bitcast(I32))
+        v_win[0] = load_words(tab_words, 0, "v_win")
+        v_win[1] = load_words(tab_words, 1, "v_win")
+        xc_raw[1] = load_xc(1)
+        v_win[2] = load_words(tab_words, 2, "v_win")
+        xc_raw[2] = load_xc(2)
+        for pair in range(1, N_PAIRS):
+            for half in range(2):
+                wd_raw[pair, half] = load_wd(pair, half)
+
+        v2_codes.append(pick_words(v2_win[K_PASSES - 1], f"v2_codes{K_PASSES - 1}"))
+        v_planes = pick_scales(v_scale_win, "v_planes")
+        v_codes = [pick_words(v_win[a], f"v_codes{a}") for a in range(K_PASSES)]
+
+        def interleave(copy, planes):
+            grouped = ring.tile([P, M, PACK], BF16, name="grouped", align_bytes=64)
+            copy(grouped[:].rearrange("p (c i) t -> p c t i", i=4), planes.rearrange("p t (c i) -> p c t i", i=4))
+            return grouped[:].rearrange("p m t -> p (m t)")
+
+        xc_codes = keep.tile([P, K_PASSES, M], U32, name="xc_codes", align_bytes=64)
+        xc_planes = keep.tile([P, K_PASSES, M], U8, name="xc_planes", align_bytes=64)
+
+        def quantise_xc(a, copy):
+            grouped = interleave(copy, xc_raw[a][:])
+            nc.vector.quantize_mx(out=xc_codes[:, a, :].bitcast(FP8X4), scales=xc_planes[:, a, :], in_=grouped)
+
+        wd_win = [keep.tile([P, T, 2], BF16, name=f"wd_win{pair}", align_bytes=64) for pair in range(N_PAIRS)]
+
+        def round_wd(pair, half, copy):
+            copy(
+                wd_win[pair][:, half * (T // 2) : (half + 1) * (T // 2), :],
+                wd_raw[pair, half][:].rearrange("p e t -> p t e"),
+            )
+
+        on_scalar, on_vector = nc.scalar.copy, nc.vector.tensor_copy
+        round_wd(0, 0, on_scalar)
+        round_wd(0, 1, on_scalar)
+        quantise_xc(0, on_scalar)
+        quantise_xc(1, on_vector)
+        quantise_xc(2, on_scalar)
+        round_wd(1, 0, on_scalar)
+        round_wd(1, 1, on_scalar)
+        round_wd(2, 0, on_scalar)
+
+        vec_cols = keep.tile([P, J_PASSES, VEC_ROWS], F32, name="vec_cols", align_bytes=64)
+        turned = psum.tile([P, J_PASSES, P], F32, name="turned", tag="turn", bufs=TURN_BANKS)
+        for jb in range(J_PASSES):
+            nc.tensor.transpose(turned[:, jb, :], vec_rows[:, jb * P : (jb + 1) * P], identity[:])
+        nc.scalar.copy(vec_cols[:], turned[:, :, 0:VEC_ROWS])
+        spread = psum.tile([P, M // P, P], F32, name="spread", tag="turn", bufs=TURN_BANKS)
+        for c in range(M // P):
+            column = vec_cols[:, 0, EW_ROW + c : EW_ROW + c + 1]
+            nc.tensor.transpose(spread[:, c, :], column.to_broadcast([P, P]), identity[:])
+        ew_all = keep.tile([P, M], F32, name="ew_all", align_bytes=64)
+        nc.scalar.copy(ew_all[:], spread[:].rearrange("p c m -> p (c m)"))
 
         resp = keep.tile([P, J_PASSES, PACK, M], F32, name="resp", align_bytes=64)
+        h_rows = keep.tile([P, J_PASSES, PACK, M], BF16, name="h_rows", align_bytes=64)
 
-        def neighbour(jb, t):
-            acc = psum.tile([P, M], F32, name="acc", tag="acc", bufs=6)
-            cs = slot_cols(jb, t)
+        def neighbour_product(jb, t):
+            acc = psum.tile([P, M], F32, name="acc", tag="sum", bufs=SUM_BANKS)
+            cols = slot_cols(jb, t)
             for a in range(K_PASSES):
+                plane = v2_planes[:] if a == 0 else v2_moved[:, a - 1, :].bitcast(U8)
                 nc.tensor.matmul_mx(
                     out=acc[:],
-                    lhsT=v2[a][:, cs].bitcast(FP8X4),
-                    lhsT_scale=v2_plane(a, cs),
-                    rhs=xn_w[:, a, :].bitcast(FP4X4),
-                    rhs_scale=xn_s[:, a, :].bitcast(U8),
+                    lhsT=v2_codes[a][:, cols].bitcast(FP8X4),
+                    lhsT_scale=plane[:, cols],
+                    rhs=xn_codes[:, a, :].bitcast(FP4X4),
+                    rhs_scale=xn_planes[:, a, :].bitcast(U8),
                     start=(a == 0),
                     stop=(a == K_PASSES - 1),
                 )
             nc.scalar.copy(resp[:, jb, t, :], acc[:])
 
-        def interleave(engine, planes_ap):
-            grouped = ring.tile([P, M, PACK], BF16, name="grouped", align_bytes=64, bufs=2)
-            copy_on(
-                engine,
-                grouped[:].rearrange("p (c i) t -> p c t i", i=4),
-                planes_ap.rearrange("p t (c i) -> p c t i", i=4),
-            )
-            return grouped[:].rearrange("p m t -> p (m t)")
-
-        xc_q = keep.tile([P, K_PASSES, M], U32, name="xc_q", align_bytes=64)
-        xc_s = keep.tile([P, K_PASSES, M], U8, name="xc_s", align_bytes=64)
-
-        def quantise_xc(a, engine):
-            grouped = interleave(engine, xc_raw[a][:])
-            nc.vector.quantize_mx(out=xc_q[:, a, :].bitcast(FP8X4), scales=xc_s[:, a, :], in_=grouped)
-
-        wd_q = keep.tile([P, N_PAIRS, J_PASSES, 2 * P], U32, name="wd_q", align_bytes=64)
-        wd_s = keep.tile([P, N_PAIRS, J_PASSES, 2 * P], U8, name="wd_s", align_bytes=64)
-        wd_win = [keep.tile([P, T, 2], BF16, name=f"wd_win{i}", align_bytes=64) for i in range(N_PAIRS)]
-        wd_b = {}
-
-        def cast_wd(i, u, engine):
-            copy_on(
-                engine, wd_win[i][:, u * (T // 2) : (u + 1) * (T // 2), :], wd_raw[i, u][:].rearrange("p e t -> p t e")
-            )
-
-        def gather_wd(i, pieces):
-            picked = ring.tile([P, S], U32, name="picked", align_bytes=64, bufs=2)
-            window = wd_win[i][:].rearrange("p t e -> p (t e)").bitcast(U32)
-            blocks = S // 32 // pieces
-            for h in range(pieces):
-                nc.vector.tensor_copy(
-                    by_slot(picked[:])[:, h * blocks : (h + 1) * blocks, :, :],
-                    window.indirect(offsets[:, 2 * h * blocks : 2 * (h + 1) * blocks]),
-                )
-            wd_b[i] = ring.tile([P, J_PASSES, 2 * P, PACK], BF16, name="wd_b", align_bytes=64, bufs=1)
-            for jb in range(J_PASSES):
-                bank = psum.tile([P, PACK, P], F32, name="bank", tag="bank", bufs=2)
-                for t in range(PACK):
-                    nc.tensor.transpose(bank[:, t, :], picked[:, slot_cols(jb, t)].bitcast(F32), ident_f[:])
-                nc.scalar.copy(wd_b[i][:, jb, :, :], bank[:].bitcast(BF16).rearrange("p t n -> p n t"))
-
-        def quantise_wd(i, pieces):
-            step = J_PASSES // pieces
-            for jb in range(0, J_PASSES, step):
-                nc.vector.quantize_mx(
-                    out=wd_q[:, i, jb : jb + step, :].rearrange("p b n -> p (b n)").bitcast(FP8X4),
-                    scales=wd_s[:, i, jb : jb + step, :].rearrange("p b n -> p (b n)"),
-                    in_=wd_b[i][:, jb : jb + step, :, :].rearrange("p b n t -> p (b n t)"),
-                )
-
-        h_q = keep.tile([P, J_PASSES, M], U32, name="h_q", align_bytes=64)
-        h_s = keep.tile([P, J_PASSES, M], U8, name="h_s", align_bytes=64)
-        h_planes = keep.tile([P, J_PASSES, PACK, M], BF16, name="h_planes", align_bytes=64)
-
-        def centre(jb, t):
-            acc = psum.tile([P, M], F32, name="acc", tag="acc", bufs=6)
-            cs = slot_cols(jb, t)
+        def centre_product(jb, t):
+            acc = psum.tile([P, M], F32, name="acc", tag="sum", bufs=SUM_BANKS)
+            cols = slot_cols(jb, t)
             for a in range(K_PASSES):
                 nc.tensor.matmul_mx(
                     out=acc[:],
-                    lhsT=v1[a][:, cs].bitcast(FP8X4),
-                    lhsT_scale=planes[1][4 * a : P, cs],
-                    rhs=xc_q[:, a, :].bitcast(FP8X4),
-                    rhs_scale=xc_s[:, a, :],
+                    lhsT=v_codes[a][:, cols].bitcast(FP8X4),
+                    lhsT_scale=v_planes[PLANE_ROWS * a : P, cols],
+                    rhs=xc_codes[:, a, :].bitcast(FP8X4),
+                    rhs_scale=xc_planes[:, a, :],
                     start=(a == 0),
                     stop=(a == K_PASSES - 1),
                 )
             nc.vector.tensor_tensor(resp[:, jb, t, :], acc[:], resp[:, jb, t, :], ALU.max)
-            nc.scalar.activation(h_planes[:, jb, t, :], resp[:, jb, t, :], ACT.Copy, scale=cols[:, jb, t : t + 1])
+            gain = vec_cols[:, jb, t : t + 1]
+            nc.gpsimd.tensor_scalar(h_rows[:, jb, t, :], resp[:, jb, t, :], gain, 0.0, ALU.mult, ALU.add)
 
-        def quantise_h(jb, engine):
-            grouped = interleave(engine, h_planes[:, jb, :, :])
-            nc.vector.quantize_mx(out=h_q[:, jb, :].bitcast(FP8X4), scales=h_s[:, jb, :], in_=grouped)
+        h_codes = keep.tile([P, J_PASSES, M], U32, name="h_codes", align_bytes=64)
+        h_planes = keep.tile([P, J_PASSES, M], U8, name="h_planes", align_bytes=64)
+
+        def quantise_h(jb, copy):
+            grouped = interleave(copy, h_rows[:, jb, :, :])
+            nc.vector.quantize_mx(out=h_codes[:, jb, :].bitcast(FP8X4), scales=h_planes[:, jb, :], in_=grouped)
+
+        wd_codes = keep.tile([P, N_PAIRS, J_PASSES, 2 * P], U32, name="wd_codes", align_bytes=64)
+        wd_planes = keep.tile([P, N_PAIRS, J_PASSES, 2 * P], U8, name="wd_planes", align_bytes=64)
+
+        def pick_wd(pair, pieces):
+            picked = ring.tile([P, S], U32, name="wd_picked", align_bytes=64)
+            window = wd_win[pair][:].rearrange("p t e -> p (t e)").bitcast(U32)
+            blocks = S // (PACK * RUN) // pieces
+            for piece in range(pieces):
+                nc.vector.tensor_copy(
+                    in_slot_order(picked[:])[:, piece * blocks : (piece + 1) * blocks, :, :],
+                    window.indirect(offsets[:, 2 * piece * blocks : 2 * (piece + 1) * blocks]),
+                )
+            grouped = ring.tile([P, J_PASSES, 2 * P, PACK], BF16, name="wd_grouped", align_bytes=64)
+            for jb in range(J_PASSES):
+                bank = psum.tile([P, PACK, P], F32, name="bank", tag="turn", bufs=TURN_BANKS)
+                for t in range(PACK):
+                    nc.tensor.transpose(bank[:, t, :], picked[:, slot_cols(jb, t)].bitcast(F32), identity[:])
+                nc.scalar.copy(grouped[:, jb, :, :], bank[:].bitcast(BF16).rearrange("p t n -> p n t"))
+            return grouped
+
+        def quantise_wd(pair, grouped, pieces):
+            step = J_PASSES // pieces
+            for jb in range(0, J_PASSES, step):
+                nc.vector.quantize_mx(
+                    out=wd_codes[:, pair, jb : jb + step, :].rearrange("p b n -> p (b n)").bitcast(FP8X4),
+                    scales=wd_planes[:, pair, jb : jb + step, :].rearrange("p b n -> p (b n)"),
+                    in_=grouped[:, jb : jb + step, :, :].rearrange("p b n t -> p (b n t)"),
+                )
 
         def project(i):
-            y = psum.tile([P, M], F32, name="y", tag="acc", bufs=6)
-            cs = slice(i % 2 * P, (i % 2 + 1) * P)
+            acc = psum.tile([P, M], F32, name="acc", tag="sum", bufs=SUM_BANKS)
+            cols = slice(i % 2 * P, (i % 2 + 1) * P)
             for jb in range(J_PASSES):
                 nc.tensor.matmul_mx(
-                    out=y[:],
-                    lhsT=wd_q[:, i // 2, jb, cs].bitcast(FP8X4),
-                    lhsT_scale=wd_s[:, i // 2, jb, cs],
-                    rhs=h_q[:, jb, :].bitcast(FP8X4),
-                    rhs_scale=h_s[:, jb, :],
+                    out=acc[:],
+                    lhsT=wd_codes[:, i // 2, jb, cols].bitcast(FP8X4),
+                    lhsT_scale=wd_planes[:, i // 2, jb, cols],
+                    rhs=h_codes[:, jb, :].bitcast(FP8X4),
+                    rhs_scale=h_planes[:, jb, :],
                     start=(jb == 0),
                     stop=(jb == J_PASSES - 1),
                 )
-            res = ring.tile([P, M], F32, name="res", align_bytes=64, bufs=4)
-            nc.vector.scalar_tensor_tensor(
-                res[:], y[:], cols[:, 0, BIAS_ROW + i : BIAS_ROW + i + 1], ew_all[:], ALU.add, ALU.mult
-            )
-            nc.sync.dma_start(out[i * P : (i + 1) * P, :], res[:])
+            result = ring.tile([P, M], F32, name="result", align_bytes=64, bufs=RESULT_BUFS)
+            bias = vec_cols[:, 0, BIAS_ROW + i : BIAS_ROW + i + 1]
+            nc.vector.scalar_tensor_tensor(result[:], acc[:], bias, ew_all[:], ALU.add, ALU.mult)
+            nc.sync.dma_start(out[i * P : (i + 1) * P, :], result[:])
 
-        win2[1] = load_words(tab2_words, 1, "win2_1")
-        load_xn_words()
-        load_scales(swin2, tab2_scales)
-        win2[0] = load_words(tab2_words, 0, "win2_0")
-        win2[2] = load_words(tab2_words, 2, "win2_2")
-        v2[2] = gather_words(win2[2], "v2_2")
-        v2[0] = gather_words(win2[0], "v2_0")
-        load_scales(swin1, tab_scales)
-        wd_raw[0, 0] = load_wd(0, 0)
-        load_xn_scales()
-        wd_raw[0, 1] = load_wd(0, 1)
-        xc_raw[0] = load_xc(0)
-        load_vectors()
-        constants()
-        planes[2] = gather_scales(swin2, "v2_s")
-        shift_planes()
-        win1[0] = load_words(tab_words, 0, "win1_0")
-        xc_raw[1] = load_xc(1)
-        win1[1] = load_words(tab_words, 1, "win1_1")
-        win1[2] = load_words(tab_words, 2, "win1_2")
-        v1[2] = gather_words(win1[2], "v1_2")
-        v1[0] = gather_words(win1[0], "v1_0")
-        quantise_xc(0, "S")
-        v2[1] = gather_words(win2[1], "v2_1")
-        v1[1] = gather_words(win1[1], "v1_1")
-        xc_raw[2] = load_xc(2)
-        wd_raw[1, 0] = load_wd(1, 0)
-        cast_wd(1, 0, "S")
-        neighbour(0, 1)
-        neighbour(0, 3)
-        quantise_xc(1, "V")
-        neighbour(0, 0)
-        neighbour(1, 3)
-        wd_raw[1, 1] = load_wd(1, 1)
-        cast_wd(1, 1, "S")
-        neighbour(0, 2)
-        neighbour(1, 1)
-        planes[1] = gather_scales(swin1, "v1_s")
-        quantise_xc(2, "S")
-        cast_wd(0, 0, "S")
-        neighbour(1, 0)
-        centre(0, 3)
-        centre(0, 0)
-        cast_wd(0, 1, "S")
-        centre(0, 2)
-        gather_wd(0, 1)
-        neighbour(1, 2)
-        centre(1, 1)
-        centre(1, 0)
-        wd_raw[2, 1] = load_wd(2, 1)
-        centre(0, 1)
-        quantise_h(0, "S")
-        centre(1, 2)
-        centre(1, 3)
-        gather_wd(1, 1)
-        cast_wd(2, 1, "V")
-        wd_raw[2, 0] = load_wd(2, 0)
-        cast_wd(2, 0, "V")
-        quantise_h(1, "S")
-        quantise_wd(0, 1)
-        quantise_wd(1, 1)
-        project(2)
-        gather_wd(2, 2)
+        for t in range(PACK):
+            neighbour_product(0, t)
+        quantise_wd(0, pick_wd(0, 1), 1)
+        for t in range(PACK):
+            neighbour_product(1, t)
+        for jb in range(J_PASSES):
+            for t in range(PACK):
+                centre_product(jb, t)
+        quantise_h(0, on_scalar)
+        grouped_1 = pick_wd(1, 1)
+        quantise_h(1, on_vector)
+        round_wd(2, 1, on_vector)
+        grouped_2 = pick_wd(2, J_PASSES)
         project(0)
-        quantise_wd(2, 2)
-        project(3)
-        project(5)
         project(1)
-        project(4)
+        quantise_wd(1, grouped_1, 1)
+        quantise_wd(2, grouped_2, J_PASSES)
+        for i in range(2, N_TILES):
+            project(i)

@@ -22,16 +22,19 @@ RUN = 8
 K_PASSES = K // (P * PACK)
 J_PASSES = S // (P * PACK)
 N_TILES = N // P
-N_PAIRS = N_TILES // 2
+N_PAIRS = 2
+N_SINGLES = N_TILES - 2 * N_PAIRS
 QUADS = 4
 PLANE_ROWS = 4
 SHIFT_ROWS = 112
-BIAS_ROW = PACK
-EW_ROW = BIAS_ROW + N_TILES
-VEC_ROWS = 16
-RAW_BUFS = 5
+BIAS_ROW = J_PASSES
+BIAS_TILES = N_TILES // 2
+EW_ROW = BIAS_ROW + 2
+VEC_ROWS = 8
+RAW_BUFS = 4
 SUM_BANKS = 6
 TURN_BANKS = 2
+GROUPED_BUFS = 3
 RESULT_BUFS = 4
 
 
@@ -59,7 +62,7 @@ def tile_list_sparse_edge_maxout_kernel(
         v2_scale_win = keep.tile([P, T // 4], I32, name="v2_scale_win", align_bytes=64)
         v_scale_win = keep.tile([P, T // 4], I32, name="v_scale_win", align_bytes=64)
         xn_planes = keep.tile([P, K_PASSES, M // 4], I32, name="xn_planes", align_bytes=64)
-        vec_rows = keep.tile([P, J_PASSES * P], F32, name="vec_rows", align_bytes=64)
+        vec_rows = keep.tile([P, PACK * P], F32, name="vec_rows", align_bytes=64)
         v2_moved = keep.tile([P, K_PASSES - 1, S // 4], I32, name="v2_moved", align_bytes=64)
         identity = keep.tile([P, P], F32, name="identity", align_bytes=64)
         nc.gpsimd.memset(v2_scale_win[:], 0)
@@ -67,20 +70,21 @@ def tile_list_sparse_edge_maxout_kernel(
         nc.vector.memset(vec_rows[:], 0.0)
         nc.vector.memset(xn_planes[:], 0)
         nc.vector.memset(v2_moved[:], 0)
-        nc.vector.memset(identity[:], 0.0)
-
-        for win, src in ((v2_scale_win, tab2_scales), (v_scale_win, tab_scales)):
-            for q in range(QUADS):
-                nc.gpsimd.dma_start(
-                    win[32 * q : 32 * q + PLANE_ROWS * K_PASSES, :],
-                    src[:, PLANE_ROWS * q : PLANE_ROWS * (q + 1), :].bitcast(I32),
-                )
-        make_identity(nc, identity[:], nomemset=True)
+        make_identity(nc, identity[:])
+        identity_bf16 = keep.tile([P, P], BF16, name="identity_bf16", align_bytes=64)
+        nc.scalar.copy(identity_bf16[:], identity[:])
 
         def load_words(src, a, name):
             win = keep.tile([P, T], I32, name=f"{name}{a}", align_bytes=64)
             nc.sync.dma_start(win[:], src[a].rearrange("p n i -> p (n i)").bitcast(I32))
             return win
+
+        def load_scale_rows(win, src):
+            for q in range(QUADS):
+                nc.sync.dma_start(
+                    win[32 * q : 32 * q + PLANE_ROWS * K_PASSES, :],
+                    src[:, PLANE_ROWS * q : PLANE_ROWS * (q + 1), :].bitcast(I32),
+                )
 
         def load_xc(a):
             raw = ring.tile([P, PACK, M], F32, name="xc_raw", tag="raw", align_bytes=64, bufs=RAW_BUFS)
@@ -93,6 +97,12 @@ def tile_list_sparse_edge_maxout_kernel(
             nc.sync.dma_start(raw[:], rows[:, :, half * (T // 2) : (half + 1) * (T // 2)])
             return raw
 
+        def load_single(s):
+            win = keep.tile([P, T], F32, name=f"single_win{s}", align_bytes=64)
+            i = 2 * N_PAIRS + s
+            nc.sync.dma_start(win[:], wdT[i * P : (i + 1) * P, :])
+            return win
+
         def load_xn_scales():
             for q in range(QUADS):
                 nc.sync.dma_start(
@@ -100,13 +110,12 @@ def tile_list_sparse_edge_maxout_kernel(
                     xn_scales[:, PLANE_ROWS * q : PLANE_ROWS * (q + 1), :].rearrange("a r m -> r a m").bitcast(I32),
                 )
 
+        g_listed = keep.tile([J_PASSES, PACK * P], F32, name="g_listed", align_bytes=64)
+
         def load_vectors():
-            nc.sync.dma_start(
-                vec_rows[0:PACK, :].rearrange("t (c r) -> t c r", r=RUN),
-                g.rearrange("(c t r) -> t c r", t=PACK, r=RUN),
-            )
-            nc.sync.dma_start(vec_rows[BIAS_ROW:EW_ROW, 0:P], b.rearrange("(i p) -> i p", p=P))
-            nc.sync.dma_start(vec_rows[EW_ROW : EW_ROW + M // P, 0:P], ew.rearrange("(c p) -> c p", p=P))
+            nc.sync.dma_start(g_listed[:], g.rearrange("(b j) -> b j", b=J_PASSES))
+            nc.sync.dma_start(vec_rows[BIAS_ROW:EW_ROW, 0 : BIAS_TILES * P], b.rearrange("(u n) -> u n", u=2))
+            nc.sync.dma_start(vec_rows[EW_ROW : EW_ROW + 1, :], ew.rearrange("(u m) -> u m", u=1))
 
         def pick_words(win, name):
             picked = keep.tile([P, S], U32, name=name, align_bytes=64)
@@ -125,38 +134,38 @@ def tile_list_sparse_edge_maxout_kernel(
 
         v2_win, v_win, xc_raw, wd_raw = {}, {}, {}, {}
         v2_win[0] = load_words(tab2_words, 0, "v2_win")
+        wd_raw[0, 0] = load_wd(0, 0)
+        load_scale_rows(v2_scale_win, tab2_scales)
         v2_win[1] = load_words(tab2_words, 1, "v2_win")
         load_xn_scales()
         v2_win[2] = load_words(tab2_words, 2, "v2_win")
-        load_vectors()
-        wd_raw[0, 0] = load_wd(0, 0)
-        xc_raw[0] = load_xc(0)
         wd_raw[0, 1] = load_wd(0, 1)
+        load_scale_rows(v_scale_win, tab_scales)
+        xc_raw[0] = load_xc(0)
+        load_vectors()
+        xn_codes = keep.tile([P, K_PASSES, 2 * M], U8, name="xn_codes", align_bytes=64)
+        nc.sync.dma_start(xn_codes[:].bitcast(I32), xn_words.rearrange("a p c -> p a c").bitcast(I32))
+        v_win[0] = load_words(tab_words, 0, "v_win")
 
-        v2_codes = [pick_words(v2_win[a], f"v2_codes{a}") for a in range(K_PASSES - 1)]
+        v2_codes = [pick_words(v2_win[a], f"v2_codes{a}") for a in range(K_PASSES)]
         v2_planes = pick_scales(v2_scale_win, "v2_planes")
         for a in range(1, K_PASSES):
             nc.sync.dma_start(
                 v2_moved[0:SHIFT_ROWS, a - 1, :], v2_planes[PLANE_ROWS * a : PLANE_ROWS * a + SHIFT_ROWS, :].bitcast(I32)
             )
 
-        xn_codes = keep.tile([P, K_PASSES, 2 * M], U8, name="xn_codes", align_bytes=64)
-        nc.sync.dma_start(xn_codes[:].bitcast(I32), xn_words.rearrange("a p c -> p a c").bitcast(I32))
-        v_win[0] = load_words(tab_words, 0, "v_win")
-        v_win[1] = load_words(tab_words, 1, "v_win")
-        xc_raw[1] = load_xc(1)
-        v_win[2] = load_words(tab_words, 2, "v_win")
-        xc_raw[2] = load_xc(2)
-        for pair in range(1, N_PAIRS):
-            for half in range(2):
-                wd_raw[pair, half] = load_wd(pair, half)
+        for a in range(1, K_PASSES):
+            v_win[a] = load_words(tab_words, a, "v_win")
+            xc_raw[a] = load_xc(a)
+        for half in range(2):
+            wd_raw[1, half] = load_wd(1, half)
+        single_win = [load_single(s) for s in range(N_SINGLES)]
 
-        v2_codes.append(pick_words(v2_win[K_PASSES - 1], f"v2_codes{K_PASSES - 1}"))
         v_planes = pick_scales(v_scale_win, "v_planes")
         v_codes = [pick_words(v_win[a], f"v_codes{a}") for a in range(K_PASSES)]
 
         def interleave(copy, planes):
-            grouped = ring.tile([P, M, PACK], BF16, name="grouped", align_bytes=64)
+            grouped = ring.tile([P, M, PACK], BF16, name="grouped", align_bytes=64, bufs=GROUPED_BUFS)
             copy(grouped[:].rearrange("p (c i) t -> p c t i", i=4), planes.rearrange("p t (c i) -> p c t i", i=4))
             return grouped[:].rearrange("p m t -> p (m t)")
 
@@ -167,38 +176,11 @@ def tile_list_sparse_edge_maxout_kernel(
             grouped = interleave(copy, xc_raw[a][:])
             nc.vector.quantize_mx(out=xc_codes[:, a, :].bitcast(FP8X4), scales=xc_planes[:, a, :], in_=grouped)
 
-        wd_win = [keep.tile([P, T, 2], BF16, name=f"wd_win{pair}", align_bytes=64) for pair in range(N_PAIRS)]
-
-        def round_wd(pair, half, copy):
-            copy(
-                wd_win[pair][:, half * (T // 2) : (half + 1) * (T // 2), :],
-                wd_raw[pair, half][:].rearrange("p e t -> p t e"),
-            )
-
-        on_scalar, on_vector = nc.scalar.copy, nc.vector.tensor_copy
-        round_wd(0, 0, on_scalar)
-        round_wd(0, 1, on_scalar)
-        quantise_xc(0, on_scalar)
-        quantise_xc(1, on_vector)
-        quantise_xc(2, on_scalar)
-        round_wd(1, 0, on_scalar)
-        round_wd(1, 1, on_scalar)
-        round_wd(2, 0, on_scalar)
-
-        vec_cols = keep.tile([P, J_PASSES, VEC_ROWS], F32, name="vec_cols", align_bytes=64)
-        turned = psum.tile([P, J_PASSES, P], F32, name="turned", tag="turn", bufs=TURN_BANKS)
-        for jb in range(J_PASSES):
-            nc.tensor.transpose(turned[:, jb, :], vec_rows[:, jb * P : (jb + 1) * P], identity[:])
-        nc.scalar.copy(vec_cols[:], turned[:, :, 0:VEC_ROWS])
-        spread = psum.tile([P, M // P, P], F32, name="spread", tag="turn", bufs=TURN_BANKS)
-        for c in range(M // P):
-            column = vec_cols[:, 0, EW_ROW + c : EW_ROW + c + 1]
-            nc.tensor.transpose(spread[:, c, :], column.to_broadcast([P, P]), identity[:])
-        ew_all = keep.tile([P, M], F32, name="ew_all", align_bytes=64)
-        nc.scalar.copy(ew_all[:], spread[:].rearrange("p c m -> p (c m)"))
+        quantise_xc(0, nc.scalar.copy)
+        quantise_xc(1, nc.vector.tensor_copy)
+        quantise_xc(2, nc.scalar.copy)
 
         resp = keep.tile([P, J_PASSES, PACK, M], F32, name="resp", align_bytes=64)
-        h_rows = keep.tile([P, J_PASSES, PACK, M], BF16, name="h_rows", align_bytes=64)
 
         def neighbour_product(jb, t):
             acc = psum.tile([P, M], F32, name="acc", tag="sum", bufs=SUM_BANKS)
@@ -216,6 +198,36 @@ def tile_list_sparse_edge_maxout_kernel(
                 )
             nc.scalar.copy(resp[:, jb, t, :], acc[:])
 
+        slots = [(jb, t) for jb in range(J_PASSES) for t in range(PACK)]
+        for jb, t in slots[:SUM_BANKS]:
+            neighbour_product(jb, t)
+
+        pair_win = [keep.tile([P, T, 2], BF16, name=f"pair_win{pair}", align_bytes=64) for pair in range(N_PAIRS)]
+        for pair in range(N_PAIRS):
+            for half in range(2):
+                nc.scalar.copy(
+                    pair_win[pair][:, half * (T // 2) : (half + 1) * (T // 2), :],
+                    wd_raw[pair, half][:].rearrange("p e t -> p t e"),
+                )
+
+        nc.scalar.copy(
+            vec_rows[0:J_PASSES, :].rearrange("b (t q r) -> b t q r", t=PACK, r=RUN),
+            g_listed[:].rearrange("b (q t r) -> b t q r", t=PACK, r=RUN),
+        )
+        vec_cols = keep.tile([P, PACK, VEC_ROWS], F32, name="vec_cols", align_bytes=64)
+        turned = psum.tile([P, PACK, P], F32, name="turned", tag="turn", bufs=TURN_BANKS)
+        for u in range(PACK):
+            nc.tensor.transpose(turned[:, u, :], vec_rows[:, u * P : (u + 1) * P], identity[:])
+        nc.scalar.copy(vec_cols[:], turned[:, :, 0:VEC_ROWS])
+        spread = psum.tile([P, M // P, P], F32, name="spread", tag="turn", bufs=TURN_BANKS)
+        for c in range(M // P):
+            column = vec_cols[:, c, EW_ROW : EW_ROW + 1]
+            nc.tensor.transpose(spread[:, c, :], column.to_broadcast([P, P]), identity[:])
+        ew_all = keep.tile([P, M], F32, name="ew_all", align_bytes=64)
+        nc.scalar.copy(ew_all[:], spread[:].rearrange("p c m -> p (c m)"))
+
+        h_rows = keep.tile([P, J_PASSES, PACK, M], BF16, name="h_rows", align_bytes=64)
+
         def centre_product(jb, t):
             acc = psum.tile([P, M], F32, name="acc", tag="sum", bufs=SUM_BANKS)
             cols = slot_cols(jb, t)
@@ -230,79 +242,97 @@ def tile_list_sparse_edge_maxout_kernel(
                     stop=(a == K_PASSES - 1),
                 )
             nc.vector.tensor_tensor(resp[:, jb, t, :], acc[:], resp[:, jb, t, :], ALU.max)
-            gain = vec_cols[:, jb, t : t + 1]
+            gain = vec_cols[:, t, jb : jb + 1]
             nc.gpsimd.tensor_scalar(h_rows[:, jb, t, :], resp[:, jb, t, :], gain, 0.0, ALU.mult, ALU.add)
 
         h_codes = keep.tile([P, J_PASSES, M], U32, name="h_codes", align_bytes=64)
         h_planes = keep.tile([P, J_PASSES, M], U8, name="h_planes", align_bytes=64)
 
-        def quantise_h(jb, copy):
-            grouped = interleave(copy, h_rows[:, jb, :, :])
+        def quantise_h(jb):
+            grouped = interleave(nc.scalar.copy, h_rows[:, jb, :, :])
             nc.vector.quantize_mx(out=h_codes[:, jb, :].bitcast(FP8X4), scales=h_planes[:, jb, :], in_=grouped)
 
-        wd_codes = keep.tile([P, N_PAIRS, J_PASSES, 2 * P], U32, name="wd_codes", align_bytes=64)
-        wd_planes = keep.tile([P, N_PAIRS, J_PASSES, 2 * P], U8, name="wd_planes", align_bytes=64)
+        wd_codes, wd_planes = {}, {}
 
-        def pick_wd(pair, pieces):
-            picked = ring.tile([P, S], U32, name="wd_picked", align_bytes=64)
-            window = wd_win[pair][:].rearrange("p t e -> p (t e)").bitcast(U32)
-            blocks = S // (PACK * RUN) // pieces
-            for piece in range(pieces):
-                nc.vector.tensor_copy(
-                    in_slot_order(picked[:])[:, piece * blocks : (piece + 1) * blocks, :, :],
-                    window.indirect(offsets[:, 2 * piece * blocks : 2 * (piece + 1) * blocks]),
-                )
-            grouped = ring.tile([P, J_PASSES, 2 * P, PACK], BF16, name="wd_grouped", align_bytes=64)
+        def turn_wd(picked, dtype, ident, width):
+            grouped = ring.tile([P, J_PASSES, width, PACK], BF16, name="wd_grouped", align_bytes=64)
             for jb in range(J_PASSES):
-                bank = psum.tile([P, PACK, P], F32, name="bank", tag="turn", bufs=TURN_BANKS)
+                bank = psum.tile([P, PACK, P], dtype, name="bank", tag="turn", bufs=TURN_BANKS)
                 for t in range(PACK):
-                    nc.tensor.transpose(bank[:, t, :], picked[:, slot_cols(jb, t)].bitcast(F32), identity[:])
+                    nc.tensor.transpose(bank[:, t, :], picked[:, slot_cols(jb, t)], ident)
                 nc.scalar.copy(grouped[:, jb, :, :], bank[:].bitcast(BF16).rearrange("p t n -> p n t"))
             return grouped
 
-        def quantise_wd(pair, grouped, pieces):
-            step = J_PASSES // pieces
-            for jb in range(0, J_PASSES, step):
-                nc.vector.quantize_mx(
-                    out=wd_codes[:, pair, jb : jb + step, :].rearrange("p b n -> p (b n)").bitcast(FP8X4),
-                    scales=wd_planes[:, pair, jb : jb + step, :].rearrange("p b n -> p (b n)"),
-                    in_=grouped[:, jb : jb + step, :, :].rearrange("p b n t -> p (b n t)"),
+        def pick_pair(pair):
+            picked = ring.tile([P, S], U32, name="wd_picked", align_bytes=64)
+            window = pair_win[pair][:].rearrange("p t e -> p (t e)").bitcast(U32)
+            nc.vector.tensor_copy(in_slot_order(picked[:]), window.indirect(offsets[:]))
+            return turn_wd(picked[:].bitcast(F32), F32, identity[:], 2 * P)
+
+        def quantise_pair(pair, grouped):
+            codes = keep.tile([P, J_PASSES, 2 * P], U32, name=f"pair_codes{pair}", align_bytes=64)
+            planes = keep.tile([P, J_PASSES, 2 * P], U8, name=f"pair_planes{pair}", align_bytes=64)
+            nc.vector.quantize_mx(
+                out=codes[:].rearrange("p b n -> p (b n)").bitcast(FP8X4),
+                scales=planes[:].rearrange("p b n -> p (b n)"),
+                in_=grouped[:].rearrange("p b n t -> p (b n t)"),
+            )
+            for e in range(2):
+                wd_codes[2 * pair + e] = codes[:, :, e * P : (e + 1) * P]
+                wd_planes[2 * pair + e] = planes[:, :, e * P : (e + 1) * P]
+
+        def pick_single(s):
+            picked = ring.tile([P, S], BF16, name="wd_picked", align_bytes=64)
+            blocks = S // (PACK * RUN) // J_PASSES
+            for jb in range(J_PASSES):
+                nc.vector.tensor_copy(
+                    in_slot_order(picked[:])[:, jb * blocks : (jb + 1) * blocks, :, :],
+                    single_win[s][:].indirect(offsets[:, 2 * jb * blocks : 2 * (jb + 1) * blocks]),
                 )
+            return turn_wd(picked[:], BF16, identity_bf16[:], P)
+
+        def quantise_single(s, grouped):
+            codes = keep.tile([P, J_PASSES, P], U32, name=f"single_codes{s}", align_bytes=64)
+            planes = keep.tile([P, J_PASSES, P], U8, name=f"single_planes{s}", align_bytes=64)
+            for jb in range(J_PASSES):
+                nc.vector.quantize_mx(
+                    out=codes[:, jb, :].bitcast(FP8X4),
+                    scales=planes[:, jb, :],
+                    in_=grouped[:, jb, :, :].rearrange("p n t -> p (n t)"),
+                )
+            wd_codes[2 * N_PAIRS + s] = codes[:]
+            wd_planes[2 * N_PAIRS + s] = planes[:]
 
         def project(i):
             acc = psum.tile([P, M], F32, name="acc", tag="sum", bufs=SUM_BANKS)
-            cols = slice(i % 2 * P, (i % 2 + 1) * P)
             for jb in range(J_PASSES):
                 nc.tensor.matmul_mx(
                     out=acc[:],
-                    lhsT=wd_codes[:, i // 2, jb, cols].bitcast(FP8X4),
-                    lhsT_scale=wd_planes[:, i // 2, jb, cols],
+                    lhsT=wd_codes[i][:, jb, :].bitcast(FP8X4),
+                    lhsT_scale=wd_planes[i][:, jb, :],
                     rhs=h_codes[:, jb, :].bitcast(FP8X4),
                     rhs_scale=h_planes[:, jb, :],
                     start=(jb == 0),
                     stop=(jb == J_PASSES - 1),
                 )
             result = ring.tile([P, M], F32, name="result", align_bytes=64, bufs=RESULT_BUFS)
-            bias = vec_cols[:, 0, BIAS_ROW + i : BIAS_ROW + i + 1]
+            bias_row = BIAS_ROW + i // BIAS_TILES
+            bias = vec_cols[:, i % BIAS_TILES, bias_row : bias_row + 1]
             nc.vector.scalar_tensor_tensor(result[:], acc[:], bias, ew_all[:], ALU.add, ALU.mult)
             nc.sync.dma_start(out[i * P : (i + 1) * P, :], result[:])
 
-        for t in range(PACK):
-            neighbour_product(0, t)
-        quantise_wd(0, pick_wd(0, 1), 1)
-        for t in range(PACK):
-            neighbour_product(1, t)
+        quantise_pair(0, pick_pair(0))
+        for jb, t in slots[SUM_BANKS:]:
+            neighbour_product(jb, t)
         for jb in range(J_PASSES):
             for t in range(PACK):
                 centre_product(jb, t)
-        quantise_h(0, on_scalar)
-        grouped_1 = pick_wd(1, 1)
-        quantise_h(1, on_vector)
-        round_wd(2, 1, on_vector)
-        grouped_2 = pick_wd(2, J_PASSES)
+            quantise_h(jb)
+        quantise_pair(1, pick_pair(1))
         project(0)
         project(1)
-        quantise_wd(1, grouped_1, 1)
-        quantise_wd(2, grouped_2, J_PASSES)
+        singles_grouped = [pick_single(s) for s in range(N_SINGLES)]
+        for s in range(N_SINGLES):
+            quantise_single(s, singles_grouped[s])
         for i in range(2, N_TILES):
             project(i)

@@ -32,10 +32,11 @@ BIAS_TILES = N_TILES // 2
 EW_ROW = BIAS_ROW + 2
 VEC_ROWS = 8
 RAW_BUFS = 4
+WINDOW_BUFS = 2 * K_PASSES
 SUM_BANKS = 6
 TURN_BANKS = 2
 GROUPED_BUFS = 3
-RESULT_BUFS = 4
+RESULT_BUFS = N_TILES
 
 
 def in_slot_order(ap):
@@ -75,7 +76,7 @@ def tile_list_sparse_edge_maxout_kernel(
         nc.scalar.copy(identity_bf16[:], identity[:])
 
         def load_words(src, a, name):
-            win = keep.tile([P, T], I32, name=f"{name}{a}", align_bytes=64)
+            win = ring.tile([P, T], I32, name=f"{name}{a}", tag="window", align_bytes=64, bufs=WINDOW_BUFS)
             nc.sync.dma_start(win[:], src[a].rearrange("p n i -> p (n i)").bitcast(I32))
             return win
 
@@ -98,7 +99,7 @@ def tile_list_sparse_edge_maxout_kernel(
             return raw
 
         def load_single(s):
-            win = keep.tile([P, T], F32, name=f"single_win{s}", align_bytes=64)
+            win = ring.tile([P, T], F32, name=f"single_win{s}", tag="window", align_bytes=64, bufs=WINDOW_BUFS)
             i = 2 * N_PAIRS + s
             nc.sync.dma_start(win[:], wdT[i * P : (i + 1) * P, :])
             return win

@@ -32,7 +32,6 @@ BIAS_TILES = N_TILES // 2
 EW_ROW = BIAS_ROW + 2
 VEC_ROWS = 8
 RAW_BUFS = 4
-WINDOW_BUFS = 2 * K_PASSES
 SUM_BANKS = 6
 TURN_BANKS = 2
 GROUPED_BUFS = 3
@@ -56,6 +55,14 @@ def tile_list_sparse_edge_maxout_kernel(
         keep = ctx.enter_context(tc.tile_pool(name="keep", bufs=1))
         ring = ctx.enter_context(tc.tile_pool(name="ring", bufs=2))
         psum = ctx.enter_context(tc.psum_pool(name="psum", bufs=1))
+        shared = ctx.enter_context(tc.tile_pool(name="shared", bufs=1))
+
+        def placed(shape, dtype, name, kib):
+            return shared.tile(shape, dtype, name=name, align_bytes=64, offset=kib * 1024)
+
+        at_window = {"v2_win": 0, "v_win": 8 * K_PASSES}
+        at_larger = at_window["v_win"]
+        at_resp = 16 * K_PASSES
 
         offsets = keep.tile([P, S // 16], U16, name="offsets")
         nc.sync.dma_start(offsets[:], offs)
@@ -76,7 +83,7 @@ def tile_list_sparse_edge_maxout_kernel(
         nc.scalar.copy(identity_bf16[:], identity[:])
 
         def load_words(src, a, name):
-            win = ring.tile([P, T], I32, name=f"{name}{a}", tag="window", align_bytes=64, bufs=WINDOW_BUFS)
+            win = placed([P, T], I32, f"{name}{a}", at_window[name] + 8 * a)
             nc.sync.dma_start(win[:], src[a].rearrange("p n i -> p (n i)").bitcast(I32))
             return win
 
@@ -99,7 +106,7 @@ def tile_list_sparse_edge_maxout_kernel(
             return raw
 
         def load_single(s):
-            win = ring.tile([P, T], F32, name=f"single_win{s}", tag="window", align_bytes=64, bufs=WINDOW_BUFS)
+            win = placed([P, T], F32, f"single_win{s}", at_window["v2_win"] + 8 * s)
             i = 2 * N_PAIRS + s
             nc.sync.dma_start(win[:], wdT[i * P : (i + 1) * P, :])
             return win
@@ -142,11 +149,8 @@ def tile_list_sparse_edge_maxout_kernel(
         v2_win[2] = load_words(tab2_words, 2, "v2_win")
         wd_raw[0, 1] = load_wd(0, 1)
         load_scale_rows(v_scale_win, tab_scales)
-        xc_raw[0] = load_xc(0)
-        load_vectors()
         xn_codes = keep.tile([P, K_PASSES, 2 * M], U8, name="xn_codes", align_bytes=64)
         nc.sync.dma_start(xn_codes[:].bitcast(I32), xn_words.rearrange("a p c -> p a c").bitcast(I32))
-        v_win[0] = load_words(tab_words, 0, "v_win")
 
         v2_codes = [pick_words(v2_win[a], f"v2_codes{a}") for a in range(K_PASSES)]
         v2_planes = pick_scales(v2_scale_win, "v2_planes")
@@ -154,6 +158,10 @@ def tile_list_sparse_edge_maxout_kernel(
             nc.sync.dma_start(
                 v2_moved[0:SHIFT_ROWS, a - 1, :], v2_planes[PLANE_ROWS * a : PLANE_ROWS * a + SHIFT_ROWS, :].bitcast(I32)
             )
+
+        xc_raw[0] = load_xc(0)
+        load_vectors()
+        v_win[0] = load_words(tab_words, 0, "v_win")
 
         for a in range(1, K_PASSES):
             v_win[a] = load_words(tab_words, a, "v_win")
@@ -177,11 +185,31 @@ def tile_list_sparse_edge_maxout_kernel(
             grouped = interleave(copy, xc_raw[a][:])
             nc.vector.quantize_mx(out=xc_codes[:, a, :].bitcast(FP8X4), scales=xc_planes[:, a, :], in_=grouped)
 
-        quantise_xc(0, nc.scalar.copy)
-        quantise_xc(1, nc.vector.tensor_copy)
-        quantise_xc(2, nc.scalar.copy)
+        def round_on_gpsimd(a):
+            grouped = ring.tile([P, M, PACK], BF16, name="grouped", align_bytes=64, bufs=GROUPED_BUFS)
+            nc.gpsimd.tensor_scalar(grouped[:], xc_raw[a][:].rearrange("p t m -> p m t"), 1.0, 0.0, ALU.mult, ALU.add)
+            nc.vector.quantize_mx(
+                out=xc_codes[:, a, :].bitcast(FP8X4),
+                scales=xc_planes[:, a, :],
+                in_=grouped[:].rearrange("p m t -> p (m t)"),
+            )
 
-        resp = keep.tile([P, J_PASSES, PACK, M], F32, name="resp", align_bytes=64)
+        round_on_gpsimd(0)
+        round_on_gpsimd(1)
+        grouped = ring.tile([P, M, PACK], BF16, name="grouped", align_bytes=64, bufs=GROUPED_BUFS)
+        cut = 288
+        nc.scalar.copy(
+            grouped[:, 0:cut, :].rearrange("p (c i) t -> p c t i", i=4),
+            xc_raw[2][:, :, 0:cut].rearrange("p t (c i) -> p c t i", i=4),
+        )
+        nc.gpsimd.tensor_scalar(
+            grouped[:, cut:M, :], xc_raw[2][:, :, cut:M].rearrange("p t m -> p m t"), 1.0, 0.0, ALU.mult, ALU.add
+        )
+        nc.vector.quantize_mx(
+            out=xc_codes[:, 2, :].bitcast(FP8X4), scales=xc_planes[:, 2, :], in_=grouped[:].rearrange("p m t -> p (m t)")
+        )
+
+        resp = {}
 
         def neighbour_product(jb, t):
             acc = psum.tile([P, M], F32, name="acc", tag="sum", bufs=SUM_BANKS)
@@ -197,7 +225,8 @@ def tile_list_sparse_edge_maxout_kernel(
                     start=(a == 0),
                     stop=(a == K_PASSES - 1),
                 )
-            nc.scalar.copy(resp[:, jb, t, :], acc[:])
+            resp[jb, t] = placed([P, M], F32, f"resp{jb}{t}", at_resp + 2 * (PACK * jb + t))
+            nc.scalar.copy(resp[jb, t][:], acc[:])
 
         slots = [(jb, t) for jb in range(J_PASSES) for t in range(PACK)]
         for jb, t in slots[:SUM_BANKS]:
@@ -229,10 +258,14 @@ def tile_list_sparse_edge_maxout_kernel(
 
         h_rows = keep.tile([P, J_PASSES, PACK, M], BF16, name="h_rows", align_bytes=64)
 
-        def centre_product(jb, t):
-            acc = psum.tile([P, M], F32, name="acc", tag="sum", bufs=SUM_BANKS)
+        centre_acc = {}
+
+        def centre_passes(jb, t, passes):
+            if (jb, t) not in centre_acc:
+                centre_acc[jb, t] = psum.tile([P, M], F32, name="acc", tag="sum", bufs=SUM_BANKS)
+            acc = centre_acc[jb, t]
             cols = slot_cols(jb, t)
-            for a in range(K_PASSES):
+            for a in passes:
                 nc.tensor.matmul_mx(
                     out=acc[:],
                     lhsT=v_codes[a][:, cols].bitcast(FP8X4),
@@ -242,9 +275,16 @@ def tile_list_sparse_edge_maxout_kernel(
                     start=(a == 0),
                     stop=(a == K_PASSES - 1),
                 )
-            nc.vector.tensor_tensor(resp[:, jb, t, :], acc[:], resp[:, jb, t, :], ALU.max)
+
+        def larger_times_gain(jb, t):
+            acc = centre_acc[jb, t]
+            larger = placed([P, M], F32, f"larger{jb}{t}", at_larger + 2 * (PACK * jb + t))
+            nc.vector.tensor_tensor(larger[:], acc[:], resp[jb, t][:], ALU.max)
             gain = vec_cols[:, t, jb : jb + 1]
-            nc.gpsimd.tensor_scalar(h_rows[:, jb, t, :], resp[:, jb, t, :], gain, 0.0, ALU.mult, ALU.add)
+            if t == PACK - 1:
+                nc.scalar.activation(h_rows[:, jb, t, :], larger[:], mybir.ActivationFunctionType.Copy, scale=gain)
+            else:
+                nc.gpsimd.tensor_scalar(h_rows[:, jb, t, :], larger[:], gain, 0.0, ALU.mult, ALU.add)
 
         h_codes = keep.tile([P, J_PASSES, M], U32, name="h_codes", align_bytes=64)
         h_planes = keep.tile([P, J_PASSES, M], U8, name="h_planes", align_bytes=64)
@@ -265,13 +305,19 @@ def tile_list_sparse_edge_maxout_kernel(
             return grouped
 
         def pick_pair(pair):
-            picked = ring.tile([P, S], U32, name="wd_picked", align_bytes=64)
+            if pair == 0:
+                picked = ring.tile([P, S], U32, name="wd_picked", align_bytes=64)
+            else:
+                picked = placed([P, S], U32, "late_picked", at_resp + 12)
             window = pair_win[pair][:].rearrange("p t e -> p (t e)").bitcast(U32)
             nc.vector.tensor_copy(in_slot_order(picked[:]), window.indirect(offsets[:]))
             return turn_wd(picked[:].bitcast(F32), F32, identity[:], 2 * P)
 
         def quantise_pair(pair, grouped):
-            codes = keep.tile([P, J_PASSES, 2 * P], U32, name=f"pair_codes{pair}", align_bytes=64)
+            if pair == 0:
+                codes = placed([P, J_PASSES, 2 * P], U32, "early_codes", at_window["v_win"] + 8 * (K_PASSES - 1))
+            else:
+                codes = keep.tile([P, J_PASSES, 2 * P], U32, name=f"pair_codes{pair}", align_bytes=64)
             planes = keep.tile([P, J_PASSES, 2 * P], U8, name=f"pair_planes{pair}", align_bytes=64)
             nc.vector.quantize_mx(
                 out=codes[:].rearrange("p b n -> p (b n)").bitcast(FP8X4),
@@ -325,9 +371,13 @@ def tile_list_sparse_edge_maxout_kernel(
         quantise_pair(0, pick_pair(0))
         for jb, t in slots[SUM_BANKS:]:
             neighbour_product(jb, t)
+        for a in range(K_PASSES - 1):
+            for jb, t in slots[:SUM_BANKS]:
+                centre_passes(jb, t, [a])
         for jb in range(J_PASSES):
             for t in range(PACK):
-                centre_product(jb, t)
+                centre_passes(jb, t, [K_PASSES - 1] if (jb, t) in centre_acc else range(K_PASSES))
+                larger_times_gain(jb, t)
             quantise_h(jb)
         quantise_pair(1, pick_pair(1))
         project(0)

@@ -15,6 +15,7 @@ U8 = mybir.dt.uint8
 FP8X4 = mybir.dt.float8_e4m3fn_x4
 FP4X4 = mybir.dt.float4_e2m1fn_x4
 ALU = mybir.AluOpType
+COPY = mybir.ActivationFunctionType.Copy
 
 P = 128
 PACK = 4
@@ -23,19 +24,18 @@ K_PASSES = K // (P * PACK)
 J_PASSES = S // (P * PACK)
 N_TILES = N // P
 N_PAIRS = 2
-N_SINGLES = N_TILES - 2 * N_PAIRS
 QUADS = 4
 PLANE_ROWS = 4
 SHIFT_ROWS = 112
 BIAS_ROW = J_PASSES
-BIAS_TILES = N_TILES // 2
-EW_ROW = BIAS_ROW + 2
-VEC_ROWS = 8
-RAW_BUFS = 4
-SUM_BANKS = 6
-TURN_BANKS = 2
-GROUPED_BUFS = 3
-RESULT_BUFS = N_TILES
+EW_ROW = BIAS_ROW + N_TILES
+VEC_ROWS = EW_ROW + M // P
+BLOCKS = P // RUN
+LIST_COLS = S // 16 // J_PASSES
+BANK = 2048
+SCALAR_GAINS = 6
+H_SPLIT_COLS = 288
+SPLIT_COLS = 512
 
 
 def in_slot_order(ap):
@@ -53,37 +53,56 @@ def tile_list_sparse_edge_maxout_kernel(
     nc = tc.nc
     with ExitStack() as ctx:
         keep = ctx.enter_context(tc.tile_pool(name="keep", bufs=1))
-        ring = ctx.enter_context(tc.tile_pool(name="ring", bufs=2))
         psum = ctx.enter_context(tc.psum_pool(name="psum", bufs=1))
         shared = ctx.enter_context(tc.tile_pool(name="shared", bufs=1))
+
+        def kept(shape, dtype, name):
+            return keep.tile(shape, dtype, name=name, align_bytes=64)
 
         def placed(shape, dtype, name, kib):
             return shared.tile(shape, dtype, name=name, align_bytes=64, offset=kib * 1024)
 
-        at_window = {"v2_win": 0, "v_win": 8 * K_PASSES}
-        at_larger = at_window["v_win"]
-        at_resp = 16 * K_PASSES
+        def in_bank(shape, dtype, name, bank):
+            return psum.tile(shape, dtype, name=name, offset=bank * BANK)
+
+        at_v2_win = [0, 8, 24]
+        at_v_win = [32, 48, 64]
+        at_xc_raw = [16, 40, 56]
+        at_wd_raw = {(0, 0): 0, (0, 1): 8, (1, 0): 24, (1, 1): 32}
+        at_single_win = [16, 40]
+        at_xc_codes_last = 48
+        at_resp = 80
+        at_v2_codes = 96
+        at_larger = [96, 98, 100, 102, 72, 74, 76, 78]
+        at_h_rows = 108
+        at_pair_win = [56, 102]
+        at_h_grouped_first = 8
+        at_result = [40, 42, 64, 66, 44, 68]
+        at_xc_grouped = [116, 120, 124]
 
         offsets = keep.tile([P, S // 16], U16, name="offsets")
         nc.sync.dma_start(offsets[:], offs)
 
-        v2_scale_win = keep.tile([P, T // 4], I32, name="v2_scale_win", align_bytes=64)
-        v_scale_win = keep.tile([P, T // 4], I32, name="v_scale_win", align_bytes=64)
-        xn_planes = keep.tile([P, K_PASSES, M // 4], I32, name="xn_planes", align_bytes=64)
-        vec_rows = keep.tile([P, PACK * P], F32, name="vec_rows", align_bytes=64)
-        v2_moved = keep.tile([P, K_PASSES - 1, S // 4], I32, name="v2_moved", align_bytes=64)
-        identity = keep.tile([P, P], F32, name="identity", align_bytes=64)
-        nc.gpsimd.memset(v2_scale_win[:], 0)
-        nc.vector.memset(v_scale_win[:], 0)
+        v2_scale_win = kept([P, T // 4], I32, "v2_scale_win")
+        v_scale_win = kept([P, T // 4], I32, "v_scale_win")
+        xn_planes = kept([P, K_PASSES, M // 4], I32, "xn_planes")
+        vec_rows = kept([P, PACK * P], F32, "vec_rows")
+        v2_moved = kept([P, K_PASSES - 1, S // 4], I32, "v2_moved")
+        identity = kept([P, P], F32, "identity")
+        nc.vector.memset(v2_scale_win[:], 0)
         nc.vector.memset(vec_rows[:], 0.0)
         nc.vector.memset(xn_planes[:], 0)
+        nc.vector.memset(v_scale_win[:], 0)
         nc.vector.memset(v2_moved[:], 0)
-        make_identity(nc, identity[:])
-        identity_bf16 = keep.tile([P, P], BF16, name="identity_bf16", align_bytes=64)
-        nc.scalar.copy(identity_bf16[:], identity[:])
 
-        def load_words(src, a, name):
-            win = placed([P, T], I32, f"{name}{a}", at_window[name] + 8 * a)
+        g_listed = kept([J_PASSES, PACK * P], F32, "g_listed")
+        nc.gpsimd.dma_start(g_listed[:], g.rearrange("(b j) -> b j", b=J_PASSES))
+        nc.gpsimd.dma_start(vec_rows[BIAS_ROW:EW_ROW, 0:P], b.rearrange("(u n) -> u n", n=P))
+        nc.gpsimd.dma_start(vec_rows[EW_ROW:VEC_ROWS, 0:P], ew.rearrange("(u m) -> u m", m=P))
+        make_identity(nc, identity[:])
+
+        def load_words(src, a, name, kib):
+            win = placed([P, T], I32, f"{name}{a}", kib)
             nc.sync.dma_start(win[:], src[a].rearrange("p n i -> p (n i)").bitcast(I32))
             return win
 
@@ -95,18 +114,18 @@ def tile_list_sparse_edge_maxout_kernel(
                 )
 
         def load_xc(a):
-            raw = ring.tile([P, PACK, M], F32, name="xc_raw", tag="raw", align_bytes=64, bufs=RAW_BUFS)
+            raw = placed([P, PACK, M], F32, f"xc_raw{a}", at_xc_raw[a])
             nc.sync.dma_start(raw[:], xc[a * P * PACK : (a + 1) * P * PACK, :].rearrange("(p i) m -> p i m", i=PACK))
             return raw
 
         def load_wd(pair, half):
             rows = wdT[2 * pair * P : 2 * (pair + 1) * P, :].rearrange("(p e) t -> p e t", e=2)
-            raw = ring.tile([P, 2, T // 2], F32, name="wd_raw", tag="raw", align_bytes=64, bufs=RAW_BUFS)
+            raw = placed([P, 2, T // 2], F32, f"wd_raw{pair}{half}", at_wd_raw[pair, half])
             nc.sync.dma_start(raw[:], rows[:, :, half * (T // 2) : (half + 1) * (T // 2)])
             return raw
 
         def load_single(s):
-            win = placed([P, T], F32, f"single_win{s}", at_window["v2_win"] + 8 * s)
+            win = placed([P, T], F32, f"single_win{s}", at_single_win[s])
             i = 2 * N_PAIRS + s
             nc.sync.dma_start(win[:], wdT[i * P : (i + 1) * P, :])
             return win
@@ -118,106 +137,93 @@ def tile_list_sparse_edge_maxout_kernel(
                     xn_scales[:, PLANE_ROWS * q : PLANE_ROWS * (q + 1), :].rearrange("a r m -> r a m").bitcast(I32),
                 )
 
-        g_listed = keep.tile([J_PASSES, PACK * P], F32, name="g_listed", align_bytes=64)
-
-        def load_vectors():
-            nc.sync.dma_start(g_listed[:], g.rearrange("(b j) -> b j", b=J_PASSES))
-            nc.sync.dma_start(vec_rows[BIAS_ROW:EW_ROW, 0 : BIAS_TILES * P], b.rearrange("(u n) -> u n", u=2))
-            nc.sync.dma_start(vec_rows[EW_ROW : EW_ROW + 1, :], ew.rearrange("(u m) -> u m", u=1))
-
-        def pick_words(win, name):
-            picked = keep.tile([P, S], U32, name=name, align_bytes=64)
-            nc.vector.tensor_copy(in_slot_order(picked[:]), win[:].bitcast(U32).indirect(offsets[:]))
+        def pick_words(win, picked, cols):
+            nc.vector.tensor_copy(in_slot_order(picked[:]), win[:].bitcast(U32).indirect(offsets[:, cols]))
             return picked
 
         def pick_scales(win, name):
-            listed = keep.tile([P, S], U8, name=name + "_listed", align_bytes=64)
+            listed = kept([P, S], U8, name + "_listed")
             nc.vector.tensor_copy(listed[:], win[:].bitcast(U8).indirect(offsets[:]))
-            planes = keep.tile([P, S], U8, name=name, align_bytes=64)
+            planes = kept([P, S], U8, name)
             nc.vector.tensor_copy(
                 planes[:].bitcast(I32).rearrange("p (t c w) -> p t c w", t=PACK, w=RUN // 4),
                 listed[:].bitcast(I32).rearrange("p (c t w) -> p t c w", t=PACK, w=RUN // 4),
             )
             return planes
 
-        v2_win, v_win, xc_raw, wd_raw = {}, {}, {}, {}
-        v2_win[0] = load_words(tab2_words, 0, "v2_win")
-        wd_raw[0, 0] = load_wd(0, 0)
-        load_scale_rows(v2_scale_win, tab2_scales)
-        v2_win[1] = load_words(tab2_words, 1, "v2_win")
-        load_xn_scales()
-        v2_win[2] = load_words(tab2_words, 2, "v2_win")
-        wd_raw[0, 1] = load_wd(0, 1)
-        load_scale_rows(v_scale_win, tab_scales)
-        xn_codes = keep.tile([P, K_PASSES, 2 * M], U8, name="xn_codes", align_bytes=64)
-        nc.sync.dma_start(xn_codes[:].bitcast(I32), xn_words.rearrange("a p c -> p a c").bitcast(I32))
+        whole_list = slice(0, S // 16)
+        half_list = [slice(jb * LIST_COLS, (jb + 1) * LIST_COLS) for jb in range(J_PASSES)]
 
-        v2_codes = [pick_words(v2_win[a], f"v2_codes{a}") for a in range(K_PASSES)]
+        v2_win, v_win, xc_raw, wd_raw, single_win = {}, {}, {}, {}, {}
+        v2_win[0] = load_words(tab2_words, 0, "v2_win", at_v2_win[0])
+        load_scale_rows(v2_scale_win, tab2_scales)
+        v2_win[1] = load_words(tab2_words, 1, "v2_win", at_v2_win[1])
+        load_xn_scales()
+        xn_codes = kept([P, K_PASSES, 2 * M], U8, "xn_codes")
+        nc.sync.dma_start(xn_codes[:].bitcast(I32), xn_words.rearrange("a p c -> p a c").bitcast(I32))
+        v2_win[2] = load_words(tab2_words, 2, "v2_win", at_v2_win[2])
+        xc_raw[0] = load_xc(0)
+
+        def pick_v2(a):
+            return pick_words(v2_win[a], placed([P, S], U32, f"v2_codes{a}", at_v2_codes + 4 * a), whole_list)
+
+        v2_codes = [pick_v2(0)]
         v2_planes = pick_scales(v2_scale_win, "v2_planes")
+        v2_codes.append(pick_v2(1))
         for a in range(1, K_PASSES):
             nc.sync.dma_start(
                 v2_moved[0:SHIFT_ROWS, a - 1, :], v2_planes[PLANE_ROWS * a : PLANE_ROWS * a + SHIFT_ROWS, :].bitcast(I32)
             )
-
-        xc_raw[0] = load_xc(0)
-        load_vectors()
-        v_win[0] = load_words(tab_words, 0, "v_win")
-
+        load_scale_rows(v_scale_win, tab_scales)
+        v_win[0] = load_words(tab_words, 0, "v_win", at_v_win[0])
         for a in range(1, K_PASSES):
-            v_win[a] = load_words(tab_words, a, "v_win")
             xc_raw[a] = load_xc(a)
-        for half in range(2):
-            wd_raw[1, half] = load_wd(1, half)
-        single_win = [load_single(s) for s in range(N_SINGLES)]
+            v_win[a] = load_words(tab_words, a, "v_win", at_v_win[a])
 
-        v_planes = pick_scales(v_scale_win, "v_planes")
-        v_codes = [pick_words(v_win[a], f"v_codes{a}") for a in range(K_PASSES)]
+        nc.scalar.copy(
+            vec_rows[0:J_PASSES, :].rearrange("b (t q r) -> b t q r", t=PACK, r=RUN),
+            g_listed[:].rearrange("b (q t r) -> b t q r", t=PACK, r=RUN),
+        )
+        vec_cols = kept([P, PACK, VEC_ROWS], F32, "vec_cols")
+        turned = in_bank([P, PACK, P], F32, "turned", 6)
+        for u in range(PACK):
+            nc.tensor.transpose(turned[:, u, :], vec_rows[:, u * P : (u + 1) * P], identity[:])
+        nc.scalar.copy(vec_cols[:], turned[:, :, 0:VEC_ROWS])
+        spread = in_bank([P, M // P, P], F32, "spread", 7)
+        for c in range(M // P):
+            column = vec_cols[:, 0, EW_ROW + c : EW_ROW + c + 1]
+            nc.tensor.transpose(spread[:, c, :], column.to_broadcast([P, P]), identity[:])
+        ew_all = kept([P, M], F32, "ew_all")
+        nc.scalar.copy(ew_all[:], spread[:].rearrange("p c m -> p (c m)"))
 
-        def interleave(copy, planes):
-            grouped = ring.tile([P, M, PACK], BF16, name="grouped", align_bytes=64, bufs=GROUPED_BUFS)
-            copy(grouped[:].rearrange("p (c i) t -> p c t i", i=4), planes.rearrange("p t (c i) -> p c t i", i=4))
-            return grouped[:].rearrange("p m t -> p (m t)")
-
-        xc_codes = keep.tile([P, K_PASSES, M], U32, name="xc_codes", align_bytes=64)
-        xc_planes = keep.tile([P, K_PASSES, M], U8, name="xc_planes", align_bytes=64)
-
-        def quantise_xc(a, copy):
-            grouped = interleave(copy, xc_raw[a][:])
-            nc.vector.quantize_mx(out=xc_codes[:, a, :].bitcast(FP8X4), scales=xc_planes[:, a, :], in_=grouped)
-
-        def round_on_gpsimd(a):
-            grouped = ring.tile([P, M, PACK], BF16, name="grouped", align_bytes=64, bufs=GROUPED_BUFS)
-            nc.gpsimd.tensor_scalar(grouped[:], xc_raw[a][:].rearrange("p t m -> p m t"), 1.0, 0.0, ALU.mult, ALU.add)
-            nc.vector.quantize_mx(
-                out=xc_codes[:, a, :].bitcast(FP8X4),
-                scales=xc_planes[:, a, :],
-                in_=grouped[:].rearrange("p m t -> p (m t)"),
+        def interleave(grouped, planes):
+            nc.scalar.copy(
+                grouped.rearrange("p (c i) t -> p c t i", i=4), planes.rearrange("p t (c i) -> p c t i", i=4)
             )
 
-        round_on_gpsimd(0)
-        round_on_gpsimd(1)
-        grouped = ring.tile([P, M, PACK], BF16, name="grouped", align_bytes=64, bufs=GROUPED_BUFS)
-        cut = 288
-        nc.scalar.copy(
-            grouped[:, 0:cut, :].rearrange("p (c i) t -> p c t i", i=4),
-            xc_raw[2][:, :, 0:cut].rearrange("p t (c i) -> p c t i", i=4),
-        )
-        nc.gpsimd.tensor_scalar(
-            grouped[:, cut:M, :], xc_raw[2][:, :, cut:M].rearrange("p t m -> p m t"), 1.0, 0.0, ALU.mult, ALU.add
-        )
-        nc.vector.quantize_mx(
-            out=xc_codes[:, 2, :].bitcast(FP8X4), scales=xc_planes[:, 2, :], in_=grouped[:].rearrange("p m t -> p (m t)")
-        )
+        def interleave_on_gpsimd(grouped, planes):
+            nc.gpsimd.tensor_scalar(grouped, planes.rearrange("p t m -> p m t"), 1.0, 0.0, ALU.mult, ALU.add)
 
-        resp = {}
+        xc_codes = [kept([P, M], U32, f"xc_codes{a}") for a in range(K_PASSES - 1)]
+        xc_codes.append(placed([P, M], U32, "xc_codes_last", at_xc_codes_last))
+        xc_planes = kept([P, K_PASSES, M], U8, "xc_planes")
+        xc_grouped = [placed([P, M, PACK], BF16, f"xc_grouped{a}", at_xc_grouped[a]) for a in range(K_PASSES)]
 
-        def neighbour_product(jb, t):
-            acc = psum.tile([P, M], F32, name="acc", tag="sum", bufs=SUM_BANKS)
-            cols = slot_cols(jb, t)
-            for a in range(K_PASSES):
-                plane = v2_planes[:] if a == 0 else v2_moved[:, a - 1, :].bitcast(U8)
+        def quantise(codes, planes, grouped):
+            nc.vector.quantize_mx(out=codes.bitcast(FP8X4), scales=planes, in_=grouped)
+
+        def quantise_xc(a):
+            quantise(xc_codes[a][:], xc_planes[:, a, :], xc_grouped[a][:].rearrange("p m t -> p (m t)"))
+
+        slots = [(jb, t) for jb in range(J_PASSES) for t in range(PACK)]
+        neighbour_acc = {s: in_bank([P, M], F32, f"neighbour_acc{i}", i) for i, s in enumerate(slots)}
+
+        def neighbour_pass(a):
+            plane = v2_planes[:] if a == 0 else v2_moved[:, a - 1, :].bitcast(U8)
+            for jb, t in slots:
+                cols = slot_cols(jb, t)
                 nc.tensor.matmul_mx(
-                    out=acc[:],
+                    out=neighbour_acc[jb, t][:],
                     lhsT=v2_codes[a][:, cols].bitcast(FP8X4),
                     lhsT_scale=plane[:, cols],
                     rhs=xn_codes[:, a, :].bitcast(FP4X4),
@@ -225,165 +231,199 @@ def tile_list_sparse_edge_maxout_kernel(
                     start=(a == 0),
                     stop=(a == K_PASSES - 1),
                 )
-            resp[jb, t] = placed([P, M], F32, f"resp{jb}{t}", at_resp + 2 * (PACK * jb + t))
-            nc.scalar.copy(resp[jb, t][:], acc[:])
 
-        slots = [(jb, t) for jb in range(J_PASSES) for t in range(PACK)]
-        for jb, t in slots[:SUM_BANKS]:
-            neighbour_product(jb, t)
+        interleave(xc_grouped[0][:], xc_raw[0][:])
+        quantise_xc(0)
+        v2_codes.append(pick_v2(K_PASSES - 1))
+        for a in range(K_PASSES):
+            neighbour_pass(a)
+        resp = {}
+        for i, s in enumerate(slots):
+            resp[s] = placed([P, M], F32, f"resp{i}", at_resp + 2 * i)
+            nc.scalar.copy(resp[s][:], neighbour_acc[s][:])
 
-        pair_win = [keep.tile([P, T, 2], BF16, name=f"pair_win{pair}", align_bytes=64) for pair in range(N_PAIRS)]
-        for pair in range(N_PAIRS):
-            for half in range(2):
-                nc.scalar.copy(
-                    pair_win[pair][:, half * (T // 2) : (half + 1) * (T // 2), :],
-                    wd_raw[pair, half][:].rearrange("p e t -> p t e"),
-                )
+        v_planes = pick_scales(v_scale_win, "v_planes")
+        centre_acc = {s: in_bank([P, M], F32, f"centre_acc{i}", i) for i, s in enumerate(slots)}
 
-        nc.scalar.copy(
-            vec_rows[0:J_PASSES, :].rearrange("b (t q r) -> b t q r", t=PACK, r=RUN),
-            g_listed[:].rearrange("b (q t r) -> b t q r", t=PACK, r=RUN),
-        )
-        vec_cols = keep.tile([P, PACK, VEC_ROWS], F32, name="vec_cols", align_bytes=64)
-        turned = psum.tile([P, PACK, P], F32, name="turned", tag="turn", bufs=TURN_BANKS)
-        for u in range(PACK):
-            nc.tensor.transpose(turned[:, u, :], vec_rows[:, u * P : (u + 1) * P], identity[:])
-        nc.scalar.copy(vec_cols[:], turned[:, :, 0:VEC_ROWS])
-        spread = psum.tile([P, M // P, P], F32, name="spread", tag="turn", bufs=TURN_BANKS)
-        for c in range(M // P):
-            column = vec_cols[:, c, EW_ROW : EW_ROW + 1]
-            nc.tensor.transpose(spread[:, c, :], column.to_broadcast([P, P]), identity[:])
-        ew_all = keep.tile([P, M], F32, name="ew_all", align_bytes=64)
-        nc.scalar.copy(ew_all[:], spread[:].rearrange("p c m -> p (c m)"))
+        def centre_pass(a, jb, t, codes):
+            nc.tensor.matmul_mx(
+                out=centre_acc[jb, t][:],
+                lhsT=codes.bitcast(FP8X4),
+                lhsT_scale=v_planes[PLANE_ROWS * a : P, slot_cols(jb, t)],
+                rhs=xc_codes[a][:].bitcast(FP8X4),
+                rhs_scale=xc_planes[:, a, :],
+                start=(a == 0),
+                stop=(a == K_PASSES - 1),
+            )
 
-        h_rows = keep.tile([P, J_PASSES, PACK, M], BF16, name="h_rows", align_bytes=64)
+        codes = pick_words(v_win[0], kept([P, S], U32, "v_codes0"), whole_list)
+        for jb, t in slots:
+            centre_pass(0, jb, t, codes[:, slot_cols(jb, t)])
+        codes = pick_words(v_win[1], placed([P, S], U32, "v_codes1", at_xc_grouped[0]), whole_list)
+        interleave_on_gpsimd(xc_grouped[1][:], xc_raw[1][:])
+        quantise_xc(1)
+        for jb, t in slots:
+            centre_pass(1, jb, t, codes[:, slot_cols(jb, t)])
+        last = K_PASSES - 1
+        interleave(xc_grouped[last][:], xc_raw[last][:])
+        last_codes = []
+        for jb in range(J_PASSES):
+            codes = placed([P, S // J_PASSES], U32, f"v_codes_last{jb}", at_xc_grouped[1 + jb])
+            last_codes.append(pick_words(v_win[last], codes, half_list[jb]))
+            if jb == 0:
+                quantise_xc(last)
+        for jb, t in slots:
+            centre_pass(last, jb, t, last_codes[jb][:, t * P : (t + 1) * P])
 
-        centre_acc = {}
+        for half in range(2):
+            wd_raw[0, half] = load_wd(0, half)
+        single_win[0] = load_single(0)
+        for half in range(2):
+            wd_raw[1, half] = load_wd(1, half)
+        single_win[1] = load_single(1)
 
-        def centre_passes(jb, t, passes):
-            if (jb, t) not in centre_acc:
-                centre_acc[jb, t] = psum.tile([P, M], F32, name="acc", tag="sum", bufs=SUM_BANKS)
-            acc = centre_acc[jb, t]
-            cols = slot_cols(jb, t)
-            for a in passes:
-                nc.tensor.matmul_mx(
-                    out=acc[:],
-                    lhsT=v_codes[a][:, cols].bitcast(FP8X4),
-                    lhsT_scale=v_planes[PLANE_ROWS * a : P, cols],
-                    rhs=xc_codes[:, a, :].bitcast(FP8X4),
-                    rhs_scale=xc_planes[:, a, :],
-                    start=(a == 0),
-                    stop=(a == K_PASSES - 1),
-                )
+        pair_win = {}
+
+        def round_pair(engine, pair, half, cols):
+            if pair not in pair_win:
+                pair_win[pair] = placed([P, T, 2], BF16, f"pair_win{pair}", at_pair_win[pair])
+            start = half * (T // 2)
+            dst = pair_win[pair][:, start + cols.start : start + cols.stop, :]
+            src = wd_raw[pair, half][:, :, cols].rearrange("p e t -> p t e")
+            if engine is nc.scalar:
+                nc.scalar.copy(dst, src)
+            else:
+                nc.gpsimd.tensor_copy(dst, src)
+
+        h_rows = [placed([P, PACK, M], BF16, f"h_rows{jb}", at_h_rows + 4 * jb) for jb in range(J_PASSES)]
+        h_grouped = [placed([P, M, PACK], BF16, "h_grouped0", at_h_grouped_first), kept([P, M, PACK], BF16, "h_grouped1")]
+        h_codes = kept([P, J_PASSES, M], U32, "h_codes")
+        h_planes = kept([P, J_PASSES, M], U8, "h_planes")
 
         def larger_times_gain(jb, t):
-            acc = centre_acc[jb, t]
-            larger = placed([P, M], F32, f"larger{jb}{t}", at_larger + 2 * (PACK * jb + t))
-            nc.vector.tensor_tensor(larger[:], acc[:], resp[jb, t][:], ALU.max)
+            i = PACK * jb + t
+            larger = placed([P, M], F32, f"larger{i}", at_larger[i])
+            nc.vector.tensor_tensor(larger[:], centre_acc[jb, t][:], resp[jb, t][:], ALU.max)
             gain = vec_cols[:, t, jb : jb + 1]
-            if t == PACK - 1:
-                nc.scalar.activation(h_rows[:, jb, t, :], larger[:], mybir.ActivationFunctionType.Copy, scale=gain)
-            else:
-                nc.gpsimd.tensor_scalar(h_rows[:, jb, t, :], larger[:], gain, 0.0, ALU.mult, ALU.add)
-
-        h_codes = keep.tile([P, J_PASSES, M], U32, name="h_codes", align_bytes=64)
-        h_planes = keep.tile([P, J_PASSES, M], U8, name="h_planes", align_bytes=64)
+            nc.gpsimd.tensor_scalar(h_rows[jb][:, t, :], larger[:], gain, 0.0, ALU.mult, ALU.add)
 
         def quantise_h(jb):
-            grouped = interleave(nc.scalar.copy, h_rows[:, jb, :, :])
-            nc.vector.quantize_mx(out=h_codes[:, jb, :].bitcast(FP8X4), scales=h_planes[:, jb, :], in_=grouped)
+            quantise(h_codes[:, jb, :], h_planes[:, jb, :], h_grouped[jb][:].rearrange("p m t -> p (m t)"))
 
         wd_codes, wd_planes = {}, {}
 
-        def turn_wd(picked, dtype, ident, width):
-            grouped = ring.tile([P, J_PASSES, width, PACK], BF16, name="wd_grouped", align_bytes=64)
-            for jb in range(J_PASSES):
-                bank = psum.tile([P, PACK, P], dtype, name="bank", tag="turn", bufs=TURN_BANKS)
-                for t in range(PACK):
-                    nc.tensor.transpose(bank[:, t, :], picked[:, slot_cols(jb, t)], ident)
-                nc.scalar.copy(grouped[:, jb, :, :], bank[:].bitcast(BF16).rearrange("p t n -> p n t"))
-            return grouped
-
-        def pick_pair(pair):
-            if pair == 0:
-                picked = ring.tile([P, S], U32, name="wd_picked", align_bytes=64)
-            else:
-                picked = placed([P, S], U32, "late_picked", at_resp + 12)
+        def pick_pair(pair, picked):
             window = pair_win[pair][:].rearrange("p t e -> p (t e)").bitcast(U32)
             nc.vector.tensor_copy(in_slot_order(picked[:]), window.indirect(offsets[:]))
-            return turn_wd(picked[:].bitcast(F32), F32, identity[:], 2 * P)
+            return picked
 
-        def quantise_pair(pair, grouped):
-            if pair == 0:
-                codes = placed([P, J_PASSES, 2 * P], U32, "early_codes", at_window["v_win"] + 8 * (K_PASSES - 1))
-            else:
-                codes = keep.tile([P, J_PASSES, 2 * P], U32, name=f"pair_codes{pair}", align_bytes=64)
-            planes = keep.tile([P, J_PASSES, 2 * P], U8, name=f"pair_planes{pair}", align_bytes=64)
-            nc.vector.quantize_mx(
-                out=codes[:].rearrange("p b n -> p (b n)").bitcast(FP8X4),
-                scales=planes[:].rearrange("p b n -> p (b n)"),
-                in_=grouped[:].rearrange("p b n t -> p (b n t)"),
+        def turn_pair(pair, picked, grouped, first_bank):
+            for jb in range(J_PASSES):
+                bank = in_bank([P, PACK, P], F32, f"pair_bank{pair}{jb}", first_bank + jb)
+                for t in range(PACK):
+                    nc.tensor.transpose(bank[:, t, :], picked[:, slot_cols(jb, t)].bitcast(F32), identity[:])
+                nc.scalar.copy(grouped[:, jb, :, :], bank[:].bitcast(BF16).rearrange("p t n -> p n t"))
+
+        def quantise_pair(pair, grouped, codes):
+            planes = kept([P, J_PASSES, 2 * P], U8, f"pair_planes{pair}")
+            quantise(
+                codes[:].rearrange("p b n -> p (b n)"),
+                planes[:].rearrange("p b n -> p (b n)"),
+                grouped[:].rearrange("p b n t -> p (b n t)"),
             )
             for e in range(2):
-                wd_codes[2 * pair + e] = codes[:, :, e * P : (e + 1) * P]
-                wd_planes[2 * pair + e] = planes[:, :, e * P : (e + 1) * P]
+                for jb in range(J_PASSES):
+                    wd_codes[2 * pair + e, jb] = codes[:, jb, e * P : (e + 1) * P]
+                    wd_planes[2 * pair + e, jb] = planes[:, jb, e * P : (e + 1) * P]
 
-        def pick_single(s):
-            picked = ring.tile([P, S], BF16, name="wd_picked", align_bytes=64)
-            blocks = S // (PACK * RUN) // J_PASSES
-            for jb in range(J_PASSES):
-                nc.vector.tensor_copy(
-                    in_slot_order(picked[:])[:, jb * blocks : (jb + 1) * blocks, :, :],
-                    single_win[s][:].indirect(offsets[:, 2 * jb * blocks : 2 * (jb + 1) * blocks]),
-                )
-            return turn_wd(picked[:], BF16, identity_bf16[:], P)
+        def pick_single(s, picked, cols):
+            nc.vector.tensor_copy(
+                picked[:].rearrange("p u (c r) e -> p c u e r", r=RUN), single_win[s][:].indirect(offsets[:, cols])
+            )
 
-        def quantise_single(s, grouped):
-            codes = keep.tile([P, J_PASSES, P], U32, name=f"single_codes{s}", align_bytes=64)
-            planes = keep.tile([P, J_PASSES, P], U8, name=f"single_planes{s}", align_bytes=64)
-            for jb in range(J_PASSES):
-                nc.vector.quantize_mx(
-                    out=codes[:, jb, :].bitcast(FP8X4),
-                    scales=planes[:, jb, :],
-                    in_=grouped[:, jb, :, :].rearrange("p n t -> p (n t)"),
-                )
-            wd_codes[2 * N_PAIRS + s] = codes[:]
-            wd_planes[2 * N_PAIRS + s] = planes[:]
+        def turn_single(picked, passes, bank, grouped):
+            words = picked[:].rearrange("p u w e -> p (u w e)").bitcast(F32)
+            for jb in range(passes):
+                for u in range(2):
+                    start = (u * passes + jb) * P
+                    nc.tensor.transpose(bank[:, jb, u, :], words[:, start : start + P], identity[:])
+            nc.scalar.copy(
+                grouped[:].bitcast(F32).rearrange("p (b n u) -> p b n u", b=passes, u=2),
+                bank[:].rearrange("p b u n -> p b n u"),
+            )
 
-        def project(i):
-            acc = psum.tile([P, M], F32, name="acc", tag="sum", bufs=SUM_BANKS)
+        def quantise_single(i, jb, passes, grouped, codes):
+            planes = kept([P, passes * P], U8, f"single_planes{i}{jb}")
+            quantise(codes[:], planes[:], grouped[:])
+            for k in range(passes):
+                wd_codes[i, jb + k] = codes[:, k * P : (k + 1) * P]
+                wd_planes[i, jb + k] = planes[:, k * P : (k + 1) * P]
+
+        sums = {}
+
+        def project(i, bank):
+            sums[i] = in_bank([P, M], F32, f"sum{i}", bank)
             for jb in range(J_PASSES):
                 nc.tensor.matmul_mx(
-                    out=acc[:],
-                    lhsT=wd_codes[i][:, jb, :].bitcast(FP8X4),
-                    lhsT_scale=wd_planes[i][:, jb, :],
+                    out=sums[i][:],
+                    lhsT=wd_codes[i, jb].bitcast(FP8X4),
+                    lhsT_scale=wd_planes[i, jb],
                     rhs=h_codes[:, jb, :].bitcast(FP8X4),
                     rhs_scale=h_planes[:, jb, :],
                     start=(jb == 0),
                     stop=(jb == J_PASSES - 1),
                 )
-            result = ring.tile([P, M], F32, name="result", align_bytes=64, bufs=RESULT_BUFS)
-            bias_row = BIAS_ROW + i // BIAS_TILES
-            bias = vec_cols[:, i % BIAS_TILES, bias_row : bias_row + 1]
-            nc.vector.scalar_tensor_tensor(result[:], acc[:], bias, ew_all[:], ALU.add, ALU.mult)
+
+        def finish(i):
+            result = placed([P, M], F32, f"result{i}", at_result[i])
+            bias = vec_cols[:, 0, BIAS_ROW + i : BIAS_ROW + i + 1]
+            nc.vector.scalar_tensor_tensor(result[:], sums[i][:], bias, ew_all[:], ALU.add, ALU.mult)
             nc.sync.dma_start(out[i * P : (i + 1) * P, :], result[:])
 
-        quantise_pair(0, pick_pair(0))
-        for jb, t in slots[SUM_BANKS:]:
-            neighbour_product(jb, t)
-        for a in range(K_PASSES - 1):
-            for jb, t in slots[:SUM_BANKS]:
-                centre_passes(jb, t, [a])
+        half_cols = slice(0, T // 2)
+        first_single, last_single = 2 * N_PAIRS, 2 * N_PAIRS + 1
+
+        for half in range(2):
+            round_pair(nc.scalar, 0, half, half_cols)
+        for jb, t in slots:
+            larger_times_gain(jb, t)
+        interleave(h_grouped[0][:], h_rows[0][:])
+        interleave_on_gpsimd(h_grouped[1][:], h_rows[1][:])
+        for half in range(2):
+            round_pair(nc.scalar, 1, half, half_cols)
+
+        first_picked = pick_pair(0, placed([P, S], U32, "pair_picked0", at_resp + 11))
+        quantise_h(0)
+        picked = placed([P, 2, S // PACK, 2], BF16, "single_picked0", at_resp + 15)
+        pick_single(0, picked, whole_list)
+        quantise_h(1)
+        single_grouped = placed([P, S], BF16, "single_grouped0", at_wd_raw[1, 1])
+        turn_single(picked, J_PASSES, in_bank([P, J_PASSES, 2, P], F32, "single_bank0", 2), single_grouped)
+        first_grouped = placed([P, J_PASSES, 2 * P, PACK], BF16, "pair_grouped0", at_wd_raw[1, 1] + 2)
+        turn_pair(0, first_picked, first_grouped, 0)
+        second_picked = pick_pair(1, kept([P, S], U32, "pair_picked1"))
+        second_grouped = kept([P, J_PASSES, 2 * P, PACK], BF16, "pair_grouped1")
+        turn_pair(1, second_picked, second_grouped, 5)
+        quantise_single(first_single, 0, J_PASSES, single_grouped, kept([P, J_PASSES * P], U32, "single_codes0"))
+        project(first_single, 7)
+        quantise_pair(0, first_grouped, kept([P, J_PASSES, 2 * P], U32, "pair_codes0"))
+        project(0, 3)
+        project(1, 4)
+        last_grouped = []
         for jb in range(J_PASSES):
-            for t in range(PACK):
-                centre_passes(jb, t, [K_PASSES - 1] if (jb, t) in centre_acc else range(K_PASSES))
-                larger_times_gain(jb, t)
-            quantise_h(jb)
-        quantise_pair(1, pick_pair(1))
-        project(0)
-        project(1)
-        singles_grouped = [pick_single(s) for s in range(N_SINGLES)]
-        for s in range(N_SINGLES):
-            quantise_single(s, singles_grouped[s])
-        for i in range(2, N_TILES):
-            project(i)
+            picked = placed([P, 2, P, 2], BF16, f"single_picked1{jb}", at_wd_raw[1, 1] + 2 + jb)
+            pick_single(1, picked, half_list[jb])
+            last_grouped.append(kept([P, S // J_PASSES], BF16, f"single_grouped1{jb}"))
+            turn_single(picked, 1, in_bank([P, 1, 2, P], F32, f"single_bank1{jb}", jb), last_grouped[jb])
+        finish(first_single)
+        finish(0)
+        finish(1)
+        quantise_pair(1, second_grouped, placed([P, J_PASSES, 2 * P], U32, "pair_codes1", at_single_win[1] + 6))
+        project(2, 2)
+        project(3, 5)
+        for jb in range(J_PASSES):
+            quantise_single(last_single, jb, 1, last_grouped[jb], kept([P, P], U32, f"single_codes1{jb}"))
+        project(last_single, 6)
+        finish(2)
+        finish(3)
+        finish(last_single)

@@ -415,15 +415,13 @@ def tile_list_sparse_edge_maxout_kernel(
             pick_single(1, picked, half_list[jb])
             last_grouped.append(kept([P, S // J_PASSES], BF16, f"single_grouped1{jb}"))
             turn_single(picked, 1, in_bank([P, 1, 2, P], F32, f"single_bank1{jb}", jb), last_grouped[jb])
-        finish(first_single)
-        finish(0)
-        finish(1)
         quantise_pair(1, second_grouped, placed([P, J_PASSES, 2 * P], U32, "pair_codes1", at_single_win[1] + 6))
         project(2, 2)
         project(3, 5)
+        finish(first_single)
         for jb in range(J_PASSES):
             quantise_single(last_single, jb, 1, last_grouped[jb], kept([P, P], U32, f"single_codes1{jb}"))
         project(last_single, 6)
-        finish(2)
-        finish(3)
+        for i in range(2 * N_PAIRS):
+            finish(i)
         finish(last_single)

@@ -26,7 +26,8 @@ N_TILES = N // P
 N_PAIRS = 2
 QUADS = 4
 PLANE_ROWS = 4
-SHIFT_ROWS = 112
+SCALE_ROWS = QUADS * PLANE_ROWS
+FIRST_ROW = 16
 BIAS_ROW = J_PASSES
 EW_ROW = BIAS_ROW + N_TILES
 VEC_ROWS = EW_ROW + M // P
@@ -87,12 +88,13 @@ def tile_list_sparse_edge_maxout_kernel(
         v_scale_win = kept([P, T // 4], I32, "v_scale_win")
         xn_planes = kept([P, K_PASSES, M // 4], I32, "xn_planes")
         vec_rows = kept([P, PACK * P], F32, "vec_rows")
-        v2_moved = kept([P, K_PASSES - 1, S // 4], I32, "v2_moved")
+        v2_moved = kept([P, K_PASSES, S // 4], I32, "v2_moved")
         identity = kept([P, P], F32, "identity")
-        nc.vector.memset(v2_scale_win[:], 0)
+        nc.vector.memset(v_scale_win[:], 0)
+        nc.vector.memset(v2_scale_win[0:FIRST_ROW, :], 0)
+        nc.vector.memset(v2_scale_win[P // 2 : P, :], 0)
         nc.vector.memset(vec_rows[:], 0.0)
         nc.vector.memset(xn_planes[:], 0)
-        nc.vector.memset(v_scale_win[:], 0)
         nc.vector.memset(v2_moved[:], 0)
 
         g_listed = kept([J_PASSES, PACK * P], F32, "g_listed")
@@ -155,27 +157,35 @@ def tile_list_sparse_edge_maxout_kernel(
         half_list = [slice(jb * LIST_COLS, (jb + 1) * LIST_COLS) for jb in range(J_PASSES)]
 
         v2_win, v_win, xc_raw, wd_raw, single_win = {}, {}, {}, {}, {}
-        v2_win[0] = load_words(tab2_words, 0, "v2_win", at_v2_win[0])
-        load_scale_rows(v2_scale_win, tab2_scales)
-        v2_win[1] = load_words(tab2_words, 1, "v2_win", at_v2_win[1])
-        load_xn_scales()
-        xn_codes = kept([P, K_PASSES, 2 * M], U8, "xn_codes")
-        nc.sync.dma_start(xn_codes[:].bitcast(I32), xn_words.rearrange("a p c -> p a c").bitcast(I32))
-        v2_win[2] = load_words(tab2_words, 2, "v2_win", at_v2_win[2])
-        xc_raw[0] = load_xc(0)
+        v2_rows = tab2_scales.rearrange("a q t -> (a q) t").bitcast(I32)
+        nc.sync.dma_start(v2_scale_win[FIRST_ROW : 2 * FIRST_ROW, :], v2_rows[0:SCALE_ROWS, :])
+        nc.sync.dma_start(v2_scale_win[2 * FIRST_ROW : P // 2, :], v2_rows[SCALE_ROWS : K_PASSES * SCALE_ROWS, :])
+        v2_planes = pick_scales(v2_scale_win, "v2_planes")
+
+        def move_plane(a):
+            for q in range(QUADS):
+                first = FIRST_ROW + SCALE_ROWS * a + PLANE_ROWS * q
+                nc.sync.dma_start(
+                    v2_moved[32 * q : 32 * q + PLANE_ROWS, a, :], v2_planes[first : first + PLANE_ROWS, :].bitcast(I32)
+                )
 
         def pick_v2(a):
             return pick_words(v2_win[a], placed([P, S], U32, f"v2_codes{a}", at_v2_codes + 4 * a), whole_list)
 
-        v2_codes = [pick_v2(0)]
-        v2_planes = pick_scales(v2_scale_win, "v2_planes")
-        v2_codes.append(pick_v2(1))
-        for a in range(1, K_PASSES):
-            nc.sync.dma_start(
-                v2_moved[0:SHIFT_ROWS, a - 1, :], v2_planes[PLANE_ROWS * a : PLANE_ROWS * a + SHIFT_ROWS, :].bitcast(I32)
-            )
+        for a in range(2):
+            v2_win[a] = load_words(tab2_words, a, "v2_win", at_v2_win[a])
         load_scale_rows(v_scale_win, tab_scales)
+        v2_win[2] = load_words(tab2_words, 2, "v2_win", at_v2_win[2])
+        load_xn_scales()
+        xn_codes = kept([P, K_PASSES, 2 * M], U8, "xn_codes")
+        nc.sync.dma_start(xn_codes[:].bitcast(I32), xn_words.rearrange("a p c -> p a c").bitcast(I32))
+        v2_codes = [pick_v2(0), pick_v2(1)]
+        v_planes = pick_scales(v_scale_win, "v_planes")
+        move_plane(0)
+        xc_raw[0] = load_xc(0)
+        move_plane(1)
         v_win[0] = load_words(tab_words, 0, "v_win", at_v_win[0])
+        move_plane(2)
         for a in range(1, K_PASSES):
             xc_raw[a] = load_xc(a)
             v_win[a] = load_words(tab_words, a, "v_win", at_v_win[a])
@@ -219,7 +229,7 @@ def tile_list_sparse_edge_maxout_kernel(
         neighbour_acc = {s: in_bank([P, M], F32, f"neighbour_acc{i}", i) for i, s in enumerate(slots)}
 
         def neighbour_pass(a):
-            plane = v2_planes[:] if a == 0 else v2_moved[:, a - 1, :].bitcast(U8)
+            plane = v2_moved[:, a, :].bitcast(U8)
             for jb, t in slots:
                 cols = slot_cols(jb, t)
                 nc.tensor.matmul_mx(
@@ -232,9 +242,9 @@ def tile_list_sparse_edge_maxout_kernel(
                     stop=(a == K_PASSES - 1),
                 )
 
+        v2_codes.append(pick_v2(K_PASSES - 1))
         interleave(xc_grouped[0][:], xc_raw[0][:])
         quantise_xc(0)
-        v2_codes.append(pick_v2(K_PASSES - 1))
         for a in range(K_PASSES):
             neighbour_pass(a)
         resp = {}
@@ -242,7 +252,6 @@ def tile_list_sparse_edge_maxout_kernel(
             resp[s] = placed([P, M], F32, f"resp{i}", at_resp + 2 * i)
             nc.scalar.copy(resp[s][:], neighbour_acc[s][:])
 
-        v_planes = pick_scales(v_scale_win, "v_planes")
         centre_acc = {s: in_bank([P, M], F32, f"centre_acc{i}", i) for i, s in enumerate(slots)}
 
         def centre_pass(a, jb, t, codes):

@@ -34,9 +34,8 @@ VEC_ROWS = EW_ROW + M // P
 BLOCKS = P // RUN
 LIST_COLS = S // 16 // J_PASSES
 BANK = 2048
-SCALAR_GAINS = 6
-H_SPLIT_COLS = 288
-SPLIT_COLS = 512
+SCALAR_COLS = 288
+WD_PIECES = 4
 
 
 def in_slot_order(ap):
@@ -69,16 +68,19 @@ def tile_list_sparse_edge_maxout_kernel(
         at_v2_win = [0, 8, 24]
         at_v_win = [32, 48, 64]
         at_xc_raw = [16, 40, 56]
-        at_wd_raw = {(0, 0): 0, (0, 1): 8, (1, 0): 24, (1, 1): 32}
+        at_wd_raw = [0, 24]
         at_single_win = [16, 40]
-        at_xc_codes_last = 48
         at_resp = 80
         at_v2_codes = 96
         at_larger = [96, 98, 100, 102, 72, 74, 76, 78]
         at_h_rows = 108
-        at_pair_win = [56, 102]
-        at_h_grouped_first = 8
-        at_result = [40, 42, 64, 66, 44, 68]
+        at_pair_win = [56, 88]
+        at_h_grouped_first = 12
+        at_h_grouped_second = 100
+        at_first_grouped = 104
+        at_single_grouped = [24, 36]
+        at_last_grouped = 72
+        at_result = [40, 90, 66, 68, 92, 74]
         at_xc_grouped = [116, 120, 124]
 
         offsets = keep.tile([P, S // 16], U16, name="offsets")
@@ -120,10 +122,11 @@ def tile_list_sparse_edge_maxout_kernel(
             nc.sync.dma_start(raw[:], xc[a * P * PACK : (a + 1) * P * PACK, :].rearrange("(p i) m -> p i m", i=PACK))
             return raw
 
-        def load_wd(pair, half):
+        def load_wd(pair, piece):
             rows = wdT[2 * pair * P : 2 * (pair + 1) * P, :].rearrange("(p e) t -> p e t", e=2)
-            raw = placed([P, 2, T // 2], F32, f"wd_raw{pair}{half}", at_wd_raw[pair, half])
-            nc.sync.dma_start(raw[:], rows[:, :, half * (T // 2) : (half + 1) * (T // 2)])
+            width = T // WD_PIECES
+            raw = placed([P, 2, width], F32, f"wd_raw{pair}{piece}", at_wd_raw[pair] + 4 * piece)
+            nc.sync.dma_start(raw[:], rows[:, :, piece * width : (piece + 1) * width])
             return raw
 
         def load_single(s):
@@ -215,7 +218,7 @@ def tile_list_sparse_edge_maxout_kernel(
             nc.gpsimd.tensor_scalar(grouped, planes.rearrange("p t m -> p m t"), 1.0, 0.0, ALU.mult, ALU.add)
 
         xc_codes = [kept([P, M], U32, f"xc_codes{a}") for a in range(K_PASSES - 1)]
-        xc_codes.append(placed([P, M], U32, "xc_codes_last", at_xc_codes_last))
+        xc_codes.append(placed([P, M], U32, "xc_codes_last", at_v_win[1]))
         xc_planes = kept([P, K_PASSES, M], U8, "xc_planes")
         xc_grouped = [placed([P, M, PACK], BF16, f"xc_grouped{a}", at_xc_grouped[a]) for a in range(K_PASSES)]
 
@@ -274,39 +277,37 @@ def tile_list_sparse_edge_maxout_kernel(
         for jb, t in slots:
             centre_pass(1, jb, t, codes[:, slot_cols(jb, t)])
         last = K_PASSES - 1
-        interleave(xc_grouped[last][:], xc_raw[last][:])
-        last_codes = []
+        interleave(xc_grouped[last][:, 0:SCALAR_COLS, :], xc_raw[last][:, :, 0:SCALAR_COLS])
+        interleave_on_gpsimd(xc_grouped[last][:, SCALAR_COLS:M, :], xc_raw[last][:, :, SCALAR_COLS:M])
+        quantise_xc(last)
         for jb in range(J_PASSES):
-            codes = placed([P, S // J_PASSES], U32, f"v_codes_last{jb}", at_xc_grouped[1 + jb])
-            last_codes.append(pick_words(v_win[last], codes, half_list[jb]))
-            if jb == 0:
-                quantise_xc(last)
-        for jb, t in slots:
-            centre_pass(last, jb, t, last_codes[jb][:, t * P : (t + 1) * P])
+            codes = placed([P, S // J_PASSES], U32, f"v_codes_last{jb}", at_xc_grouped[last] + 2 * jb)
+            pick_words(v_win[last], codes, half_list[jb])
+            for t in range(PACK):
+                centre_pass(last, jb, t, codes[:, t * P : (t + 1) * P])
 
-        for half in range(2):
-            wd_raw[0, half] = load_wd(0, half)
+        for piece in range(WD_PIECES):
+            wd_raw[0, piece] = load_wd(0, piece)
         single_win[0] = load_single(0)
-        for half in range(2):
-            wd_raw[1, half] = load_wd(1, half)
         single_win[1] = load_single(1)
+        for piece in range(WD_PIECES):
+            wd_raw[1, piece] = load_wd(1, piece)
 
         pair_win = {}
 
-        def round_pair(engine, pair, half, cols):
+        def round_pair(pair, pieces):
             if pair not in pair_win:
                 pair_win[pair] = placed([P, T, 2], BF16, f"pair_win{pair}", at_pair_win[pair])
-            start = half * (T // 2)
-            dst = pair_win[pair][:, start + cols.start : start + cols.stop, :]
-            src = wd_raw[pair, half][:, :, cols].rearrange("p e t -> p t e")
-            if engine is nc.scalar:
-                nc.scalar.copy(dst, src)
-            else:
-                nc.gpsimd.tensor_copy(dst, src)
+            width = T // WD_PIECES
+            for piece in pieces:
+                nc.scalar.copy(
+                    pair_win[pair][:, piece * width : (piece + 1) * width, :],
+                    wd_raw[pair, piece][:].rearrange("p e t -> p t e"),
+                )
 
         h_rows = [placed([P, PACK, M], BF16, f"h_rows{jb}", at_h_rows + 4 * jb) for jb in range(J_PASSES)]
-        h_grouped = [placed([P, M, PACK], BF16, "h_grouped0", at_h_grouped_first), kept([P, M, PACK], BF16, "h_grouped1")]
-        h_codes = kept([P, J_PASSES, M], U32, "h_codes")
+        h_grouped = [placed([P, M, PACK], BF16, "h_grouped0", at_h_grouped_first), placed([P, M, PACK], BF16, "h_grouped1", at_h_grouped_second)]
+        h_codes = placed([P, J_PASSES, M], U32, "h_codes", at_single_win[0])
         h_planes = kept([P, J_PASSES, M], U8, "h_planes")
 
         def larger_times_gain(jb, t):
@@ -321,67 +322,61 @@ def tile_list_sparse_edge_maxout_kernel(
 
         wd_codes, wd_planes = {}, {}
 
-        def pick_pair(pair, picked):
+        def pick_pair(pair, picked, cols):
             window = pair_win[pair][:].rearrange("p t e -> p (t e)").bitcast(U32)
-            nc.vector.tensor_copy(in_slot_order(picked[:]), window.indirect(offsets[:]))
-            return picked
+            nc.vector.tensor_copy(in_slot_order(picked[:]), window.indirect(offsets[:, cols]))
 
-        def turn_pair(pair, picked, grouped, first_bank):
-            for jb in range(J_PASSES):
-                bank = in_bank([P, PACK, P], F32, f"pair_bank{pair}{jb}", first_bank + jb)
-                for t in range(PACK):
-                    nc.tensor.transpose(bank[:, t, :], picked[:, slot_cols(jb, t)].bitcast(F32), identity[:])
-                nc.scalar.copy(grouped[:, jb, :, :], bank[:].bitcast(BF16).rearrange("p t n -> p n t"))
+        def turn_pair(words, bank, grouped):
+            for t in range(PACK):
+                nc.tensor.transpose(bank[:, t, :], words[t].bitcast(F32), identity[:])
+            nc.scalar.copy(grouped, bank[:].bitcast(BF16).rearrange("p t n -> p n t"))
 
-        def quantise_pair(pair, grouped, codes):
-            planes = kept([P, J_PASSES, 2 * P], U8, f"pair_planes{pair}")
+        def quantise_pair(pair, jb, passes, grouped, codes):
+            planes = kept([P, passes, 2 * P], U8, f"pair_planes{pair}{jb}")
             quantise(
                 codes[:].rearrange("p b n -> p (b n)"),
                 planes[:].rearrange("p b n -> p (b n)"),
                 grouped[:].rearrange("p b n t -> p (b n t)"),
             )
             for e in range(2):
-                for jb in range(J_PASSES):
-                    wd_codes[2 * pair + e, jb] = codes[:, jb, e * P : (e + 1) * P]
-                    wd_planes[2 * pair + e, jb] = planes[:, jb, e * P : (e + 1) * P]
+                for k in range(passes):
+                    wd_codes[2 * pair + e, jb + k] = codes[:, k, e * P : (e + 1) * P]
+                    wd_planes[2 * pair + e, jb + k] = planes[:, k, e * P : (e + 1) * P]
 
         def pick_single(s, picked, cols):
             nc.vector.tensor_copy(
                 picked[:].rearrange("p u (c r) e -> p c u e r", r=RUN), single_win[s][:].indirect(offsets[:, cols])
             )
 
-        def turn_single(picked, passes, bank, grouped):
+        def turn_single(picked, bank, grouped):
             words = picked[:].rearrange("p u w e -> p (u w e)").bitcast(F32)
-            for jb in range(passes):
+            for jb in range(J_PASSES):
                 for u in range(2):
-                    start = (u * passes + jb) * P
+                    start = (u * J_PASSES + jb) * P
                     nc.tensor.transpose(bank[:, jb, u, :], words[:, start : start + P], identity[:])
             nc.scalar.copy(
-                grouped[:].bitcast(F32).rearrange("p (b n u) -> p b n u", b=passes, u=2),
+                grouped.bitcast(F32).rearrange("p (b n u) -> p b n u", b=J_PASSES, u=2),
                 bank[:].rearrange("p b u n -> p b n u"),
             )
 
-        def quantise_single(i, jb, passes, grouped, codes):
-            planes = kept([P, passes * P], U8, f"single_planes{i}{jb}")
-            quantise(codes[:], planes[:], grouped[:])
-            for k in range(passes):
-                wd_codes[i, jb + k] = codes[:, k * P : (k + 1) * P]
-                wd_planes[i, jb + k] = planes[:, k * P : (k + 1) * P]
-
         sums = {}
 
+        def project_pass(i, jb, bank):
+            if jb == 0:
+                sums[i] = in_bank([P, M], F32, f"sum{i}", bank)
+            nc.tensor.matmul_mx(
+                out=sums[i][:],
+                lhsT=wd_codes[i, jb].bitcast(FP8X4),
+                lhsT_scale=wd_planes[i, jb],
+                rhs=h_codes[:, jb, :].bitcast(FP8X4),
+                rhs_scale=h_planes[:, jb, :],
+                start=(jb == 0),
+                stop=(jb == J_PASSES - 1),
+            )
+
         def project(i, bank):
-            sums[i] = in_bank([P, M], F32, f"sum{i}", bank)
             for jb in range(J_PASSES):
-                nc.tensor.matmul_mx(
-                    out=sums[i][:],
-                    lhsT=wd_codes[i, jb].bitcast(FP8X4),
-                    lhsT_scale=wd_planes[i, jb],
-                    rhs=h_codes[:, jb, :].bitcast(FP8X4),
-                    rhs_scale=h_planes[:, jb, :],
-                    start=(jb == 0),
-                    stop=(jb == J_PASSES - 1),
-                )
+                project_pass(i, jb, bank)
 
         def finish(i):
             result = placed([P, M], F32, f"result{i}", at_result[i])
@@ -389,48 +384,62 @@ def tile_list_sparse_edge_maxout_kernel(
             nc.vector.scalar_tensor_tensor(result[:], sums[i][:], bias, ew_all[:], ALU.add, ALU.mult)
             nc.sync.dma_start(out[i * P : (i + 1) * P, :], result[:])
 
-        half_cols = slice(0, T // 2)
         first_single, last_single = 2 * N_PAIRS, 2 * N_PAIRS + 1
 
-        for half in range(2):
-            round_pair(nc.scalar, 0, half, half_cols)
+        round_pair(0, range(WD_PIECES))
         for jb, t in slots:
             larger_times_gain(jb, t)
         interleave(h_grouped[0][:], h_rows[0][:])
         interleave_on_gpsimd(h_grouped[1][:], h_rows[1][:])
-        for half in range(2):
-            round_pair(nc.scalar, 1, half, half_cols)
 
-        first_picked = pick_pair(0, placed([P, S], U32, "pair_picked0", at_resp + 11))
-        quantise_h(0)
-        picked = placed([P, 2, S // PACK, 2], BF16, "single_picked0", at_resp + 15)
-        pick_single(0, picked, whole_list)
-        quantise_h(1)
-        single_grouped = placed([P, S], BF16, "single_grouped0", at_wd_raw[1, 1])
-        turn_single(picked, J_PASSES, in_bank([P, J_PASSES, 2, P], F32, "single_bank0", 2), single_grouped)
-        first_grouped = placed([P, J_PASSES, 2 * P, PACK], BF16, "pair_grouped0", at_wd_raw[1, 1] + 2)
-        turn_pair(0, first_picked, first_grouped, 0)
-        second_picked = pick_pair(1, kept([P, S], U32, "pair_picked1"))
-        second_grouped = kept([P, J_PASSES, 2 * P, PACK], BF16, "pair_grouped1")
-        turn_pair(1, second_picked, second_grouped, 5)
-        quantise_single(first_single, 0, J_PASSES, single_grouped, kept([P, J_PASSES * P], U32, "single_codes0"))
-        project(first_single, 7)
-        quantise_pair(0, first_grouped, kept([P, J_PASSES, 2 * P], U32, "pair_codes0"))
-        project(0, 3)
-        project(1, 4)
-        last_grouped = []
+        def pick_and_turn_pair(pair, jb, kib, grouped):
+            picked = placed([P, S // J_PASSES], U32, f"pair_picked{pair}{jb}", kib)
+            pick_pair(pair, picked, half_list[jb])
+            bank = in_bank([P, PACK, P], F32, f"pair_bank{pair}{jb}", jb)
+            turn_pair([picked[:, t * P : (t + 1) * P] for t in range(PACK)], bank, grouped)
+
+        first_grouped = placed([P, J_PASSES, 2 * P, PACK], BF16, "pair_grouped0", at_first_grouped)
         for jb in range(J_PASSES):
-            picked = placed([P, 2, P, 2], BF16, f"single_picked1{jb}", at_wd_raw[1, 1] + 2 + jb)
-            pick_single(1, picked, half_list[jb])
-            last_grouped.append(kept([P, S // J_PASSES], BF16, f"single_grouped1{jb}"))
-            turn_single(picked, 1, in_bank([P, 1, 2, P], F32, f"single_bank1{jb}", jb), last_grouped[jb])
-        quantise_pair(1, second_grouped, placed([P, J_PASSES, 2 * P], U32, "pair_codes1", at_single_win[1] + 6))
-        project(2, 2)
-        project(3, 5)
-        finish(first_single)
+            pick_and_turn_pair(0, jb, at_resp + 12 + 2 * jb, first_grouped[:, jb, :, :])
+
+        def pick_and_turn_single(s, kib):
+            picked = placed([P, 2, S // PACK, 2], BF16, f"single_picked{s}", kib)
+            pick_single(s, picked, whole_list)
+            grouped = placed([P, S], BF16, f"single_grouped{s}", at_single_grouped[s])
+            turn_single(picked, in_bank([P, J_PASSES, 2, P], F32, f"single_bank{s}", 2 + s), grouped[:])
+            return grouped
+
+        def quantise_single(i, grouped, codes):
+            planes = kept([P, J_PASSES, P], U8, f"single_planes{i}")
+            quantise(codes[:].rearrange("p b n -> p (b n)"), planes[:].rearrange("p b n -> p (b n)"), grouped[:])
+            for jb in range(J_PASSES):
+                wd_codes[i, jb] = codes[:, jb, :]
+                wd_planes[i, jb] = planes[:, jb, :]
+
+        round_pair(1, range(1))
+        grouped = pick_and_turn_single(0, at_larger[-1])
+        round_pair(1, range(1, WD_PIECES))
         for jb in range(J_PASSES):
-            quantise_single(last_single, jb, 1, last_grouped[jb], kept([P, P], U32, f"single_codes1{jb}"))
-        project(last_single, 6)
-        for i in range(2 * N_PAIRS):
+            quantise_h(jb)
+        codes = placed([P, J_PASSES, 2 * P], U32, "pair_codes0", at_h_grouped_second)
+        quantise_pair(0, 0, J_PASSES, first_grouped, codes)
+        project(0, 4)
+        project(1, 5)
+        quantise_single(first_single, grouped, placed([P, J_PASSES, P], U32, "single_codes0", at_first_grouped))
+        project(first_single, 6)
+        grouped = pick_and_turn_single(1, at_single_grouped[0])
+        finish(0)
+        last_grouped = [placed([P, 1, 2 * P, PACK], BF16, f"pair_grouped1{jb}", at_last_grouped + 2 * jb) for jb in range(J_PASSES)]
+        pick_and_turn_pair(1, 0, at_single_win[1] + 2, last_grouped[0][:, 0, :, :])
+        quantise_single(last_single, grouped, kept([P, J_PASSES, P], U32, "single_codes1"))
+        project(last_single, 7)
+        pick_and_turn_pair(1, 1, at_single_grouped[1], last_grouped[1][:, 0, :, :])
+        for jb in range(J_PASSES):
+            quantise_pair(1, jb, 1, last_grouped[jb], placed([P, 1, 2 * P], U32, f"pair_codes1{jb}", at_pair_win[1] + jb))
+            for i in (2, 3):
+                project_pass(i, jb, i)
+            if jb == 0:
+                finish(1)
+                finish(first_single)
+        for i in (last_single, 2, 3):
             finish(i)
-        finish(last_single)

@@ -60,27 +60,28 @@ def tile_list_sparse_edge_maxout_kernel(
             return keep.tile(shape, dtype, name=name, align_bytes=64)
 
         def placed(shape, dtype, name, kib):
-            return shared.tile(shape, dtype, name=name, align_bytes=64, offset=kib * 1024)
+            return shared.tile(shape, dtype, name=name, align_bytes=64, offset=int(kib * 1024))
 
         def in_bank(shape, dtype, name, bank):
             return psum.tile(shape, dtype, name=name, offset=bank * BANK)
 
-        at_v2_win = [0, 8, 24]
-        at_v_win = [32, 48, 64]
-        at_xc_raw = [16, 40, 56]
-        at_wd_raw = [0, 24]
-        at_single_win = [16, 40]
+        at_v2_win = [23.5, 46.5, 62]
+        at_v_win = [8, 31, 54]
+        at_xc_raw = [0, 16, 39]
+        at_v2_listed = 7.5
+        at_wd_raw = [[0, 4, 8, 12], [41, 45, 54, 58]]
+        at_single_win = [16, 33]
         at_resp = 80
         at_v2_codes = 96
         at_larger = [96, 98, 100, 102, 72, 74, 76, 78]
         at_h_rows = 108
-        at_pair_win = [56, 88]
+        at_pair_win = [62, 88]
         at_h_grouped_first = 12
         at_h_grouped_second = 100
         at_first_grouped = 104
-        at_single_grouped = [24, 36]
+        at_single_grouped = [41, 58]
         at_last_grouped = 72
-        at_result = [40, 90, 66, 68, 92, 74]
+        at_result = [33, 90, 66, 68, 92, 74]
         at_xc_grouped = [116, 120, 124]
 
         offsets = keep.tile([P, S // 16], U16, name="offsets")
@@ -92,12 +93,13 @@ def tile_list_sparse_edge_maxout_kernel(
         vec_rows = kept([P, PACK * P], F32, "vec_rows")
         v2_moved = kept([P, K_PASSES, S // 4], I32, "v2_moved")
         identity = kept([P, P], F32, "identity")
-        nc.vector.memset(v_scale_win[:], 0)
-        nc.vector.memset(v2_scale_win[0:FIRST_ROW, :], 0)
-        nc.vector.memset(v2_scale_win[P // 2 : P, :], 0)
         nc.vector.memset(vec_rows[:], 0.0)
         nc.vector.memset(xn_planes[:], 0)
+        nc.vector.memset(v2_scale_win[0:FIRST_ROW, :], 0)
+        nc.vector.memset(v2_scale_win[P // 2 : P, :], 0)
+        nc.vector.memset(v_scale_win[:], 0)
         nc.vector.memset(v2_moved[:], 0)
+
 
         g_listed = kept([J_PASSES, PACK * P], F32, "g_listed")
         nc.gpsimd.dma_start(g_listed[:], g.rearrange("(b j) -> b j", b=J_PASSES))
@@ -112,7 +114,7 @@ def tile_list_sparse_edge_maxout_kernel(
 
         def load_scale_rows(win, src):
             for q in range(QUADS):
-                nc.sync.dma_start(
+                nc.gpsimd.dma_start(
                     win[32 * q : 32 * q + PLANE_ROWS * K_PASSES, :],
                     src[:, PLANE_ROWS * q : PLANE_ROWS * (q + 1), :].bitcast(I32),
                 )
@@ -125,7 +127,7 @@ def tile_list_sparse_edge_maxout_kernel(
         def load_wd(pair, piece):
             rows = wdT[2 * pair * P : 2 * (pair + 1) * P, :].rearrange("(p e) t -> p e t", e=2)
             width = T // WD_PIECES
-            raw = placed([P, 2, width], F32, f"wd_raw{pair}{piece}", at_wd_raw[pair] + 4 * piece)
+            raw = placed([P, 2, width], F32, f"wd_raw{pair}{piece}", at_wd_raw[pair][piece])
             nc.sync.dma_start(raw[:], rows[:, :, piece * width : (piece + 1) * width])
             return raw
 
@@ -146,8 +148,7 @@ def tile_list_sparse_edge_maxout_kernel(
             nc.vector.tensor_copy(in_slot_order(picked[:]), win[:].bitcast(U32).indirect(offsets[:, cols]))
             return picked
 
-        def pick_scales(win, name):
-            listed = kept([P, S], U8, name + "_listed")
+        def pick_scales(win, listed, name):
             nc.vector.tensor_copy(listed[:], win[:].bitcast(U8).indirect(offsets[:]))
             planes = kept([P, S], U8, name)
             nc.vector.tensor_copy(
@@ -163,7 +164,7 @@ def tile_list_sparse_edge_maxout_kernel(
         v2_rows = tab2_scales.rearrange("a q t -> (a q) t").bitcast(I32)
         nc.sync.dma_start(v2_scale_win[FIRST_ROW : 2 * FIRST_ROW, :], v2_rows[0:SCALE_ROWS, :])
         nc.sync.dma_start(v2_scale_win[2 * FIRST_ROW : P // 2, :], v2_rows[SCALE_ROWS : K_PASSES * SCALE_ROWS, :])
-        v2_planes = pick_scales(v2_scale_win, "v2_planes")
+        v2_planes = pick_scales(v2_scale_win, placed([P, S], U8, "v2_listed", at_v2_listed), "v2_planes")
 
         def move_plane(a):
             for q in range(QUADS):
@@ -183,7 +184,6 @@ def tile_list_sparse_edge_maxout_kernel(
         xn_codes = kept([P, K_PASSES, 2 * M], U8, "xn_codes")
         nc.sync.dma_start(xn_codes[:].bitcast(I32), xn_words.rearrange("a p c -> p a c").bitcast(I32))
         v2_codes = [pick_v2(0), pick_v2(1)]
-        v_planes = pick_scales(v_scale_win, "v_planes")
         move_plane(0)
         xc_raw[0] = load_xc(0)
         move_plane(1)
@@ -246,6 +246,7 @@ def tile_list_sparse_edge_maxout_kernel(
                 )
 
         v2_codes.append(pick_v2(K_PASSES - 1))
+        v_planes = pick_scales(v_scale_win, placed([P, S], U8, "v_listed", at_v2_win[K_PASSES - 1]), "v_planes")
         interleave(xc_grouped[0][:], xc_raw[0][:])
         quantise_xc(0)
         for a in range(K_PASSES):
@@ -431,9 +432,9 @@ def tile_list_sparse_edge_maxout_kernel(
         finish(0)
         last_grouped = [placed([P, 1, 2 * P, PACK], BF16, f"pair_grouped1{jb}", at_last_grouped + 2 * jb) for jb in range(J_PASSES)]
         pick_and_turn_pair(1, 0, at_single_win[1] + 2, last_grouped[0][:, 0, :, :])
-        quantise_single(last_single, grouped, kept([P, J_PASSES, P], U32, "single_codes1"))
+        pick_and_turn_pair(1, 1, at_single_win[1] + 4, last_grouped[1][:, 0, :, :])
+        quantise_single(last_single, grouped, placed([P, J_PASSES, P], U32, "single_codes1", at_pair_win[1] + 6))
         project(last_single, 7)
-        pick_and_turn_pair(1, 1, at_single_grouped[1], last_grouped[1][:, 0, :, :])
         for jb in range(J_PASSES):
             quantise_pair(1, jb, 1, last_grouped[jb], placed([P, 1, 2 * P], U32, f"pair_codes1{jb}", at_pair_win[1] + jb))
             for i in (2, 3):

@@ -15,7 +15,7 @@ U8 = mybir.dt.uint8
 FP8X4 = mybir.dt.float8_e4m3fn_x4
 FP4X4 = mybir.dt.float4_e2m1fn_x4
 ALU = mybir.AluOpType
-COPY = mybir.ActivationFunctionType.Copy
+IDENTITY = mybir.ActivationFunctionType.Identity
 
 P = 128
 PACK = 4
@@ -81,7 +81,7 @@ def tile_list_sparse_edge_maxout_kernel(
         at_first_grouped = 104
         at_single_grouped = [41, 58]
         at_last_grouped = 72
-        at_result = [33, 90, 66, 68, 92, 74]
+        at_result = [62, 64, 76, 68, 92, 74]
         at_xc_grouped = [116, 120, 124]
 
         offsets = keep.tile([P, S // 16], U16, name="offsets")
@@ -379,6 +379,24 @@ def tile_list_sparse_edge_maxout_kernel(
             for jb in range(J_PASSES):
                 project_pass(i, jb, bank)
 
+        def add_bias(i, kib):
+            biased = placed([P, M], F32, f"biased{i}", kib)
+            nc.scalar.activation(biased[:], sums[i][:], IDENTITY, bias=vec_cols[:, 0, BIAS_ROW + i : BIAS_ROW + i + 1])
+            return biased
+
+        def weigh_on_gpsimd(i, biased):
+            result = placed([P, M], F32, f"result{i}", at_result[i])
+            nc.gpsimd.tensor_tensor(result[:], biased[:], ew_all[:], ALU.mult)
+            nc.sync.dma_start(out[i * P : (i + 1) * P, :], result[:])
+
+        def finish_in_halves(i):
+            bias = vec_cols[:, 0, BIAS_ROW + i : BIAS_ROW + i + 1]
+            for half in range(2):
+                cols = slice(half * M // 2, (half + 1) * M // 2)
+                result = placed([P, M // 2], F32, f"result{i}{half}", at_result[i] + half)
+                nc.vector.scalar_tensor_tensor(result[:], sums[i][:, cols], bias, ew_all[:, cols], ALU.add, ALU.mult)
+                nc.sync.dma_start(out[i * P : (i + 1) * P, cols], result[:])
+
         def finish(i):
             result = placed([P, M], F32, f"result{i}", at_result[i])
             bias = vec_cols[:, 0, BIAS_ROW + i : BIAS_ROW + i + 1]
@@ -419,7 +437,7 @@ def tile_list_sparse_edge_maxout_kernel(
 
         round_pair(1, range(1))
         grouped = pick_and_turn_single(0, at_larger[-1])
-        round_pair(1, range(1, WD_PIECES))
+        round_pair(1, range(1, WD_PIECES - 1))
         for jb in range(J_PASSES):
             quantise_h(jb)
         codes = placed([P, J_PASSES, 2 * P], U32, "pair_codes0", at_h_grouped_second)
@@ -428,19 +446,34 @@ def tile_list_sparse_edge_maxout_kernel(
         project(1, 5)
         quantise_single(first_single, grouped, placed([P, J_PASSES, P], U32, "single_codes0", at_first_grouped))
         project(first_single, 6)
+        weigh_on_gpsimd(0, add_bias(0, at_wd_raw[1][2]))
+        round_pair(1, range(WD_PIECES - 1, WD_PIECES))
+        weigh_on_gpsimd(1, add_bias(1, at_wd_raw[1][3] + 2))
         grouped = pick_and_turn_single(1, at_single_grouped[0])
-        finish(0)
-        last_grouped = [placed([P, 1, 2 * P, PACK], BF16, f"pair_grouped1{jb}", at_last_grouped + 2 * jb) for jb in range(J_PASSES)]
-        pick_and_turn_pair(1, 0, at_single_win[1] + 2, last_grouped[0][:, 0, :, :])
-        pick_and_turn_pair(1, 1, at_single_win[1] + 4, last_grouped[1][:, 0, :, :])
+        first_half = placed([P, 1, 2 * P, PACK], BF16, "pair_grouped10", at_last_grouped)
+        pick_and_turn_pair(1, 0, at_single_win[1] + 2, first_half[:, 0, :, :])
+        picked = placed([P, S // J_PASSES], U32, "pair_picked11", at_single_win[1] + 4)
+        pick_pair(1, picked, half_list[1])
+        bank = in_bank([P, PACK, P], F32, "pair_bank11", 1)
+        for t in range(PACK):
+            nc.tensor.transpose(bank[:, t, :], picked[:, t * P : (t + 1) * P].bitcast(F32), identity[:])
+        last_grouped = []
+        for e in range(2):
+            last_grouped.append(placed([P, P, PACK], BF16, f"pair_grouped11{e}", at_last_grouped + 2 + 2 * e))
+            nc.scalar.copy(last_grouped[e][:], bank[:].bitcast(BF16)[:, :, e * P : (e + 1) * P].rearrange("p t n -> p n t"))
         quantise_single(last_single, grouped, placed([P, J_PASSES, P], U32, "single_codes1", at_pair_win[1] + 6))
         project(last_single, 7)
-        for jb in range(J_PASSES):
-            quantise_pair(1, jb, 1, last_grouped[jb], placed([P, 1, 2 * P], U32, f"pair_codes1{jb}", at_pair_win[1] + jb))
-            for i in (2, 3):
-                project_pass(i, jb, i)
-            if jb == 0:
-                finish(1)
-                finish(first_single)
-        for i in (last_single, 2, 3):
-            finish(i)
+        quantise_pair(1, 0, 1, first_half, placed([P, 1, 2 * P], U32, "pair_codes10", at_pair_win[1]))
+        for i in (2, 3):
+            project_pass(i, 0, i)
+        finish(first_single)
+        for e in range(2):
+            codes = kept([P, P], U32, f"pair_codes11{e}")
+            planes = kept([P, P], U8, f"pair_planes11{e}")
+            quantise(codes[:], planes[:], last_grouped[e][:].rearrange("p n t -> p (n t)"))
+            wd_codes[2 + e, 1], wd_planes[2 + e, 1] = codes[:], planes[:]
+            project_pass(2 + e, 1, 2 + e)
+            if e == 0:
+                finish(last_single)
+        finish(2)
+        finish_in_halves(3)

@@ -69,8 +69,8 @@ def tile_list_sparse_edge_maxout_kernel(
         at_v_win = [8, 31, 54]
         at_xc_raw = [0, 16, 39]
         at_v2_listed = 7.5
-        at_wd_raw = [[0, 4, 8, 12], [41, 45, 54, 58]]
-        at_single_win = [16, 33]
+        at_wd_raw = [[0, 4, 8, 12], [31, 35, 39, 43]]
+        at_single_win = [16, 54]
         at_resp = 80
         at_v2_codes = 96
         at_larger = [96, 98, 100, 102, 72, 74, 76, 78]
@@ -79,9 +79,9 @@ def tile_list_sparse_edge_maxout_kernel(
         at_h_grouped_first = 12
         at_h_grouped_second = 100
         at_first_grouped = 104
-        at_single_grouped = [41, 58]
+        at_single_grouped = [31, 128]
         at_last_grouped = 72
-        at_result = [62, 64, 76, 68, 92, 74]
+        at_result = [62, 64, 76, 68, 66, 130]
         at_xc_grouped = [116, 120, 124]
 
         offsets = keep.tile([P, S // 16], U16, name="offsets")
@@ -290,18 +290,18 @@ def tile_list_sparse_edge_maxout_kernel(
         for piece in range(WD_PIECES):
             wd_raw[0, piece] = load_wd(0, piece)
         single_win[0] = load_single(0)
-        single_win[1] = load_single(1)
         for piece in range(WD_PIECES):
             wd_raw[1, piece] = load_wd(1, piece)
+        single_win[1] = load_single(1)
 
         pair_win = {}
 
-        def round_pair(pair, pieces):
+        def round_pair(pair, pieces, copy=nc.scalar.copy):
             if pair not in pair_win:
                 pair_win[pair] = placed([P, T, 2], BF16, f"pair_win{pair}", at_pair_win[pair])
             width = T // WD_PIECES
             for piece in pieces:
-                nc.scalar.copy(
+                copy(
                     pair_win[pair][:, piece * width : (piece + 1) * width, :],
                     wd_raw[pair, piece][:].rearrange("p e t -> p t e"),
                 )
@@ -437,7 +437,7 @@ def tile_list_sparse_edge_maxout_kernel(
 
         round_pair(1, range(1))
         grouped = pick_and_turn_single(0, at_larger[-1])
-        round_pair(1, range(1, WD_PIECES - 1))
+        round_pair(1, [1, 3])
         for jb in range(J_PASSES):
             quantise_h(jb)
         codes = placed([P, J_PASSES, 2 * P], U32, "pair_codes0", at_h_grouped_second)
@@ -446,34 +446,36 @@ def tile_list_sparse_edge_maxout_kernel(
         project(1, 5)
         quantise_single(first_single, grouped, placed([P, J_PASSES, P], U32, "single_codes0", at_first_grouped))
         project(first_single, 6)
-        weigh_on_gpsimd(0, add_bias(0, at_wd_raw[1][2]))
-        round_pair(1, range(WD_PIECES - 1, WD_PIECES))
+        round_pair(1, [2], nc.vector.tensor_copy)
+        weigh_on_gpsimd(0, add_bias(0, at_wd_raw[1][3]))
         weigh_on_gpsimd(1, add_bias(1, at_wd_raw[1][3] + 2))
-        grouped = pick_and_turn_single(1, at_single_grouped[0])
-        first_half = placed([P, 1, 2 * P, PACK], BF16, "pair_grouped10", at_last_grouped)
-        pick_and_turn_pair(1, 0, at_single_win[1] + 2, first_half[:, 0, :, :])
-        picked = placed([P, S // J_PASSES], U32, "pair_picked11", at_single_win[1] + 4)
-        pick_pair(1, picked, half_list[1])
-        bank = in_bank([P, PACK, P], F32, "pair_bank11", 1)
-        for t in range(PACK):
-            nc.tensor.transpose(bank[:, t, :], picked[:, t * P : (t + 1) * P].bitcast(F32), identity[:])
+        weigh_on_gpsimd(first_single, add_bias(first_single, at_wd_raw[1][2]))
+        second_grouped = []
+        for jb in range(J_PASSES):
+            second_grouped.append(placed([P, 1, 2 * P, PACK], BF16, f"pair_grouped1{jb}", at_last_grouped + 2 * jb))
+            pick_and_turn_pair(1, jb, at_h_grouped_first + 2 * jb, second_grouped[jb][:, 0, :, :])
         last_grouped = []
-        for e in range(2):
-            last_grouped.append(placed([P, P, PACK], BF16, f"pair_grouped11{e}", at_last_grouped + 2 + 2 * e))
-            nc.scalar.copy(last_grouped[e][:], bank[:].bitcast(BF16)[:, :, e * P : (e + 1) * P].rearrange("p t n -> p n t"))
-        quantise_single(last_single, grouped, placed([P, J_PASSES, P], U32, "single_codes1", at_pair_win[1] + 6))
-        project(last_single, 7)
-        quantise_pair(1, 0, 1, first_half, placed([P, 1, 2 * P], U32, "pair_codes10", at_pair_win[1]))
-        for i in (2, 3):
-            project_pass(i, 0, i)
-        finish(first_single)
-        for e in range(2):
-            codes = kept([P, P], U32, f"pair_codes11{e}")
-            planes = kept([P, P], U8, f"pair_planes11{e}")
-            quantise(codes[:], planes[:], last_grouped[e][:].rearrange("p n t -> p (n t)"))
-            wd_codes[2 + e, 1], wd_planes[2 + e, 1] = codes[:], planes[:]
-            project_pass(2 + e, 1, 2 + e)
-            if e == 0:
-                finish(last_single)
+        for jb in range(J_PASSES):
+            picked = placed([P, 2, P, 2], BF16, f"last_picked{jb}", [at_h_grouped_first, at_last_grouped][jb])
+            pick_single(1, picked, half_list[jb])
+            words = picked[:].rearrange("p u w e -> p (u w e)").bitcast(F32)
+            bank = in_bank([P, 2, P], F32, f"last_bank{jb}", 2 + jb)
+            for u in range(2):
+                nc.tensor.transpose(bank[:, u, :], words[:, u * P : (u + 1) * P], identity[:])
+            last_grouped.append(placed([P, S // J_PASSES], BF16, f"last_grouped{jb}", at_single_grouped[1] + jb))
+            nc.scalar.copy(
+                last_grouped[jb][:].bitcast(F32).rearrange("p (n u) -> p n u", u=2), bank[:].rearrange("p u n -> p n u")
+            )
+            codes = placed([P, 1, 2 * P], U32, f"pair_codes1{jb}", at_h_grouped_first + 2 + jb)
+            quantise_pair(1, jb, 1, second_grouped[jb], codes)
+            project_pass(2, jb, 7)
+            project_pass(3, jb, 4)
+        for jb in range(J_PASSES):
+            codes = kept([P, P], U32, f"last_codes{jb}")
+            planes = kept([P, P], U8, f"last_planes{jb}")
+            quantise(codes[:], planes[:], last_grouped[jb][:])
+            wd_codes[last_single, jb], wd_planes[last_single, jb] = codes[:], planes[:]
+            project_pass(last_single, jb, 5)
         finish(2)
-        finish_in_halves(3)
+        finish(3)
+        finish_in_halves(last_single)

from contextlib import ExitStack

import concourse.mybir as mybir
from concourse.masks import make_identity

K, T, S, M, N = 1536, 2048, 1024, 512, 768
FLOPS = 2 * (2 * K * S * M) + 2 * N * S * M

F32 = mybir.dt.float32
BF16 = mybir.dt.bfloat16
I32 = mybir.dt.int32
U32 = mybir.dt.uint32
U16 = mybir.dt.uint16
U8 = mybir.dt.uint8
FP8X4 = mybir.dt.float8_e4m3fn_x4
FP4X4 = mybir.dt.float4_e2m1fn_x4
ALU = mybir.AluOpType
IDENTITY = mybir.ActivationFunctionType.Identity

P = 128
PACK = 4
RUN = 8
K_PASSES = K // (P * PACK)
J_PASSES = S // (P * PACK)
N_TILES = N // P
N_PAIRS = 2
QUADS = 4
PLANE_ROWS = 4
SCALE_ROWS = QUADS * PLANE_ROWS
FIRST_ROW = 16
BIAS_ROW = J_PASSES
EW_ROW = BIAS_ROW + N_TILES
VEC_ROWS = EW_ROW + M // P
BLOCKS = P // RUN
LIST_COLS = S // 16 // J_PASSES
BANK = 2048
SCALAR_COLS = 288
WD_PIECES = 4


def in_slot_order(ap):
    return ap.rearrange("p (t c r) -> p c t r", t=PACK, r=RUN)


def slot_cols(jb, t):
    start = t * (S // PACK) + jb * P
    return slice(start, start + P)


def tile_list_sparse_edge_maxout_kernel(
    tc, tab_words, tab_scales, tab2_words, tab2_scales, offs, xc, xn_words, xn_scales, g, wdT, b, ew, out
):
    nc = tc.nc
    with ExitStack() as ctx:
        keep = ctx.enter_context(tc.tile_pool(name="keep", bufs=1))
        psum = ctx.enter_context(tc.psum_pool(name="psum", bufs=1))
        shared = ctx.enter_context(tc.tile_pool(name="shared", bufs=1))

        def kept(shape, dtype, name):
            return keep.tile(shape, dtype, name=name, align_bytes=64)

        def placed(shape, dtype, name, kib):
            return shared.tile(shape, dtype, name=name, align_bytes=64, offset=int(kib * 1024))

        def in_bank(shape, dtype, name, bank):
            return psum.tile(shape, dtype, name=name, offset=bank * BANK)

        at_v2_win = [23.5, 46.5, 62]
        at_v_win = [8, 31, 54]
        at_xc_raw = [0, 16, 39]
        at_v2_listed = 7.5
        at_wd_raw = [[0, 4, 8, 12], [31, 35, 39, 43]]
        at_single_win = [16, 54]
        at_resp = 80
        at_v2_codes = 96
        at_larger = [96, 98, 100, 102, 72, 74, 76, 78]
        at_h_rows = 108
        at_pair_win = [62, 88]
        at_h_grouped_first = 12
        at_h_grouped_second = 100
        at_first_grouped = 104
        at_single_grouped = [31, 128]
        at_last_grouped = 72
        at_result = [62, 64, 76, 68, 66, 130]
        at_xc_grouped = [116, 120, 124]

        offsets = keep.tile([P, S // 16], U16, name="offsets")
        nc.sync.dma_start(offsets[:], offs)

        v2_scale_win = kept([P, T // 4], I32, "v2_scale_win")
        v_scale_win = kept([P, T // 4], I32, "v_scale_win")
        xn_planes = kept([P, K_PASSES, M // 4], I32, "xn_planes")
        vec_rows = kept([P, PACK * P], F32, "vec_rows")
        v2_moved = kept([P, K_PASSES, S // 4], I32, "v2_moved")
        identity = kept([P, P], F32, "identity")
        nc.vector.memset(vec_rows[:], 0.0)
        nc.vector.memset(xn_planes[:], 0)
        nc.vector.memset(v2_scale_win[0:FIRST_ROW, :], 0)
        nc.vector.memset(v2_scale_win[P // 2 : P, :], 0)
        nc.vector.memset(v_scale_win[:], 0)
        nc.vector.memset(v2_moved[:], 0)


        g_listed = kept([J_PASSES, PACK * P], F32, "g_listed")
        nc.gpsimd.dma_start(g_listed[:], g.rearrange("(b j) -> b j", b=J_PASSES))
        nc.gpsimd.dma_start(vec_rows[BIAS_ROW:EW_ROW, 0:P], b.rearrange("(u n) -> u n", n=P))
        nc.gpsimd.dma_start(vec_rows[EW_ROW:VEC_ROWS, 0:P], ew.rearrange("(u m) -> u m", m=P))
        make_identity(nc, identity[:])

        def load_words(src, a, name, kib):
            win = placed([P, T], I32, f"{name}{a}", kib)
            nc.sync.dma_start(win[:], src[a].rearrange("p n i -> p (n i)").bitcast(I32))
            return win

        def load_scale_rows(win, src):
            for q in range(QUADS):
                nc.gpsimd.dma_start(
                    win[32 * q : 32 * q + PLANE_ROWS * K_PASSES, :],
                    src[:, PLANE_ROWS * q : PLANE_ROWS * (q + 1), :].bitcast(I32),
                )

        def load_xc(a):
            raw = placed([P, PACK, M], F32, f"xc_raw{a}", at_xc_raw[a])
            nc.sync.dma_start(raw[:], xc[a * P * PACK : (a + 1) * P * PACK, :].rearrange("(p i) m -> p i m", i=PACK))
            return raw

        def load_wd(pair, piece):
            rows = wdT[2 * pair * P : 2 * (pair + 1) * P, :].rearrange("(p e) t -> p e t", e=2)
            width = T // WD_PIECES
            raw = placed([P, 2, width], F32, f"wd_raw{pair}{piece}", at_wd_raw[pair][piece])
            nc.sync.dma_start(raw[:], rows[:, :, piece * width : (piece + 1) * width])
            return raw

        def load_single(s):
            win = placed([P, T], F32, f"single_win{s}", at_single_win[s])
            i = 2 * N_PAIRS + s
            nc.sync.dma_start(win[:], wdT[i * P : (i + 1) * P, :])
            return win

        def load_xn_scales():
            for q in range(QUADS):
                nc.sync.dma_start(
                    xn_planes[32 * q : 32 * q + PLANE_ROWS, :, :],
                    xn_scales[:, PLANE_ROWS * q : PLANE_ROWS * (q + 1), :].rearrange("a r m -> r a m").bitcast(I32),
                )

        def pick_words(win, picked, cols):
            nc.vector.tensor_copy(in_slot_order(picked[:]), win[:].bitcast(U32).indirect(offsets[:, cols]))
            return picked

        def pick_scales(win, listed, name):
            nc.vector.tensor_copy(listed[:], win[:].bitcast(U8).indirect(offsets[:]))
            planes = kept([P, S], U8, name)
            nc.vector.tensor_copy(
                planes[:].bitcast(I32).rearrange("p (t c w) -> p t c w", t=PACK, w=RUN // 4),
                listed[:].bitcast(I32).rearrange("p (c t w) -> p t c w", t=PACK, w=RUN // 4),
            )
            return planes

        whole_list = slice(0, S // 16)
        half_list = [slice(jb * LIST_COLS, (jb + 1) * LIST_COLS) for jb in range(J_PASSES)]

        v2_win, v_win, xc_raw, wd_raw, single_win = {}, {}, {}, {}, {}
        v2_rows = tab2_scales.rearrange("a q t -> (a q) t").bitcast(I32)
        nc.sync.dma_start(v2_scale_win[FIRST_ROW : 2 * FIRST_ROW, :], v2_rows[0:SCALE_ROWS, :])
        nc.sync.dma_start(v2_scale_win[2 * FIRST_ROW : P // 2, :], v2_rows[SCALE_ROWS : K_PASSES * SCALE_ROWS, :])
        v2_planes = pick_scales(v2_scale_win, placed([P, S], U8, "v2_listed", at_v2_listed), "v2_planes")

        def move_plane(a):
            for q in range(QUADS):
                first = FIRST_ROW + SCALE_ROWS * a + PLANE_ROWS * q
                nc.sync.dma_start(
                    v2_moved[32 * q : 32 * q + PLANE_ROWS, a, :], v2_planes[first : first + PLANE_ROWS, :].bitcast(I32)
                )

        def pick_v2(a):
            return pick_words(v2_win[a], placed([P, S], U32, f"v2_codes{a}", at_v2_codes + 4 * a), whole_list)

        for a in range(2):
            v2_win[a] = load_words(tab2_words, a, "v2_win", at_v2_win[a])
        load_scale_rows(v_scale_win, tab_scales)
        v2_win[2] = load_words(tab2_words, 2, "v2_win", at_v2_win[2])
        load_xn_scales()
        xn_codes = kept([P, K_PASSES, 2 * M], U8, "xn_codes")
        nc.sync.dma_start(xn_codes[:].bitcast(I32), xn_words.rearrange("a p c -> p a c").bitcast(I32))
        v2_codes = [pick_v2(0), pick_v2(1)]
        move_plane(0)
        xc_raw[0] = load_xc(0)
        move_plane(1)
        v_win[0] = load_words(tab_words, 0, "v_win", at_v_win[0])
        move_plane(2)
        for a in range(1, K_PASSES):
            xc_raw[a] = load_xc(a)
            v_win[a] = load_words(tab_words, a, "v_win", at_v_win[a])

        nc.scalar.copy(
            vec_rows[0:J_PASSES, :].rearrange("b (t q r) -> b t q r", t=PACK, r=RUN),
            g_listed[:].rearrange("b (q t r) -> b t q r", t=PACK, r=RUN),
        )
        vec_cols = kept([P, PACK, VEC_ROWS], F32, "vec_cols")
        turned = in_bank([P, PACK, P], F32, "turned", 6)
        for u in range(PACK):
            nc.tensor.transpose(turned[:, u, :], vec_rows[:, u * P : (u + 1) * P], identity[:])
        nc.scalar.copy(vec_cols[:], turned[:, :, 0:VEC_ROWS])
        spread = in_bank([P, M // P, P], F32, "spread", 7)
        for c in range(M // P):
            column = vec_cols[:, 0, EW_ROW + c : EW_ROW + c + 1]
            nc.tensor.transpose(spread[:, c, :], column.to_broadcast([P, P]), identity[:])
        ew_all = kept([P, M], F32, "ew_all")
        nc.scalar.copy(ew_all[:], spread[:].rearrange("p c m -> p (c m)"))

        def interleave(grouped, planes):
            nc.scalar.copy(
                grouped.rearrange("p (c i) t -> p c t i", i=4), planes.rearrange("p t (c i) -> p c t i", i=4)
            )

        def interleave_on_gpsimd(grouped, planes):
            nc.gpsimd.tensor_scalar(grouped, planes.rearrange("p t m -> p m t"), 1.0, 0.0, ALU.mult, ALU.add)

        xc_codes = [kept([P, M], U32, f"xc_codes{a}") for a in range(K_PASSES - 1)]
        xc_codes.append(placed([P, M], U32, "xc_codes_last", at_v_win[1]))
        xc_planes = kept([P, K_PASSES, M], U8, "xc_planes")
        xc_grouped = [placed([P, M, PACK], BF16, f"xc_grouped{a}", at_xc_grouped[a]) for a in range(K_PASSES)]

        def quantise(codes, planes, grouped):
            nc.vector.quantize_mx(out=codes.bitcast(FP8X4), scales=planes, in_=grouped)

        def quantise_xc(a):
            quantise(xc_codes[a][:], xc_planes[:, a, :], xc_grouped[a][:].rearrange("p m t -> p (m t)"))

        slots = [(jb, t) for jb in range(J_PASSES) for t in range(PACK)]
        neighbour_acc = {s: in_bank([P, M], F32, f"neighbour_acc{i}", i) for i, s in enumerate(slots)}

        def neighbour_pass(a):
            plane = v2_moved[:, a, :].bitcast(U8)
            for jb, t in slots:
                cols = slot_cols(jb, t)
                nc.tensor.matmul_mx(
                    out=neighbour_acc[jb, t][:],
                    lhsT=v2_codes[a][:, cols].bitcast(FP8X4),
                    lhsT_scale=plane[:, cols],
                    rhs=xn_codes[:, a, :].bitcast(FP4X4),
                    rhs_scale=xn_planes[:, a, :].bitcast(U8),
                    start=(a == 0),
                    stop=(a == K_PASSES - 1),
                )

        v2_codes.append(pick_v2(K_PASSES - 1))
        v_planes = pick_scales(v_scale_win, placed([P, S], U8, "v_listed", at_v2_win[K_PASSES - 1]), "v_planes")
        interleave(xc_grouped[0][:], xc_raw[0][:])
        quantise_xc(0)
        for a in range(K_PASSES):
            neighbour_pass(a)
        resp = {}
        for i, s in enumerate(slots):
            resp[s] = placed([P, M], F32, f"resp{i}", at_resp + 2 * i)
            nc.scalar.copy(resp[s][:], neighbour_acc[s][:])

        centre_acc = {s: in_bank([P, M], F32, f"centre_acc{i}", i) for i, s in enumerate(slots)}

        def centre_pass(a, jb, t, codes):
            nc.tensor.matmul_mx(
                out=centre_acc[jb, t][:],
                lhsT=codes.bitcast(FP8X4),
                lhsT_scale=v_planes[PLANE_ROWS * a : P, slot_cols(jb, t)],
                rhs=xc_codes[a][:].bitcast(FP8X4),
                rhs_scale=xc_planes[:, a, :],
                start=(a == 0),
                stop=(a == K_PASSES - 1),
            )

        codes = pick_words(v_win[0], kept([P, S], U32, "v_codes0"), whole_list)
        for jb, t in slots:
            centre_pass(0, jb, t, codes[:, slot_cols(jb, t)])
        codes = pick_words(v_win[1], placed([P, S], U32, "v_codes1", at_xc_grouped[0]), whole_list)
        interleave_on_gpsimd(xc_grouped[1][:], xc_raw[1][:])
        quantise_xc(1)
        for jb, t in slots:
            centre_pass(1, jb, t, codes[:, slot_cols(jb, t)])
        last = K_PASSES - 1
        interleave(xc_grouped[last][:, 0:SCALAR_COLS, :], xc_raw[last][:, :, 0:SCALAR_COLS])
        interleave_on_gpsimd(xc_grouped[last][:, SCALAR_COLS:M, :], xc_raw[last][:, :, SCALAR_COLS:M])
        quantise_xc(last)
        for jb in range(J_PASSES):
            codes = placed([P, S // J_PASSES], U32, f"v_codes_last{jb}", at_xc_grouped[last] + 2 * jb)
            pick_words(v_win[last], codes, half_list[jb])
            for t in range(PACK):
                centre_pass(last, jb, t, codes[:, t * P : (t + 1) * P])

        for piece in range(WD_PIECES):
            wd_raw[0, piece] = load_wd(0, piece)
        single_win[0] = load_single(0)
        for piece in range(WD_PIECES):
            wd_raw[1, piece] = load_wd(1, piece)
        single_win[1] = load_single(1)

        pair_win = {}

        def round_pair(pair, pieces, copy=nc.scalar.copy):
            if pair not in pair_win:
                pair_win[pair] = placed([P, T, 2], BF16, f"pair_win{pair}", at_pair_win[pair])
            width = T // WD_PIECES
            for piece in pieces:
                copy(
                    pair_win[pair][:, piece * width : (piece + 1) * width, :],
                    wd_raw[pair, piece][:].rearrange("p e t -> p t e"),
                )

        h_rows = [placed([P, PACK, M], BF16, f"h_rows{jb}", at_h_rows + 4 * jb) for jb in range(J_PASSES)]
        h_grouped = [placed([P, M, PACK], BF16, "h_grouped0", at_h_grouped_first), placed([P, M, PACK], BF16, "h_grouped1", at_h_grouped_second)]
        h_codes = placed([P, J_PASSES, M], U32, "h_codes", at_single_win[0])
        h_planes = kept([P, J_PASSES, M], U8, "h_planes")

        def larger_times_gain(jb, t):
            i = PACK * jb + t
            larger = placed([P, M], F32, f"larger{i}", at_larger[i])
            nc.vector.tensor_tensor(larger[:], centre_acc[jb, t][:], resp[jb, t][:], ALU.max)
            gain = vec_cols[:, t, jb : jb + 1]
            nc.gpsimd.tensor_scalar(h_rows[jb][:, t, :], larger[:], gain, 0.0, ALU.mult, ALU.add)

        def quantise_h(jb):
            quantise(h_codes[:, jb, :], h_planes[:, jb, :], h_grouped[jb][:].rearrange("p m t -> p (m t)"))

        wd_codes, wd_planes = {}, {}

        def pick_pair(pair, picked, cols):
            window = pair_win[pair][:].rearrange("p t e -> p (t e)").bitcast(U32)
            nc.vector.tensor_copy(in_slot_order(picked[:]), window.indirect(offsets[:, cols]))

        def turn_pair(words, bank, grouped):
            for t in range(PACK):
                nc.tensor.transpose(bank[:, t, :], words[t].bitcast(F32), identity[:])
            nc.scalar.copy(grouped, bank[:].bitcast(BF16).rearrange("p t n -> p n t"))

        def quantise_pair(pair, jb, passes, grouped, codes):
            planes = kept([P, passes, 2 * P], U8, f"pair_planes{pair}{jb}")
            quantise(
                codes[:].rearrange("p b n -> p (b n)"),
                planes[:].rearrange("p b n -> p (b n)"),
                grouped[:].rearrange("p b n t -> p (b n t)"),
            )
            for e in range(2):
                for k in range(passes):
                    wd_codes[2 * pair + e, jb + k] = codes[:, k, e * P : (e + 1) * P]
                    wd_planes[2 * pair + e, jb + k] = planes[:, k, e * P : (e + 1) * P]

        def pick_single(s, picked, cols):
            nc.vector.tensor_copy(
                picked[:].rearrange("p u (c r) e -> p c u e r", r=RUN), single_win[s][:].indirect(offsets[:, cols])
            )

        def turn_single(picked, bank, grouped):
            words = picked[:].rearrange("p u w e -> p (u w e)").bitcast(F32)
            for jb in range(J_PASSES):
                for u in range(2):
                    start = (u * J_PASSES + jb) * P
                    nc.tensor.transpose(bank[:, jb, u, :], words[:, start : start + P], identity[:])
            nc.scalar.copy(
                grouped.bitcast(F32).rearrange("p (b n u) -> p b n u", b=J_PASSES, u=2),
                bank[:].rearrange("p b u n -> p b n u"),
            )

        sums = {}

        def project_pass(i, jb, bank):
            if jb == 0:
                sums[i] = in_bank([P, M], F32, f"sum{i}", bank)
            nc.tensor.matmul_mx(
                out=sums[i][:],
                lhsT=wd_codes[i, jb].bitcast(FP8X4),
                lhsT_scale=wd_planes[i, jb],
                rhs=h_codes[:, jb, :].bitcast(FP8X4),
                rhs_scale=h_planes[:, jb, :],
                start=(jb == 0),
                stop=(jb == J_PASSES - 1),
            )

        def project(i, bank):
            for jb in range(J_PASSES):
                project_pass(i, jb, bank)

        def add_bias(i, kib):
            biased = placed([P, M], F32, f"biased{i}", kib)
            nc.scalar.activation(biased[:], sums[i][:], IDENTITY, bias=vec_cols[:, 0, BIAS_ROW + i : BIAS_ROW + i + 1])
            return biased

        def weigh_on_gpsimd(i, biased):
            result = placed([P, M], F32, f"result{i}", at_result[i])
            nc.gpsimd.tensor_tensor(result[:], biased[:], ew_all[:], ALU.mult)
            nc.sync.dma_start(out[i * P : (i + 1) * P, :], result[:])

        def finish_in_halves(i):
            bias = vec_cols[:, 0, BIAS_ROW + i : BIAS_ROW + i + 1]
            for half in range(2):
                cols = slice(half * M // 2, (half + 1) * M // 2)
                result = placed([P, M // 2], F32, f"result{i}{half}", at_result[i] + half)
                nc.vector.scalar_tensor_tensor(result[:], sums[i][:, cols], bias, ew_all[:, cols], ALU.add, ALU.mult)
                nc.sync.dma_start(out[i * P : (i + 1) * P, cols], result[:])

        def finish(i):
            result = placed([P, M], F32, f"result{i}", at_result[i])
            bias = vec_cols[:, 0, BIAS_ROW + i : BIAS_ROW + i + 1]
            nc.vector.scalar_tensor_tensor(result[:], sums[i][:], bias, ew_all[:], ALU.add, ALU.mult)
            nc.sync.dma_start(out[i * P : (i + 1) * P, :], result[:])

        first_single, last_single = 2 * N_PAIRS, 2 * N_PAIRS + 1

        round_pair(0, range(WD_PIECES))
        for jb, t in slots:
            larger_times_gain(jb, t)
        interleave(h_grouped[0][:], h_rows[0][:])
        interleave_on_gpsimd(h_grouped[1][:], h_rows[1][:])

        def pick_and_turn_pair(pair, jb, kib, grouped):
            picked = placed([P, S // J_PASSES], U32, f"pair_picked{pair}{jb}", kib)
            pick_pair(pair, picked, half_list[jb])
            bank = in_bank([P, PACK, P], F32, f"pair_bank{pair}{jb}", jb)
            turn_pair([picked[:, t * P : (t + 1) * P] for t in range(PACK)], bank, grouped)

        first_grouped = placed([P, J_PASSES, 2 * P, PACK], BF16, "pair_grouped0", at_first_grouped)
        for jb in range(J_PASSES):
            pick_and_turn_pair(0, jb, at_resp + 12 + 2 * jb, first_grouped[:, jb, :, :])

        def pick_and_turn_single(s, kib):
            picked = placed([P, 2, S // PACK, 2], BF16, f"single_picked{s}", kib)
            pick_single(s, picked, whole_list)
            grouped = placed([P, S], BF16, f"single_grouped{s}", at_single_grouped[s])
            turn_single(picked, in_bank([P, J_PASSES, 2, P], F32, f"single_bank{s}", 2 + s), grouped[:])
            return grouped

        def quantise_single(i, grouped, codes):
            planes = kept([P, J_PASSES, P], U8, f"single_planes{i}")
            quantise(codes[:].rearrange("p b n -> p (b n)"), planes[:].rearrange("p b n -> p (b n)"), grouped[:])
            for jb in range(J_PASSES):
                wd_codes[i, jb] = codes[:, jb, :]
                wd_planes[i, jb] = planes[:, jb, :]

        round_pair(1, range(1))
        grouped = pick_and_turn_single(0, at_larger[-1])
        round_pair(1, [1, 3])
        for jb in range(J_PASSES):
            quantise_h(jb)
        codes = placed([P, J_PASSES, 2 * P], U32, "pair_codes0", at_h_grouped_second)
        quantise_pair(0, 0, J_PASSES, first_grouped, codes)
        project(0, 4)
        project(1, 5)
        quantise_single(first_single, grouped, placed([P, J_PASSES, P], U32, "single_codes0", at_first_grouped))
        project(first_single, 6)
        round_pair(1, [2], nc.vector.tensor_copy)
        weigh_on_gpsimd(0, add_bias(0, at_wd_raw[1][3]))
        weigh_on_gpsimd(1, add_bias(1, at_wd_raw[1][3] + 2))
        weigh_on_gpsimd(first_single, add_bias(first_single, at_wd_raw[1][2]))
        second_grouped = []
        for jb in range(J_PASSES):
            second_grouped.append(placed([P, 1, 2 * P, PACK], BF16, f"pair_grouped1{jb}", at_last_grouped + 2 * jb))
            pick_and_turn_pair(1, jb, at_h_grouped_first + 2 * jb, second_grouped[jb][:, 0, :, :])
        last_grouped = []
        for jb in range(J_PASSES):
            picked = placed([P, 2, P, 2], BF16, f"last_picked{jb}", [at_h_grouped_first, at_last_grouped][jb])
            pick_single(1, picked, half_list[jb])
            words = picked[:].rearrange("p u w e -> p (u w e)").bitcast(F32)
            bank = in_bank([P, 2, P], F32, f"last_bank{jb}", 2 + jb)
            for u in range(2):
                nc.tensor.transpose(bank[:, u, :], words[:, u * P : (u + 1) * P], identity[:])
            last_grouped.append(placed([P, S // J_PASSES], BF16, f"last_grouped{jb}", at_single_grouped[1] + jb))
            nc.scalar.copy(
                last_grouped[jb][:].bitcast(F32).rearrange("p (n u) -> p n u", u=2), bank[:].rearrange("p u n -> p n u")
            )
            codes = placed([P, 1, 2 * P], U32, f"pair_codes1{jb}", at_h_grouped_first + 2 + jb)
            quantise_pair(1, jb, 1, second_grouped[jb], codes)
            project_pass(2, jb, 7)
            project_pass(3, jb, 4)
        for jb in range(J_PASSES):
            codes = kept([P, P], U32, f"last_codes{jb}")
            planes = kept([P, P], U8, f"last_planes{jb}")
            quantise(codes[:], planes[:], last_grouped[jb][:])
            wd_codes[last_single, jb], wd_planes[last_single, jb] = codes[:], planes[:]
            project_pass(last_single, jb, 5)
        finish(2)
        finish(3)
        finish_in_halves(last_single)
